import numpy as np, ml_dtypes
CORES = [9,25,41,57]
N = 4
BF = ml_dtypes.bfloat16
def gentries(a):
    return np.ascontiguousarray(a.reshape(8, 16, -1).transpose(0, 2, 1)).reshape(8, -1)
def gtable(e):
    e = np.asarray(e); return np.ascontiguousarray(e.reshape(8, -1, 16).transpose(0, 2, 1)).reshape(128, -1).astype(np.int32)
V, TL, FM, LM = 4096, 2, 7, 896
NT = 8 // TL
def pick(a, i):
    return np.take_along_axis(a, i, -1)
def turn(x):
    return np.argsort(x, axis=-1)
def put(P, a, b, g, p):
    P[min(a, b), max(a, b), g] = p if a < b else turn(p)
def setw(W, a, b, t, w):
    W[min(a, b), max(a, b), t] = w
def same():
    P = np.empty((N, N, 8, V), np.int64); P[...] = np.arange(V)
    return P
def noise(rng, part):
    p = np.tile(np.arange(V), (len(part), 1))
    for i in range(len(part)):
        x = rng.permutation(V)[:max(2, int(part[i] * V))]; p[i, x] = np.roll(x, 1)
    return p
def twins(rng, share, n):
    return np.arange(V)[None, :] ^ np.repeat((rng.random((n, V // 2)) < share).astype(np.int64), 2, axis=1)
def swaps(n):
    p = np.arange(V); p[n] = n.reshape(-1, 2)[:, ::-1].reshape(-1)
    return p
def paired(rng, b):
    c = np.where(rng.random(b.shape) < 0.4, np.where(b < FM, b + 1, b - 1), b)
    f = np.tile(np.stack([b, c], -1).reshape(8, 16, V), (N, 1, 1, 1))
    return np.clip(f + (rng.random(f.shape) < 0.05) * rng.integers(-1, 2, f.shape), 0, FM)
def scene(rng, P, W, lo, hi):
    def good():
        return noise(rng, lo * (0.25 + 0.75 * rng.random(TL)))
    def bad():
        return noise(rng, hi + 0.2 * rng.random(TL))
    kinds = min(3, NT * (N // 4)); s = int(rng.integers(0, kinds))
    for t in range(NT):
        g = slice(t * TL, t * TL + TL)
        for a in range(N):
            for b in range(a + 1, N): put(P, a, b, g, bad())
        for q in range(N // 4):
            m = int(rng.integers(0, 4)); L = [4 * q + (i ^ m) for i in range(4)]; kind = (t * (N // 4) + q + s) % kinds
            if kind < 2:
                for i, k in (((0, 3), (3, 1), (1, 2)), ((0, 2), (2, 1), (1, 3)))[kind]: put(P, L[i], L[k], g, good())
            else:
                for i in range(4):
                    for k in range(i): put(P, L[i], L[k], g, good())
                x = twins(rng, 0.5, TL); put(P, L[0], L[2], g, x); put(P, L[1], L[3], g, x)
                setw(W, L[0], L[1], t, LM); setw(W, L[2], L[3], t, 0)
        if N == 8:
            for d in (4, 6):
                h = int(rng.integers(0, 2)); b = (2 * h) ^ int(rng.integers(0, 2)); put(P, b, b ^ (d + 1), g, good())
                a = 2 - 2 * h; x = twins(rng, 0.5, TL)
                put(P, a, a ^ d, g, good()); put(P, a ^ 1, a ^ 1 ^ d, g, good()); put(P, a, a ^ d ^ 1, g, x); put(P, a ^ 1, a ^ d, g, x)
                setw(W, a, a ^ d, t, LM); setw(W, a ^ 1, a ^ 1 ^ d, t, 0)
def pack(Q, f, P, W):
    ft = pick(f, Q[:, :, None, :]); back = turn(Q); X = np.empty((N, 8, N - 1, V), np.int64); lam = np.empty((N, NT, N - 1), np.int32)
    for a in range(N):
        for b in range(a + 1, N):
            x = pick(back[b], pick(P[a, b], Q[a])); d = a ^ b
            X[a, :, d - 1] = x; X[b, :, d - 1] = turn(x); lam[a, :, d - 1] = W[a, b]; lam[b, :, d - 1] = W[a, b]
    return {"ft": np.ascontiguousarray(ft.reshape(N, 128, V)).astype(np.float32).astype(BF), "mp": np.stack([gtable(x.reshape(8, -1)) for x in X]), "lam": lam}
def setup_inputs(rng):
    Q = np.argsort(rng.random((N, 8, V)), axis=-1); f = paired(rng, rng.integers(0, FM + 1, (8, 16, V // 2)))
    P = same(); W = rng.integers(0, LM + 1, (N, N, NT)); scene(rng, P, W, 0.04, 0.7)
    return pack(Q, f, P, W)
def setup_inputs_spread(rng):
    Q = np.argsort(rng.random((N, 8, V)), axis=-1)
    b = np.minimum(((FM + 1) * rng.random((8, 16, V // 2)) ** np.exp2(rng.integers(-2, 4, (8, 16, 1)))).astype(np.int64), FM); f = paired(rng, b)
    P = same(); W = np.clip(np.exp2(rng.random((N, N, NT)) * np.log2(LM + 2.0)).astype(np.int64) - 1, 0, LM); scene(rng, P, W, 0.06, 0.55)
    return pack(Q, f, P, W)
def setup_inputs_ends(rng):
    h = V // 2; x = np.arange(V)
    f = np.tile(FM * ((x & 1) ^ rng.integers(0, 2, (8, 16, 1))), (N, 1, 1, 1))
    Q = np.empty((N, 8, V), np.int64); Q[..., 0::2] = 2 * np.argsort(rng.random((N, 8, h)), axis=-1); Q[..., 1::2] = 2 * np.argsort(rng.random((N, 8, h)), axis=-1) + 1
    P = same(); W = LM * rng.integers(0, 2, (N, N, NT))
    for a in range(N):
        for b in range(a + 1, N):
            k = (a ^ b) & 1
            P[a, b, :, 0::2] = 2 * np.argsort(rng.random((8, h)), axis=-1) + k; P[a, b, :, 1::2] = 2 * np.argsort(rng.random((8, h)), axis=-1) + 1 - k
            for g in range(8):
                m = int(rng.choice(np.array([0, 0, 1, 3, V // 16]))); i = 2 * rng.permutation(h)[:m]; o = 2 * rng.permutation(h)[:m] + 1
                u = P[a, b, g, i].copy(); P[a, b, g, i] = P[a, b, g, o]; P[a, b, g, o] = u
    for r in range(N): setw(W, r, r ^ 1, slice(0, NT), LM); setw(W, r, r ^ 2, slice(0, NT), 0)
    L = N - 4
    for g in range(8 - TL, 8):
        o = 2 * int(rng.integers(0, h)) + 1; y = 2 * int(rng.integers(1, V // 8)); z = h + 2 * int(rng.integers(0, V // 8))
        t02 = 2 * int(rng.integers(0, h)); t12 = 2 * int(rng.integers(0, h)) + 1; t23 = o; t03 = o + y + t02; t13 = o + z + t12
        t01 = t03 - t23 - t12 + (0 if g == 8 - TL else y)
        for i, k, s in ((0, 1, t01), (0, 2, t02), (0, 3, t03), (1, 2, t12), (1, 3, t13), (2, 3, t23)): P[L + i, L + k, g] = (x + s) % V
    for i, k, w in ((0, 1, LM), (0, 2, LM), (0, 3, 0), (1, 2, 0), (1, 3, 0), (2, 3, LM)): setw(W, L + i, L + k, NT - 1, w)
    return pack(Q, f, P, W)
def plain(rng):
    x = np.arange(V); e = x.copy(); e[0] = V - 1; e[V - 1] = 0
    S = [x, x[::-1], (x + 1) % V, (x - 1) % V, x ^ 1, e]
    Q = np.tile(x, (N, 8, 1)); P = same(); W = rng.choice(np.array([0, 1, LM - 1, LM]), (N, N, NT))
    for a in range(N):
        for b in range(a + 1, N):
            for g in range(8):
                i = int(rng.integers(0, 8)); P[a, b, g] = S[i] if i < 6 else rng.permutation(V)
    f = rng.integers(0, FM + 1, (N, 8, 16, V)); k = rng.permutation(8)
    f[:, k[0]] = FM * rng.integers(0, 2, (N, 16, 1)); f[:, k[1]] = FM * (x == V - 1); f[:, k[2]] = x * (FM + 1) // V; f[:, k[3]] = FM * rng.integers(0, 2, (N, 16, V)); f[:, k[4]] = f[:1, k[4]]
    return Q, f, P, W
def late(rng, f, P, W):
    x = np.arange(V); S = [x, x[::-1], (x + 1) % V, (x - 1) % V, x ^ 1]; k = int(rng.integers(0, TL)); ramp = x * (FM + 1) // V
    for g in range(TL):
        if g == k:
            p, q, a, y, o = [rng.permutation(V) for i in range(5)]; s = np.empty(V, np.int64); s[o] = np.roll(o, -1)
            b = a[p[swaps(o[[0, 2]])[turn(q)]]]; M = (p, q, a[p[s]], y, a, b)
            e = np.where(rng.random((16, 1)) < 0.5, ramp, FM - ramp)
            f[0, g] = e[:, q]; f[1, g] = e[:, q[turn(p)]]; f[2:4, g] = FM * rng.integers(0, 2, (2, 16, 1))
        else:
            c = [S[int(rng.integers(0, 5))] for i in range(4)]; M = [c[j][turn(c[i])] for i, j in ((0, 1), (0, 2), (0, 3), (1, 2), (1, 3), (2, 3))]
        for n, (i, j) in enumerate(((0, 1), (0, 2), (0, 3), (1, 2), (1, 3), (2, 3))): put(P, i, j, g, M[n])
    for i, j in ((0, 1), (0, 2), (1, 2), (1, 3), (2, 3)): setw(W, i, j, 0, 0)
    setw(W, 0, 3, 0, int(rng.choice(np.array([1, LM]))))
def edge(rng, f, P, W):
    x = np.arange(V); S = [x, x[::-1], (x + 1) % V, (x - 1) % V, x ^ 1]; L = N - 4; k = 8 - TL + int(rng.integers(0, TL))
    for g in range(8 - TL, 8):
        a = S[int(rng.integers(0, 5))]; h = S[int(rng.integers(0, 5))]; s = S[int(rng.integers(1, 5))]; t = x; u = x
        if g == k:
            c = 4 * (1 + rng.permutation(V // 4 - 1)[:14]); n = np.concatenate([np.array([0]), c[:7]]); m = c[7:]
            rest = rng.permutation(np.setdiff1d(x, np.concatenate([n, m])))
            o = np.concatenate([n[[1, 0, 2, 4, 6]], rest[:V // 2], n[[3, 5, 7]], m[[0, 1, 2, 4]], rest[V // 2:], m[[3, 5, 6]]])
            s = np.empty(V, np.int64); s[o] = np.roll(o, -1)
            m = np.concatenate([m[:6], np.array([0]), m[6:]]); t = swaps(n); u = swaps(m); a = rng.permutation(V); h = rng.permutation(V)
            for r, q, w in ((L, a, n), (L + 2, h, m)):
                y = rng.integers(0, FM + 1, (16, V))
                for i in range(4):
                    z = (LM // 64 + i) // 4; lo = rng.integers(0, FM + 1 - z, 16); y[:, w[2 * i]] = lo; y[:, w[2 * i + 1]] = lo + z
                f[r, g] = y; f[r + 1, g] = y[:, turn(q)]
        for i, j, p in ((0, 1, a[t]), (0, 2, x), (0, 3, h), (1, 2, turn(a)), (1, 3, h[s[turn(a)]]), (2, 3, h[u])): put(P, L + i, L + j, g, p)
    setw(W, L, L + 1, NT - 1, LM); setw(W, L + 2, L + 3, NT - 1, LM - 1)
def setup_inputs_shapes(rng):
    Q, f, P, W = plain(rng); late(rng, f, P, W); edge(rng, f, P, W)
    return pack(Q, f, P, W)
def setup_inputs_corners(rng):
    Q, f, P, W = plain(rng); x = np.arange(V); e = x.copy(); e[0] = V - 1; e[V - 1] = 0
    for a in range(4):
        for b in range(a + 1, 4): P[a, b, :TL] = x
    n = rng.permutation(V // 2)[:2]; P[0, 1, :TL] = x[::-1]; P[1, 3, :TL] = swaps(n); f[:4, :TL] = FM; setw(W, 0, 1, 0, 1)
    m = 3 * V // 4 - 2; k = int(rng.integers(0, TL)); rest = np.setdiff1d(x, n)
    for g in range(TL):
        o = rng.permutation(rest)
        o = np.concatenate([n[:1], o[:m - 1]]) if g == k else np.concatenate([n[:1], o[:m // 2], n[1:], o[m // 2:m - 2]])
        p = x.copy(); p[o] = np.roll(o, -1); P[2, 3, g] = p
    setw(W, 2, 3, 0, 0); setw(W, 1, 3, 0, int(rng.choice(np.array([1, LM]))))
    L = N - 4
    for a in range(L, N):
        for b in range(a + 1, N): P[a, b, 8 - TL:] = x
    f[L:, 8 - TL:] = rng.integers(0, FM + 1, (TL, 16, V)); f[L:, 7, :, 0] = 0; f[L:, 7, :, V - 1] = FM
    P[N - 2, N - 1, 7] = e; setw(W, N - 2, N - 1, NT - 1, 0)
    return pack(Q, f, P, W)
def setup_inputs_calm(rng):
    Q = np.empty((N, 8, V), np.int64); Q[..., :V - 1] = np.argsort(rng.random((N, 8, V - 1)), axis=-1); Q[..., V - 1] = V - 1
    f = np.tile(rng.integers(0, FM + 1, (8, 16, V)), (N, 1, 1, 1)); f[:, :, 8:] = rng.integers(0, FM + 1, (N, 8, 8, V))
    P = same(); W = rng.integers(0, LM + 1, (N, N, NT))
    fours = [(4 * q, 2) for q in range(N // 4)] + ([(0, 4), (2, 4), (0, 6), (2, 6)] if N == 8 else [])
    for t in range(NT):
        ids = rng.permutation(V - 1)[:8 * len(fours)]
        for n in range(len(fours)):
            r, d = fours[n]; L = [r, r ^ 1, r ^ d, r ^ d ^ 1]; g = t * TL + int(rng.integers(0, TL)); z = int(rng.integers(1, FM + 1))
            u = ids[8 * n:8 * n + 4].copy(); w = ids[8 * n + 4:8 * n + 8].copy()
            if n == 0: u[0] = V - 1
            p = np.arange(V); p[u] = w; p[w] = u; P[min(L[0], L[3]), max(L[0], L[3]), g] = p; P[min(L[1], L[2]), max(L[1], L[2]), g] = p
            for i in range(4):
                a, b = int(u[i]), int(w[i]); lo = int(rng.integers(0, FM + 1 - z))
                f[:, g, :, b] = f[:, g, :, a]; f[:, g, i, a] = lo; f[:, g, i, b] = lo + z
            if d == 2: setw(W, L[0], L[1], t, 2 * z - int(rng.integers(0, 2))); setw(W, L[2], L[3], t, 2 * z - int(rng.integers(0, 2)))
            k = int(rng.integers(0, 2)); setw(W, L[0], L[2], t, 2 * z + k); setw(W, L[1], L[3], t, 2 * z + 1 - k)
            k = int(rng.integers(0, 2)); setw(W, L[0], L[3], t, 2 * z - k); setw(W, L[1], L[2], t, 2 * z - 1 + k)
    return pack(Q, f, P, W)
def check_inputs(d):
    bad = []
    f = np.asarray(d["ft"]).astype(np.float64)
    if not np.all((f >= 0) & (f <= FM) & (f == np.floor(f))): bad.append("range of ft")
    m = np.asarray(d["mp"]).astype(np.int64); w = np.asarray(d["lam"]).astype(np.int64)
    if np.min(w) < 0 or np.max(w) > LM: bad.append("range of lam")
    if any(np.any(w[r, :, k - 1] != w[r ^ k, :, k - 1]) for r in range(N) for k in range(1, N)): bad.append("lam differs between the two ranks of a pair")
    if np.min(m) < 0 or np.max(m) > V - 1: bad.append("range of mp")
    else:
        X = [gentries(a).astype(np.int64).reshape(8, N - 1, V) for a in m]
        if any(np.any(pick(X[r ^ k][:, k - 1], X[r][:, k - 1]) != np.arange(V)) for r in range(N) for k in range(1, N)): bad.append("mp: a map is not the inverse of its partner's")
    return bad
def reference(ft, mp, lam):
    F = ft.astype(np.float32).astype(np.int32).reshape(N, 8, 16, V); S = F - np.roll(F, -1, axis=3)
    X = {}
    for r in range(N):
        x = gentries(mp[r]).astype(np.int64).reshape(8, N - 1, V)
        for d in range(1, N): X[r, r ^ d] = x[:, d - 1]
    for d in range(1, N):
        e = 2 if d == 1 else 1
        for r in range(N):
            j = r ^ d
            if r > j: continue
            C = [X[r, j]] + [pick(X[k, j], X[r, k]) for k in (r ^ e, j ^ e)]
            score = []
            for c in range(3):
                G = pick(F[j], C[c][:, None, :]); A = np.abs(S[r] - (G - np.roll(G, -1, axis=2)))
                A = np.add.reduce(A.reshape(NT, -1), axis=1, dtype=np.int64); D = np.zeros(NT, np.int64)
                for o in range(3): D = D + np.add.reduce((C[c] != C[o]).reshape(NT, -1), axis=1, dtype=np.int64)
                score.append(A + lam[r][:, d - 1].astype(np.int64) * D)
            win = np.argmin(np.stack(score), axis=0)
            X[r, j] = np.stack(C)[np.repeat(win, TL), np.arange(8)]; X[j, r] = turn(X[r, j])
    ym = np.stack([gtable(np.stack([X[r, r ^ d] for d in range(1, N)], axis=1).reshape(8, -1)) for r in range(N)])
    return {"ym": ym.astype(np.float32)}

@@ -1,0 +1,737 @@
+import numpy as np
+from concourse.bass import DstId, RemoteDMATransfer
+from concourse.mybir import AluOpType as A, AxisListType, ActivationFunctionType as AF
+
+N, V, Q = 4, 4096, 1024
+ACT_H = True
+SEEDS = [[19, 61898, 34908, 66228, 64185, 5699, 11932, 68760, 45576, 13228, 76997], [78, 17509],
+         [74, 56747, 72125, 1906, 30423, 43207, 29139, 88216], [43, 66308, 1922, 30483, 32589, 16691, 18544]]
+PAIRS = [(0, 1), (2, 3), (0, 2), (1, 3), (0, 3), (1, 2)]
+EXTRA = ["10", "20", "21", "30", "31", "IC", "id"]
+NR, NTB = 19, 11
+LN_X = 6 * 192
+LN_W = LN_X + 64 * len(EXTRA)
+LN_END = LN_W + 256 + 256 + 128
+
+SCRATCH = {
+    "M": ("sbuf", [128, 4, 256], "int32"),
+    "M16": ("sbuf", [128, 1024], "float16"),
+    "Z16": ("sbuf", [128, 1024], "float16"),
+    "T1": ("sbuf", [128, 1024], "float16"),
+    "HI": ("sbuf", [128, 1024], "bfloat16"),
+    "LO": ("sbuf", [128, 1024], "bfloat16"),
+    "Z2": ("sbuf", [128, 4 * 512], "bfloat16"),
+    "MW": ("sbuf", [128, 5 * V], "bfloat16"),
+    "FW1": ("sbuf", [128, V], "bfloat16"),
+    "FW2": ("sbuf", [128, V], "bfloat16"),
+    "FW3": ("sbuf", [128, V], "bfloat16"),
+    "FR": ("sbuf", [128, 3 * Q], "bfloat16"),
+    "FS": ("sbuf", [128, 3 * Q], "bfloat16"),
+    "FD": ("dram", [4, 128, Q], "bfloat16"),
+    "H": ("sbuf", [128, 18 * Q], "bfloat16"),
+    "R": ("sbuf", [128, NR * Q], "bfloat16"),
+    "JK": ("sbuf", [128, 2 * Q], "bfloat16"),
+    "JS": ("sbuf", [128, 18 * 64], "float32"),
+    "LN": ("sbuf", [128, LN_END], "float32"),
+    "U": ("sbuf", [128, LN_W], "uint16"),
+    "US": ("sbuf", [128, 64 * 16], "uint16"),
+    "TB": ("sbuf", [128, NTB * 192], "float32"),
+    "NE": ("sbuf", [128, 6 * 256], "bfloat16"),
+    "AC": ("sbuf", [128, 24], "float32"),
+    "EC": ("sbuf", [128, 24], "float32"),
+    "FL": ("sbuf", [128, 28], "float32"),
+    "WC": ("sbuf", [128, 12], "float32"),
+    "OF": ("sbuf", [128, 6 * 16], "uint16"),
+    "OUT": ("sbuf", [128, 12 * 64], "float32"),
+    "YL": ("sbuf", [128, 12 * 64], "float32"),
+    "IOT": ("sbuf", [128, 192], "float32"),
+    "IOT2": ("sbuf", [128, 128], "float32"),
+    "IOT3": ("sbuf", [128, 16], "float32"),
+    "KI": ("sbuf", [128, 2], "int32"),
+    "CI": ("sbuf", [128, 10], "int32"),
+    "CF": ("sbuf", [128, 10], "float32"),
+    "CD": ("sbuf", [128, 16], "float32"),
+    "WB": ("sbuf", [128, 12], "float32"),
+    "MB": ("sbuf", [128, 4], "float32"),
+    "MK": ("sbuf", [128, 8], "float32"),
+    "PC": ("sbuf", [128, 16], "float32"),
+    "EW": ("sbuf", [128, 128], "bfloat16"),
+    "BW": ("sbuf", [128, 1024], "bfloat16"),
+    "BC": ("sbuf", [128, 4 * 144], "bfloat16"),
+    "BO": ("sbuf", [128, 2 * 192], "bfloat16"),
+    "BL": ("sbuf", [128, 4 * 176], "float16"),
+    "OH": ("sbuf", [128, 3 * 128], "float16"),
+    "ID": ("sbuf", [128, 4 * 128], "bfloat16"),
+    "PM": ("sbuf", [128, 128], "float32"),
+    "ONE": ("sbuf", [128, 128], "float32"),
+    "E0": ("psum", [128, 1024], "float32"),
+    "E1": ("psum", [128, 1024], "float32"),
+    "P4": ("psum", [128, 512], "float32"),
+    "P5": ("psum", [128, 512], "float32"),
+    "P6": ("psum", [128, 512], "float32"),
+    "P7": ("psum", [128, 512], "float32"),
+}
+SEMAPHORES = (["pe", "dve", "act", "pool", "lsem", "hs0", "hs1"] + ["ma%d" % a for a in range(4)] + ["fa%d" % a for a in range(4)]
+              + ["oa%d" % k for k in range(12)] + ["d%d" % k for k in range(48)])
+
+CY, PCY, GA, LAT = 1.04e-3, 0.52e-3, 1.56, 0.12
+ARR_MAP = {1: 8.5, 3: 10.0, 2: 11.5}
+ARR_FT = {1: 13.0, 3: 15.0, 2: 21.0}
+ISSUE, DLAT, DRATE = 0.08, 2.0, 250e3
+
+
+def helpers(topo, core):
+    near = [c for c in topo.cores_of(core) if c != core and topo.die(c) == topo.die(core)]
+    far = [c for c in topo.cores_of(core) if topo.die(c) != topo.die(core)]
+    return near[0], far[0]
+
+
+def bits(es):
+    return sum(1 << e for e in es)
+
+
+def plan(ops, seed):
+    rng = np.random.RandomState(seed[0])
+    slack, pen = float(rng.uniform(0.0, 0.3)), float(rng.uniform(0.0, 1.5))
+    dp, de = np.zeros(len(ops)), np.zeros(len(ops))
+    for s in seed[1:]:
+        rng = np.random.RandomState(s)
+        part = (0.005, 0.015, 0.04)[s % 3]
+        dp = dp + (rng.uniform(size=len(ops)) < part) * rng.normal(0.0, 5.0, size=len(ops))
+        de = de + (rng.uniform(size=len(ops)) < part) * rng.normal(0.0, 1.0, size=len(ops))
+    succ = [[] for _ in ops]
+    for o in ops:
+        o["open"] = len(o["deps"] + o["ord"])
+        for d in o["deps"] + o["ord"]:
+            succ[d["n"]].append(o)
+    for o in reversed(ops):
+        o["path"] = min(o["dur"].values()) + o["tail"] + LAT + max([s["path"] for s in succ[o["n"]]] + [o.get("boost", 0.0)])
+        o["prio"] = o["path"] + float(dp[o["n"]])
+        o["pen"] = max(-0.9, (-0.5 if "twice" in o else pen) + float(de[o["n"]]))
+    free = {}
+    holder = [None] * 8
+    left = [o for o in ops if o["open"] == 0]
+    order = []
+
+    def bank_at(b):
+        h = holder[b]
+        if h is None:
+            return 0.0
+        if any("end" not in c for c in h["cons"]):
+            return None
+        return max(c["end"] for c in h["cons"]) + LAT
+
+    while left:
+        cand = []
+        for o in left:
+            if "rdy" not in o:
+                o["rdy"] = max([d["end"] + LAT for d in o["deps"]] + [o["at"]])
+            rdy = o["rdy"]
+            bk = None
+            if o["psum"]:
+                sets = [(0, 1), (2, 3)] if o["psum"] == 2 else ([(4,), (5,), (6,), (7,)] if o["psum"] == 1 else [(b,) for b in (4, 5, 6, 0, 1, 2, 3)])
+                best = None
+                for s in sets:
+                    ts = [bank_at(b) for b in s]
+                    if None in ts:
+                        continue
+                    tm = max(max(ts), rdy, free.get("pe", 0.0))
+                    if best is None or tm < best[0]:
+                        best = (tm, s)
+                if best is None:
+                    continue
+                rdy, bk = best
+            e = min(o["dur"], key=lambda x: max(rdy, free.get(x, 0.0)) + o["dur"][x] * (1.0 + (o["pen"] if x == "dve" else 0.0)))
+            cand.append((max(rdy, free.get(e, 0.0)), o, e, bk))
+        t0 = min(c[0] for c in cand)
+        st, o, e, bk = max([c for c in cand if c[0] <= t0 + slack], key=lambda c: c[1]["prio"])
+        o["eng"], o["start"] = e, st
+        if e != "arr":
+            free[e] = st + o["dur"][e]
+        o["end"] = st + o["dur"][e] + o["tail"]
+        if bk:
+            o["bank"] = bk
+            for b in bk:
+                if holder[b] is not None:
+                    o["deps"] = o["deps"] + holder[b]["cons"]
+                holder[b] = o
+        if e == "act" and "twice" in o:
+            o["twice"]["dur"] = {"pe": 2 * o["twice"]["dur"]["pe"]}
+        left = [x for x in left if x is not o]
+        for s in succ[o["n"]]:
+            s["open"] -= 1
+            if s["open"] == 0:
+                left.append(s)
+        order.append(o)
+    return order
+
+
+def build(t, T, topo, core):
+    ops = []
+    nd = [0]
+
+    def op(name, dur, deps, fn, psum=0, tail=0.0, at=0.0, after=(), sem=None, uses=None):
+        o = {"n": len(ops), "name": name, "dur": dur, "deps": [d for d in deps if d is not None], "ord": list(after), "fn": fn,
+             "psum": psum, "tail": tail, "at": at, "sem": sem, "cons": []}
+        if uses is not None:
+            uses["cons"].append(o)
+            o["deps"].append(uses)
+        ops.append(o)
+        return o
+
+    def ps(o):
+        b = o["bank"]
+        if len(b) == 2:
+            return T["E%d" % (b[0] // 2)], 0
+        return (T["E%d" % (b[0] // 2)], 512 * (b[0] % 2)) if b[0] < 4 else (T["P%d" % b[0]], 0)
+
+    def pv(o, a, b):
+        buf, c = ps(o)
+        return buf[:, c + a:c + b]
+
+    def dve(name, n, deps, f, **k):
+        return op(name, {"dve": (max(n, 64) + 50) * CY}, deps, lambda q, e, o: [f(q)], **k)
+
+    def ts(name, out, in0, s1, s2, o0, o1, deps, n=64, **k):
+        if o1 is None:
+            return dve(name, n, deps, lambda q: q.tensor_scalar(out, in0, s1, None, o0), **k)
+        return dve(name, n, deps, lambda q: q.tensor_scalar(out, in0, s1, s2, o0, o1), **k)
+
+    def addc(name, out, src, c, deps, n=64, **k):
+        def f(q, e, o):
+            s = src() if not isinstance(src, tuple) else src[0]
+            if isinstance(c, tuple):
+                return [q.tensor_scalar(out, s, c[0], None, A.add) if e == "dve" else q.activation(out, s, AF.Identity, bias=c[0])]
+            if e == "dve":
+                return [q.tensor_scalar(out, s, float(c), None, A.add)]
+            return [q.activation(out, s, AF.Copy, bias=float(c))]
+        return op(name, {"dve": (n + 50) * CY, "act": (n + 110) * CY}, deps, f, **k)
+
+    def dma(name, pairs, nbytes, deps, queues=("sp",), **k):
+        s = "d%d" % nd[0]
+        nd[0] += 1
+        return op(name, {x: ISSUE * len(pairs) for x in queues}, deps, lambda q, e, o: [q.dma_start(a, b) for a, b in pairs],
+                  tail=DLAT + nbytes / DRATE, sem=s, **k)
+
+    def pe(name, cyc, deps, f, psum):
+        return op(name, {"pe": cyc * PCY + 0.05}, deps, f, psum=psum, tail=0.1)
+
+    def arrive(name, sem, val, at, deps=()):
+        o = op(name, {"arr": 0.0}, list(deps), None, at=at)
+        o["tok"] = (sem, val)
+        return o
+
+    def remote(name, f, n, deps, after=(), boost=6.0):
+        o = op(name, {"g": 0.8}, deps, lambda q, e, o: f(q), after=after)
+        o["lsem"], o["boost"] = n, boost
+        return o
+
+    cores = T.cores
+    a0 = t
+    pad = dve("pad", 1024, [], lambda q: q.memset(T.M[32 * a0:32 * a0 + 32, :, :], 2048))
+    ml = {}
+    for tt in (t ^ 1, t ^ 3, t ^ 2, t):
+        prs = [(T.M[32 * b:32 * b + 32, tt, :], T.mp[32 * tt:32 * tt + 32, 256 * ((a0 ^ b) - 1):256 * (a0 ^ b)]) for b in range(4) if b != a0]
+        ml[tt] = dma("mp%d" % tt, prs, 200e3, [], queues=("sp", "act"))
+    lam = dma("lam", [(T.M[32 * a0:32 * a0 + 1, :, 0:3], T.lam[:])], 0, [pad], queues=("sp", "act"))
+    fs = {}
+    for k, d in enumerate((1, 3, 2)):
+        tt = t ^ d
+        fs[d] = dma("fs%d" % d, [(T.FS[:, Q * k:Q * k + Q], T.ft[32 * tt:32 * tt + 32, :])], 262e3 * (k + 1) + 300e3, [], queues=("sp", "act"))
+    gq = []
+
+    def gop(name, n, f):
+        o = op(name, {"g": 0.13 + 2 * n * CY}, [], lambda q, e, o: [f(q)], after=gq[-1:])
+        gq.append(o)
+        return o
+    ki = gop("ki", 2, lambda q: q.iota(T.KI[:], [[48, 2]], 0, 1))
+    iot = gop("iot", 192, lambda q: q.iota(T.IOT[:], [[1, 192]], 0, 0, allow_small_or_imprecise_dtypes=True))
+    iot2 = gop("iot2", 128, lambda q: q.iota(T.IOT2[:], [[64, 2], [0, 4], [1, 16]], 0, 0, allow_small_or_imprecise_dtypes=True))
+    iot3 = gop("iot3", 16, lambda q: q.iota(T.IOT3[:], [[192, 4], [16, 4]], 0, 0, allow_small_or_imprecise_dtypes=True))
+    k0 = T.KI[:, 0:1]
+    ci = [ts("c0", T.CI[:, 0:1], k0, 15, None, A.bitwise_and, None, [ki]),
+          ts("c1", T.CI[:, 1:2], k0, 112, None, A.bitwise_and, None, [ki]),
+          ts("c2", T.CI[:, 2:3], k0, 64, None, A.bitwise_and, None, [ki]),
+          ts("c3", T.CI[:, 3:4], k0, 4, 3, A.arith_shift_right, A.bitwise_and, [ki]),
+          ts("c4", T.CI[:, 4:5], k0, 4, 1, A.arith_shift_right, A.bitwise_and, [ki]),
+          ts("c5", T.CI[:, 5:6], k0, 5, None, A.arith_shift_right, None, [ki]),
+          ts("c6", T.CI[:, 6:7], T.KI[:, 1:2], 63, None, A.bitwise_and, None, [ki]),
+          ts("c7", T.CI[:, 7:8], k0, 127, None, A.bitwise_and, None, [ki]),
+          ts("c8", T.CI[:, 8:9], k0, 3, 1, A.arith_shift_right, A.bitwise_and, [ki]),
+          ts("c9", T.CI[:, 9:10], k0, 7, None, A.bitwise_and, None, [ki])]
+    cf = dve("cf", 10, ci, lambda q: q.tensor_copy(T.CF[:], T.CI[:]))
+
+    def C(j):
+        return T.CF[:, j:j + 1]
+
+    def D(j):
+        return T.CD[:, j:j + 1]
+    d0 = ts("d0", D(0), C(1), 15.0, None, A.add, None, [cf])
+    d1 = ts("d1", D(1), C(2), C(3), 60.0, A.add, A.add, [cf])
+    d2a = ts("d2a", D(8), C(0), 4.0, C(2), A.mult, A.add, [cf])
+    d2 = ts("d2", D(2), D(8), C(3), None, A.add, None, [d2a])
+    d3a = ts("d3a", D(9), C(4), 64.0, C(0), A.mult, A.add, [cf])
+    d3 = ts("d3", D(3), D(9), 48.0, None, A.add, None, [d3a])
+    d4a = ts("d4a", D(10), C(2), 1.0 / 16, C(3), A.mult, A.add, [cf])
+    d4 = ts("d4", D(4), C(8), 64.0, D(10), A.mult, A.add, [d4a])
+    d5 = ts("d5", D(5), C(2), C(6), None, A.add, None, [cf])
+    d6 = ts("d6", D(6), C(3), 1024.0, C(0), A.mult, A.add, [cf])
+    dm = ts("dm", T.CD[:, 12:15], T.IOT[:, 0:96:32], C(7), None, A.is_equal, None, [cf, iot])
+    wa = ts("wa", T.WB[:, 4:8], T.IOT[:, 0:4], C(0), 32.0, A.is_equal, A.mult, [cf, iot])
+    wb_ = ts("wb", T.WB[:, 8:12], T.IOT[:, 4:8], C(0), None, A.is_equal, None, [cf, iot])
+    wc = dve("wc", 8, [wa, wb_], lambda q: q.tensor_tensor(T.WB[:, 0:4], T.WB[:, 4:8], T.WB[:, 8:12], A.add))
+    mb = ts("mb", T.MB[:], T.IOT[:, 0:4], C(5), None, A.is_equal, None, [cf, iot])
+    mk = ts("mk", T.MK[:], T.IOT[:, 0:8], C(9), None, A.is_equal, None, [cf, iot])
+    pc = ts("pc", T.PC[:], T.IOT3[:], C(0), None, A.add, None, [cf, iot3])
+    ew = ts("ew", T.EW[:], T.IOT2[:], D(4), None, A.is_equal, None, [d4, iot2], n=128)
+    bw = []
+    for i in range(8):
+        def f(q, e, o, i=i):
+            out = T.BW[:, 128 * i:128 * i + 128]
+            if e == "dve":
+                return [q.tensor_scalar(out, T.EW[:], T.MK[:, i:i + 1], None, A.mult)]
+            return [q.activation(out, T.EW[:], AF.Identity, scale=T.MK[:, i:i + 1])]
+        bw.append(op("bw%d" % i, {"dve": 114 * CY, "act": 240 * CY}, [ew, mk], f))
+    bc = [ts("bc%d" % b, T.BC[:, 144 * b:144 * b + 144], T.IOT[:, 0:144], D(0), T.WB[:, b:b + 1], A.is_equal, A.mult, [d0, wc], n=144) for b in range(4)]
+    bo = [ts("bo%d" % b, T.BO[:, 192 * b:192 * b + 192], T.IOT[:], D(1), T.WB[:, b:b + 1], A.is_equal, A.mult, [d1, wc], n=192) for b in range(2)]
+    bl = [ts("bl%d" % b, T.BL[:, 176 * b:176 * b + 176], T.IOT[:, 0:176], D(3), T.MB[:, b:b + 1], A.is_equal, A.mult, [d3, mb], n=176) for b in range(4)]
+    oh = [ts("oh%d" % b, T.OH[:, 128 * b:128 * b + 128], T.IOT[:, 0:128], 0.0, D(12 + b), A.mult, A.add, [dm], n=128) for b in range(3)]
+    idm = [ts("id0", T.ID[:, 0:128], T.IOT[:, 0:128], C(7), None, A.is_equal, None, [cf, iot], n=128),
+           ts("id1", T.ID[:, 128:256], T.IOT[:, 0:128], C(7), -1.0, A.is_equal, A.mult, [cf, iot], n=128),
+           ts("id2", T.ID[:, 256:384], T.IOT[:, 0:128], D(5), -1.0, A.is_equal, A.mult, [d5, iot], n=128),
+           ts("id3", T.ID[:, 384:512], T.IOT[:, 0:128], D(5), None, A.is_equal, None, [d5, iot], n=128)]
+    pm = ts("pm", T.PM[:], T.IOT[:, 0:128], D(2), None, A.is_equal, None, [d2, iot], n=128)
+    one = dve("one", 128, [], lambda q: q.memset(T.ONE[:], 1.0))
+    ac0 = dve("ac0", 24, [], lambda q: q.memset(T.AC[:], 0.0))
+    ec0 = dve("ec0", 24, [], lambda q: q.memset(T.EC[:], 0.0))
+    cast = {tt: ts("cast%d" % tt, T.M16[:, 256 * tt:256 * tt + 256], T.M[:, tt, :], -2048.0, None, A.add, None, [ml[tt], lam, pad], n=256)
+            for tt in (t ^ 1, t ^ 3, t ^ 2, t)}
+    near, far = helpers(topo, core)
+    up = topo.engines(core, near)
+    up = up[len(up) // 2:]
+    h = len(up) // 2
+
+    def dst(c):
+        r, p, _ = topo.addr(c)
+        return DstId(rid=r, pnc=p)
+
+    def f_h0(q):
+        q.remote_dma_fused([
+            RemoteDMATransfer(dst_ids=[dst(near)], dma_engine_mask=bits(up[:h]), remote_sem=T.sem.hs0, src=T.FS[:, 0:Q], dst=T.FS[:, 0:Q]),
+            RemoteDMATransfer(dst_ids=[dst(far)], dma_engine_mask=bits(up[h:]), remote_sem=T.sem.hs0, src=T.FS[:, Q:2 * Q], dst=T.FS[:, Q:2 * Q])],
+            local_sem=T.sem.lsem)
+        return []
+    sends = []
+    for d in (1, 3, 2):
+        tt = t ^ d
+
+        def f(q, tt=tt):
+            r, p, _ = topo.addr(cores[tt])
+            q.remote_dma(T.Z16[:, 256 * a0:256 * a0 + 256], T.M16[:, 256 * tt:256 * tt + 256], T.sem["ma%d" % a0], T.sem.lsem, p, r, topo.mask(core, cores[tt]))
+            return []
+        o = remote("sm%d" % d, f, len(topo.engines(core, cores[tt])), [cast[tt]], after=gq[-1:], boost=300.0)
+        gq.append(o)
+        if d == 1:
+            gq.append(remote("h0", f_h0, 2 * h, [fs[1], fs[3]], after=gq[-1:]))
+
+    def f_h1(q):
+        r, p, _ = topo.addr(far)
+        q.remote_dma(T.FS[:, 2 * Q:3 * Q], T.FS[:, 2 * Q:3 * Q], T.sem.hs1, T.sem.lsem, p, r, bits(up))
+        return []
+    gq.append(remote("h1", f_h1, len(up), [fs[2]], after=gq[-1:], boost=300.0))
+    fw, fr = {}, {}
+    for a in range(4):
+        if a == t:
+            dep = [fs[2]]
+            rows = [T.ft[32 * t + 16 * l:32 * t + 16 * l + 16, :] for l in range(2)]
+            qr = [[T.ft[32 * t + 16 * l:32 * t + 16 * l + 16, Q * q:Q * q + Q] for q in range(4)] for l in range(2)]
+        else:
+            snd = helpers(topo, cores[a])[0 if a ^ t == 1 else 1]
+            dep = [arrive("fa%d" % a, "fa%d" % a, len(topo.engines(snd, core)), ARR_FT[a ^ t])]
+            rows = [T.FD[a, 64 * l:64 * l + 64, :] for l in range(2)]
+            qr = [[T.FD[a, 64 * l + q:64 * l + 64:4, :] for q in range(4)] for l in range(2)]
+        if a > 0:
+            fw[a] = dma("fw%d" % a, [(T["FW%d" % a][64 * l + 16 * q:64 * l + 16 * q + 16, :], rows[l]) for l in range(2) for q in range(4)], 1050e3, dep)
+        if a < 3:
+            fr[a] = dma("fr%d" % a, [(T.FR[64 * l + 16 * q:64 * l + 16 * q + 16, Q * a:Q * a + Q], qr[l][q]) for l in range(2) for q in range(4)], 262e3, dep)
+    za, zs = {}, {}
+    for a in range(4):
+        if a == t:
+            za[a], zs[a] = cast[t], T.M16
+        else:
+            za[a], zs[a] = arrive("ma%d" % a, "ma%d" % a, len(topo.engines(cores[a], core)), ARR_MAP[a ^ t]), T.Z16
+    win = {}
+    for a in (t, t ^ 1, t ^ 3, t ^ 2):
+        s = slice(256 * a, 256 * a + 256)
+        hi = ts("hi%d" % a, T.HI[:, s], zs[a][:, s], 1.0 / 32, 192.0 - 31.0 / 64, A.mult, A.add, [za[a]], n=128)
+        t1 = ts("t1%d" % a, T.T1[:, s], T.HI[:, s], -32.0, 6144.0, A.mult, A.add, [hi], n=128)
+        lo = dve("lo%d" % a, 512, [t1], lambda q, s=s, a=a: q.tensor_tensor(T.LO[:, s], zs[a][:, s], T.T1[:, s], A.add))
+        z2 = dma("z%d" % a, [(T.Z2[0:64, 512 * a:512 * a + 512], T.HI[:, s]), (T.Z2[64:128, 512 * a:512 * a + 512], T.LO[:, s])], 130e3, [lo])
+        win[a] = []
+        for j in range(8):
+            p = pe("wp%d_%d" % (a, j), 512, [z2, bw[j]],
+                   lambda q, e, o, j=j, a=a: [q.matmul(pv(o, 0, 512), T.BW[:, 128 * j:128 * j + 128], T.Z2[:, 512 * a:512 * a + 512], True, True)], 3)
+
+            def cp(q, e, o, j=j, a=a, p=p):
+                r = []
+                for x in range(2):
+                    i = 2 * j + x
+                    out = T.MW[:, V * a + i:V * a + V:16]
+                    r.append(q.tensor_copy(out, pv(p, 256 * x, 256 * x + 256)) if e == "dve" else q.activation(out, pv(p, 256 * x, 256 * x + 256), AF.Copy))
+                return r
+            win[a].append(op("wc%d_%d" % (a, j), {"dve": 612 * CY, "act": 680 * CY}, [], cp, uses=p))
+
+    col = {}
+    for p, (r, j) in enumerate(PAIRS):
+        for c in range(3):
+            col[(p, c)] = 192 * p + 64 * c
+        col["%d%d" % (r, j)] = 192 * p
+    for k, x in enumerate(EXTRA):
+        col[x] = LN_X + 64 * k
+    for a in range(4):
+        col["W%d%d" % (a, a ^ 1)] = LN_W + 64 * a
+        col["W%d%d" % (a, a ^ 2)] = LN_W + 256 + 64 * a
+    col["W03"], col["W12"] = LN_W + 512, LN_W + 576
+
+    def LN(x, n=64):
+        return T.LN[:, col[x]:col[x] + n]
+
+    def U(x):
+        return T.U[:, col[x]:col[x] + 64]
+    ln, ul = {}, {}
+    ln["id"] = ts("idl", LN("id"), T.IOT[:, 0:64], 16.0, D(6), A.mult, A.add, [d6, iot])
+    wgt = {}
+    needu = ("01", "23", "02", "13", "03", "12", "20", "21")
+    for a in (t, t ^ 1, t ^ 3, t ^ 2):
+        bs = [b for b in range(4) if b != a and (a, b) != (3, 2)]
+
+        def f(q, e, o, a=a, bs=bs):
+            r = []
+            for n, b in enumerate(bs):
+                for x in range(4):
+                    r.append(q.matmul(pv(o, 64 * n, 64 * n + 64), T.BL[:, 176 * b + 48 - 16 * x:176 * b + 176 - 16 * x],
+                                      zs[a][:, 256 * a + 64 * x:256 * a + 64 * x + 64], x == 0, x == 3))
+            if a < 3:
+                r.append(q.matmul(pv(o, 192, 196), T.OH[:, 128 * a:128 * a + 128], zs[a][:, 256 * a:256 * a + 4], True, True))
+            return r
+        p = pe("lp%d" % a, 832, [za[a]] + [bl[b] for b in bs] + oh[a:a + 1], f, 1)
+        prev = None
+        for n, b in enumerate(bs):
+            x = "%d%d" % (a, b)
+            if x in needu:
+                ul[x] = prev = dve("u" + x, 64, [prev], lambda q, p=p, n=n, x=x: q.tensor_scalar(U(x), pv(p, 64 * n, 64 * n + 64), 2048.0, None, A.add), uses=p)
+            ln[x] = prev = dve("n" + x, 64, [prev], lambda q, p=p, n=n, x=x: q.tensor_scalar(LN(x), pv(p, 64 * n, 64 * n + 64), 2048.0, None, A.add), uses=p)
+        if a < 3:
+            wgt[a] = dve("w%d" % a, 4, [prev], lambda q, p=p, a=a: q.tensor_scalar(T.WC[:, 4 * a:4 * a + 4], pv(p, 192, 196), 2048.0, -1.0, A.add, A.mult), uses=p)
+    for p, (r, j) in enumerate(PAIRS):
+        ln[(p, 0)], ul[(p, 0)] = ln["%d%d" % (r, j)], ul["%d%d" % (r, j)]
+
+    nr = [0]
+    rrow = {}
+
+    def mapg(name, lst, dep, a, b, key, want_u, out_to=None):
+        k = nr[0]
+        nr[0] += 1
+        Rk = T.R[:, Q * k:Q * k + Q]
+        w = T.MW[:, V * a:V * a + V] if a is not None else T.MW[:, 0:5 * V]
+
+        def f(q, e, o):
+            return [q.tensor_copy(Rk, w.indirect(lst)) if e == "dve" else q.activation(Rk, w.indirect(lst), AF.Copy)]
+        dur = {"dve": (Q * GA + 60) * CY, "act": (Q * GA + 80) * CY}
+        if out_to is not None:
+            dur.pop("dve" if b else "act")
+        gth = op("g" + name, dur, dep, f)
+        rrow[name] = k
+
+        def cv(q, e, o):
+            r = []
+            for i in range(16):
+                lt = T.BC[:, 144 * b + 15 - i:144 * b + 143 - i] if out_to is None else T.BO[:, 192 * b + 60 - 4 * i:192 * b + 188 - 4 * i]
+                r.append(q.matmul(pv(o, 0, 64), lt, T.R[:, Q * k + i:Q * k + Q:16], i == 0, i == 15))
+            return r
+        p = pe("cv" + name, 1024, [gth, bc[b] if out_to is None else bo[b]], cv, 1)
+        if out_to is not None:
+            return gth, addc("o" + name, out_to, lambda: pv(p, 0, 64), -4096, [], uses=p)
+        prev = None
+        if want_u:
+            ul[key] = prev = dve("u" + name, 64, [], lambda q: q.tensor_scalar(U(key), pv(p, 0, 64), -4096.0, None, A.add), uses=p)
+            ln[key] = dve("n" + name, 64, [prev], lambda q: q.tensor_scalar(LN(key), pv(p, 0, 64), -4096.0, None, A.add), uses=p)
+        else:
+            ln[key] = addc("n" + name, LN(key), lambda: pv(p, 0, 64), -4096, [], uses=p)
+        return gth, None
+
+    junk = [None, None]
+    nj = [0]
+
+    def evaluate(p, c):
+        r, j = PAIRS[p]
+        k = 3 * p + c
+        h0 = Q * k
+        w = T["FW%d" % j][:, 0:V].indirect(U((p, c)))
+
+        def fh(q, e, o):
+            if e == "dve":
+                return [q.tensor_tensor(T.H[:, h0:h0 + Q], w, T.FR[:, Q * r:Q * r + Q], A.subtract)]
+            return [q.activation(T.H[:, h0:h0 + Q], w, AF.Copy)]
+        hd = {"dve": (Q * GA + 60) * CY}
+        if ACT_H:
+            hd["act"] = (Q * GA + 80) * CY
+        hg = op("h%d%d" % (p, c), hd, [fw[j], fr[r], ul[(p, c)]], fh)
+
+        def f(q, e, o):
+            I, NI, NS, S = [T.ID[:, 128 * x:128 * x + 128] for x in range(4)]
+            terms = [(T.H, h0, I, NI, NS)] + ([(T.FR, Q * r, NI, I, S)] if hg["eng"] == "act" else [])
+            res = []
+            for n, (B, z, P, M, W) in enumerate(terms):
+                res += [q.matmul(pv(o, 0, 512), P, B[:, z:z + 512], n == 0, False),
+                        q.matmul(pv(o, 0, 512), M, B[:, z + 1:z + 513], False, n == len(terms) - 1)]
+            for n, (B, z, P, M, W) in enumerate(terms):
+                res += [q.matmul(pv(o, 512, 1024), P, B[:, z + 512:z + Q], n == 0, False),
+                        q.matmul(pv(o, 512, 1023), M, B[:, z + 513:z + Q], False, False),
+                        q.matmul(pv(o, 1023, 1024), W, B[:, z:z + 1], False, n == len(terms) - 1)]
+            return res
+        df = pe("df%d%d" % (p, c), 2112, [hg, fr[r]] + idm, f, 2)
+        hg["twice"] = df
+        acc = T.AC[:, 4 * p + c:4 * p + c + 1]
+
+        def ab(q, e, o):
+            if e == "dve":
+                return [q.tensor_reduce(acc, pv(df, 0, Q), AxisListType.X, A.add, apply_absolute_value=True)]
+            x = nj[0] % 2
+            nj[0] += 1
+            if junk[x] is not None:
+                o["wait"](junk[x])
+            junk[x] = o
+            return [q.activation(T.JK[:, Q * x:Q * x + Q], pv(df, 0, Q), AF.Abs, accum_out=acc)]
+        return op("ab%d%d" % (p, c), {"dve": (Q + 60) * CY, "act": (Q + 110) * CY}, [ac0], ab, uses=df)
+
+    base = {}
+
+    def decide(p, abs_, nsel):
+        r, j = PAIRS[p]
+        n0 = 256 * p
+        L = [ln[(p, c)] for c in range(3)]
+        c0 = col[(p, 0)]
+        n1 = dve("ne1%d" % p, 256, L, lambda q: q.tensor_tensor(T.NE[:, n0:n0 + 128], T.LN[:, c0:c0 + 128], T.LN[:, c0 + 64:c0 + 192], A.not_equal))
+        n2 = dve("ne2%d" % p, 128, L, lambda q: q.tensor_tensor(T.NE[:, n0 + 128:n0 + 192], T.LN[:, c0 + 128:c0 + 192], T.LN[:, c0:c0 + 64], A.not_equal))
+        wcol = T.WC[:, 4 * r + (r ^ j) - 1:4 * r + (r ^ j)]
+        es = []
+        for c in range(3):
+            s = n0 + 64 * ((c + 1) % 3)
+            es.append(op("e%d%d" % (p, c), {"act": 180 * CY}, [n1, n2, wgt[r], ec0],
+                         lambda q, e, o, s=s, c=c: [q.activation(T.JS[:, 64 * (3 * p + c):64 * (3 * p + c) + 64], T.NE[:, s:s + 64], AF.Identity,
+                                                                 scale=wcol, accum_out=T.EC[:, 4 * p + c:4 * p + c + 1])]))
+        sc = pe("sc%d" % p, 512, es + abs_ + [one],
+                lambda q, e, o: [q.matmul(pv(o, 0, 4), T.ONE[:], T.EC[:, 4 * p:4 * p + 4], True, False),
+                                 q.matmul(pv(o, 0, 4), T.ONE[:], T.AC[:, 4 * p:4 * p + 4], False, True)], 1)
+        F = [T.FL[:, 4 * p + x:4 * p + x + 1] for x in range(3)]
+        f2 = dve("f2%d" % p, 1, [], lambda q: q.tensor_scalar(F[2], pv(sc, 0, 1), pv(sc, 1, 2), pv(sc, 2, 3), A.min, A.is_gt), uses=sc)
+        f1 = dve("f1%d" % p, 1, [], lambda q: q.tensor_scalar(F[1], pv(sc, 0, 1), pv(sc, 1, 2), 64.0, A.is_gt, A.mult), uses=sc)
+        fw_ = ts("fw%d" % p, F[0], F[2], 128.0, F[1], A.mult, A.max, [f1, f2])
+        if p == 0:
+            b1 = ts("b1", T.FL[:, 26:27], F[0], 64.0, None, A.mult, None, [fw_])
+            base["X01"] = (T.FL[:, 24:25], ts("b01", T.FL[:, 24:25], F[2], 2.0 * V, T.FL[:, 26:27], A.mult, A.add, [b1]))
+        if p == 1:
+            base["X23"] = (T.FL[:, 25:26], ts("b23", T.FL[:, 25:26], F[0], 64.0, 2.0 * V, A.mult, A.add, [fw_]))
+        return ts("of%d" % p, T.OF[:, 16 * p:16 * p + 4 * nsel], T.PC[:, 0:4 * nsel], F[0], None, A.add, None, [fw_, pc])
+
+    ntb, nus = [0], [0]
+
+    def select(p, of, tables):
+        b0 = 192 * ntb[0]
+        ntb[0] += len(tables)
+        fill = []
+        for k, tb in enumerate(tables):
+            for c, (a, x) in enumerate(tb):
+                o0 = b0 + 192 * k + 64 * c
+                if a in base:
+                    fill.append(addc("tb%d%d%d" % (p, k, c), T.TB[:, o0:o0 + 64], (LN(x),), base[a][:1], [ln[x], base[a][1]]))
+                else:
+                    fill.append(addc("tb%d%d%d" % (p, k, c), T.TB[:, o0:o0 + 64], (LN(x),), V * a, [ln[x]]))
+        n = len(tables)
+        u0 = 64 * nus[0]
+        nus[0] += n
+        s = dve("sl%d" % p, 64 * n * GA, fill + [of],
+                lambda q: q.tensor_copy(T.US[:, u0:u0 + 64 * n], T.TB[:, b0:b0 + 192 * n].indirect(T.OF[:, 16 * p:16 * p + 4 * n])))
+        return s, [T.US[:, u0 + 64 * k:u0 + 64 * k + 64] for k in range(n)]
+
+    def chosen(p, of, key=None, at=None):
+        c0 = col[(p, 0)]
+        w = T.LN[:, c0:c0 + 192].indirect(T.OF[:, 16 * p:16 * p + 4])
+        dep = [of] + [ln[(p, c)] for c in range(3)]
+        if key is not None:
+            ln[key] = dve("ch" + key, 100, dep, lambda q: q.tensor_copy(LN(key), w))
+            return None
+        u0 = 64 * nus[0]
+        nus[0] += 1
+        if at is not None:
+            return (dve("cu%d" % p, 100, dep + [base[at][1]], lambda q: q.tensor_scalar(T.US[:, u0:u0 + 64], w, base[at][0], None, A.add)),
+                    T.US[:, u0:u0 + 64])
+        return dve("cu%d" % p, 100, dep, lambda q: q.tensor_copy(T.US[:, u0:u0 + 64], w)), T.US[:, u0:u0 + 64]
+
+    def renew(name, maps, dep):
+        prs = []
+        for x, a, b in maps:
+            k = rrow[x]
+            for dg in range(2):
+                r = 4 * dg + b
+                for q in range(4):
+                    prs.append((T.MW[16 * q + r:128:64, V * a:V * a + V], T.R[r:128:16, Q * k:Q * k + Q]))
+        return dma(name, prs, 16e3 * len(prs), dep)
+
+    outs = []
+
+    def ship(name, d, dests, dep, late):
+        far_ = [a for a in dests if a != t]
+        if t in dests:
+            outs.append(dma("y%d%d" % (t, d), [(T.ym[32 * t:32 * t + 32, 256 * (d - 1):256 * d], T.OUT[:, 64 * (4 * (d - 1) + t):64 * (4 * (d - 1) + t) + 64])],
+                            32e3, dep + late))
+        if not far_:
+            return
+        es = topo.engines(core, cores[far_[0]])
+        per = {1: len(es), 2: len(es) // 2, 3: len(es) // 4}[len(far_)]
+
+        def f(q):
+            q.remote_dma_fused([RemoteDMATransfer(dst_ids=[dst(cores[a])], dma_engine_mask=bits(es[per * n:per * n + per]), remote_sem=T.sem["oa%d" % (3 * t + d - 1)],
+                                                  src=T.OUT[:, 64 * (4 * (d - 1) + a):64 * (4 * (d - 1) + a) + 64],
+                                                  dst=T.YL[:, 64 * (3 * t + d - 1):64 * (3 * t + d - 1) + 64]) for n, a in enumerate(far_)], local_sem=T.sem.lsem)
+            return []
+        gq.append(remote(name, f, per * len(far_), dep, after=gq[-1:], boost=(30.0, 14.0, 6.5)[d - 1]))
+        return gq[-1]
+
+    def turn(name, key, n, o0, dep):
+        p = pe("tp" + name, 4 * n, dep + [pm], lambda q, e, o: [q.matmul(pv(o, 0, n), T.PM[:], LN(key, n), True, True)], 1)
+        return addc("to" + name, T.OUT[:, o0:o0 + n], lambda: pv(p, 0, n), 0, [], n=n, uses=p)
+
+    allwin = win[0] + win[1] + win[2] + win[3]
+    ab = {(p, 0): evaluate(p, 0) for p in range(6)}
+    G = []
+    for name, a, b, x, key, wu in (("C011", 2, 1, "02", (0, 1), True), ("C012", 3, 1, "03", (0, 2), True), ("C231", 0, 3, "20", (1, 1), True),
+                                   ("C232", 1, 3, "21", (1, 2), True), ("IC", 2, 0, "12", "IC", False)):
+        G.append(mapg(name, U(x), [ul[x]] + win[a], a, b, key, wu)[0])
+    for p in (0, 1):
+        for c in (1, 2):
+            ab[(p, c)] = evaluate(p, c)
+    fill4 = [dve("m4%d" % x, 512, [], lambda q, x=x: q.memset(T.MW[:, 4 * V + Q * x:4 * V + Q * x + Q], 0.0)) for x in range(4)]
+    nw0 = renew("nw0", [("C011", 1, 1), ("C012", 4, 1), ("C231", 3, 3), ("C232", 4, 3)], G + allwin + fill4)
+    of0 = decide(0, [ab[(0, c)] for c in range(3)], 2)
+    of1 = decide(1, [ab[(1, c)] for c in range(3)], 3)
+    G = []
+    cu, lst = chosen(0, of0)
+    G.append(mapg("C021", lst, [cu, nw0], 1, 2, (2, 1), True)[0])
+    s0, l0 = select(0, of0, [[(0, "10"), (0, "IC"), (1, "id")], [(1, "id"), (2, "12"), (3, "13")]])
+    s1, l1 = select(1, of1, [[(3, "03"), (0, "id"), (1, (0, 2))], [(2, "12"), (0, "IC"), (1, "id")], [(3, "id"), (0, "30"), (1, "31")]])
+    G.append(mapg("C131", l0[0], [s0, nw0], None, 3, (3, 1), True)[0])
+    G.append(mapg("C022", l1[0], [s1, nw0], None, 2, (2, 2), True)[0])
+    G.append(mapg("C132", l1[1], [s1, nw0], None, 3, (3, 2), True)[0])
+    G.append(mapg("W10", l0[1], [s0, nw0], None, 0, "W10", False)[0])
+    G.append(mapg("W32", l1[2], [s1, nw0], None, 2, "W32", False)[0])
+    nw1 = renew("nw1", [("W32", 3, 2), ("W10", 1, 0)], G)
+    chosen(0, of0, "W01")
+    chosen(1, of1, "W23")
+    o1 = turn("1", "W01", 256, 0, [ln[x] for x in ("W01", "W10", "W23", "W32")])
+    for p in (2, 3):
+        for c in (1, 2):
+            ab[(p, c)] = evaluate(p, c)
+    of2 = decide(2, [ab[(2, c)] for c in range(3)], 2)
+    of3 = decide(3, [ab[(3, c)] for c in range(3)], 2)
+    G = []
+    cu2, lst2 = chosen(2, of2, at="X23")
+    cu3, lst3 = chosen(3, of3)
+    s2, l2 = select(2, of2, [[(0, "W10"), (1, "id"), (3, (3, 1))], [(2, "id"), (1, "21"), (3, "W23")]])
+    s3, l3 = select(3, of3, [[(1, "W01"), (0, "id"), ("X23", (2, 1))], [(3, "id"), ("X01", "30"), (2, "W32")]])
+    G.append(mapg("C032", lst2, [cu2, nw1], None, 3, (4, 2), True)[0])
+    G.append(mapg("C121", l2[0], [s2, nw1], None, 2, (5, 1), True)[0])
+    G.append(mapg("C031", l3[0], [s3, nw1], None, 3, (4, 1), True)[0])
+    G.append(mapg("C122", lst3, [cu3, nw1], 3, 2, (5, 2), True)[0])
+    G.append(mapg("W20", l2[1], [s2, nw1], None, 0, "W20", False)[0])
+    G.append(mapg("W31", l3[1], [s3, nw1], None, 1, "W31", False)[0])
+    nw2 = renew("nw2", [("W20", 2, 0), ("W31", 3, 1)], G)
+    chosen(2, of2, "W02")
+    chosen(3, of3, "W13")
+    o2 = turn("2", "W02", 256, 256, [ln[x] for x in ("W02", "W13", "W20", "W31")])
+    for p in (4, 5):
+        for c in (1, 2):
+            ab[(p, c)] = evaluate(p, c)
+    of4 = decide(4, [ab[(4, c)] for c in range(3)], 1)
+    of5 = decide(5, [ab[(5, c)] for c in range(3)], 1)
+    s4, l4 = select(4, of4, [[(3, "id"), (1, "W31"), (2, "W32")]])
+    s5, l5 = select(5, of5, [[(2, "id"), ("X01", "W20"), (3, "W23")]])
+    o30 = mapg("W30", l4[0], [s4, nw2], None, 0, None, False, out_to=T.OUT[:, 64 * 11:64 * 12])[1]
+    o21 = mapg("W21", l5[0], [s5, nw2], None, 1, None, False, out_to=T.OUT[:, 64 * 10:64 * 11])[1]
+    chosen(4, of4, "W03")
+    chosen(5, of5, "W12")
+    o3 = turn("3", "W03", 128, 512, [ln["W03"], ln["W12"]])
+    x1 = ship("x1", 1, [0, 1, 2, 3], [o1], [nw1])
+    x2 = ship("x2", 2, [0, 1, 2, 3], [o2], [nw2])
+    x3 = ship("x3", 3, [0, 1], [o3], [])
+    x4 = ship("x4", 3, [2, 3], [o30, o21], [])
+    for d, mine, late in ((1, o1, [nw2]), (2, o2, [of4]), (3, o3 if t < 2 else o21, [])):
+        for s in range(4):
+            if s == t:
+                continue
+            ne = len(topo.engines(cores[s], core))
+            grp = [a for a in ([0, 1, 2, 3] if d < 3 else ([0, 1] if t < 2 else [2, 3])) if a != s]
+            k = 3 * s + d - 1
+            ar = arrive("oa%d" % k, "oa%d" % k, {1: ne, 2: ne // 2, 3: ne // 4}[len(grp)], 0.0, [mine])
+            ar["tail"] = 4.0
+            outs.append(dma("y%d%d" % (s, d), [(T.ym[32 * s:32 * s + 32, 256 * (d - 1):256 * d], T.YL[:, 64 * k:64 * k + 64])], 32e3, [ar] + late,
+                            queues=("sp", "act") if d == 3 else ("sp",)))
+    return ops
+
+
+def rank_program(g, core, T, topo):
+    rank = T.rank_of(core)
+    if rank is None:
+        for a, c in enumerate(T.cores):
+            near, far = helpers(topo, c)
+            if core not in (near, far):
+                continue
+            up = len(topo.engines(c, near)) // 2
+            jobs = [(0, 1, "hs0", up // 2)] if core == near else [(1, 3, "hs0", up // 2), (2, 2, "hs1", up)]
+            n = 0
+            for k, d, s, v in jobs:
+                to = T.cores[a ^ d]
+                r, p, _ = topo.addr(to)
+                g.wait_ge(T.sem[s], v)
+                g.remote_dma(T.FD[a], T.FS[:, Q * k:Q * k + Q], T.sem["fa%d" % a], T.sem.lsem, p, r, topo.mask(core, to))
+                n += len(topo.engines(core, to))
+            g.wait_ge(T.sem.lsem, n)
+        return
+    order = plan(build(rank, T, topo, core), SEEDS[rank])
+    queue = {"pe": g.tensor, "dve": g.vector, "act": g.scalar, "sp": g.sync, "g": g}
+    own = {"pe": "pe", "dve": "dve", "act": "act", "g": "pool"}
+    count = {}
+    seen = {}
+
+    def wait(e, d):
+        if "tok" not in d:
+            return
+        s, v = d["tok"]
+        if seen.get((e, s), 0) < v:
+            queue[e].wait_ge(T.sem[s], v)
+            seen[(e, s)] = v
+
+    for o in order:
+        e = o["eng"]
+        if e == "arr":
+            count[o["tok"][0]] = o["tok"][1]
+            continue
+        need = {}
+        for d in o["deps"]:
+            if "tok" in d and d["tok"][1] > need.get(d["tok"][0], {"tok": (0, 0)})["tok"][1]:
+                need[d["tok"][0]] = d
+        for d in need.values():
+            wait(e, d)
+        o["wait"] = lambda d, e=e: wait(e, d)
+        ins = o["fn"](queue[e], e, o)
+        if "lsem" in o:
+            count["lsem"] = count.get("lsem", 0) + o["lsem"]
+            continue
+        s, step = (o["sem"], 16) if o["sem"] else (own[e], 1)
+        for x in ins:
+            x.then_inc(T.sem[s], step)
+        count[s] = count.get(s, 0) + step * len(ins)
+        o["tok"] = (s, count[s])
+    for s, v in count.items():
+        g.wait_ge(T.sem[s], v)

@@ -3,12 +3,14 @@ from concourse.bass import DstId, RemoteDMATransfer
 from concourse.mybir import AluOpType as A, AxisListType, ActivationFunctionType as AF
 
 N, V, Q = 4, 4096, 1024
-ACT_H = True
-SEEDS = [[19, 61898, 34908, 66228, 64185, 5699, 11932, 68760, 45576, 13228, 76997], [78, 17509],
-         [74, 56747, 72125, 1906, 30423, 43207, 29139, 88216], [43, 66308, 1922, 30483, 32589, 16691, 18544]]
+ACT_H = False
+PASSES = ((0, None), (1, None), (2, 3))
+SEEDS = [[31, 80725, 3044, 65945, 8560, 61206, 57262, 25811, 67318], [124, 32876, 9405, 79899, 72206, 46818, 85960, 86616, 93005, 57730, 59866, 79372],
+         [122, 85383, 56362, 13238, 89976, 4429, 99622, 36666, 16093, 78920, 94701, 79383, 30889],
+         [122, 91852, 30353, 45049, 14138, 61100, 45163, 44008, 12483, 39688]]
 PAIRS = [(0, 1), (2, 3), (0, 2), (1, 3), (0, 3), (1, 2)]
-EXTRA = ["10", "20", "21", "30", "31", "IC", "id"]
-NR, NTB = 19, 11
+EXTRA = ["10", "20", "21", "30", "31", "id"]
+NR, NTB = 18, 11
 LN_X = 6 * 192
 LN_W = LN_X + 64 * len(EXTRA)
 LN_END = LN_W + 256 + 256 + 128
@@ -56,7 +58,7 @@ SCRATCH = {
     "MK": ("sbuf", [128, 8], "float32"),
     "PC": ("sbuf", [128, 16], "float32"),
     "EW": ("sbuf", [128, 128], "bfloat16"),
-    "BW": ("sbuf", [128, 1024], "bfloat16"),
+    "BW": ("sbuf", [128, 1040], "bfloat16"),
     "BC": ("sbuf", [128, 4 * 144], "bfloat16"),
     "BO": ("sbuf", [128, 2 * 192], "bfloat16"),
     "BL": ("sbuf", [128, 4 * 176], "float16"),
@@ -74,16 +76,16 @@ SCRATCH = {
 SEMAPHORES = (["pe", "dve", "act", "pool", "lsem", "hs0", "hs1"] + ["ma%d" % a for a in range(4)] + ["fa%d" % a for a in range(4)]
               + ["oa%d" % k for k in range(12)] + ["d%d" % k for k in range(48)])
 
-CY, PCY, GA, LAT = 1.04e-3, 0.52e-3, 1.56, 0.12
-ARR_MAP = {1: 8.5, 3: 10.0, 2: 11.5}
-ARR_FT = {1: 13.0, 3: 15.0, 2: 21.0}
+CY, PCY, GA, LAT = 0.92e-3, 0.48e-3, 1.5, 0.12
+ARR_MAP = {1: 9.5, 3: 11.0, 2: 12.5}
+ARR_FT = {1: 14.5, 3: 16.5, 2: 20.0}
 ISSUE, DLAT, DRATE = 0.08, 2.0, 250e3
 
 
 def helpers(topo, core):
     near = [c for c in topo.cores_of(core) if c != core and topo.die(c) == topo.die(core)]
     far = [c for c in topo.cores_of(core) if topo.die(c) != topo.die(core)]
-    return near[0], far[0]
+    return near[0], far[0], far[1]
 
 
 def bits(es):
@@ -228,7 +230,7 @@ def build(t, T, topo, core):
 
     cores = T.cores
     a0 = t
-    pad = dve("pad", 1024, [], lambda q: q.memset(T.M[32 * a0:32 * a0 + 32, :, :], 2048))
+    pad = dve("pad", 16, [], lambda q: q.memset(T.M[32 * a0:32 * a0 + 32, :, 0:4], 2048))
     ml = {}
     for tt in (t ^ 1, t ^ 3, t ^ 2, t):
         prs = [(T.M[32 * b:32 * b + 32, tt, :], T.mp[32 * tt:32 * tt + 32, 256 * ((a0 ^ b) - 1):256 * (a0 ^ b)]) for b in range(4) if b != a0]
@@ -248,6 +250,8 @@ def build(t, T, topo, core):
     iot = gop("iot", 192, lambda q: q.iota(T.IOT[:], [[1, 192]], 0, 0, allow_small_or_imprecise_dtypes=True))
     iot2 = gop("iot2", 128, lambda q: q.iota(T.IOT2[:], [[64, 2], [0, 4], [1, 16]], 0, 0, allow_small_or_imprecise_dtypes=True))
     iot3 = gop("iot3", 16, lambda q: q.iota(T.IOT3[:], [[192, 4], [16, 4]], 0, 0, allow_small_or_imprecise_dtypes=True))
+    pad2 = gop("pad2", 1008, lambda q: q.iota(T.M[32 * a0:32 * a0 + 32, :, 4:256], [[0, 1008]], 2048, 0))
+    pad2["deps"].append(iot3)
     k0 = T.KI[:, 0:1]
     ci = [ts("c0", T.CI[:, 0:1], k0, 15, None, A.bitwise_and, None, [ki]),
           ts("c1", T.CI[:, 1:2], k0, 112, None, A.bitwise_and, None, [ki]),
@@ -284,10 +288,11 @@ def build(t, T, topo, core):
     mk = ts("mk", T.MK[:], T.IOT[:, 0:8], C(9), None, A.is_equal, None, [cf, iot])
     pc = ts("pc", T.PC[:], T.IOT3[:], C(0), None, A.add, None, [cf, iot3])
     ew = ts("ew", T.EW[:], T.IOT2[:], D(4), None, A.is_equal, None, [d4, iot2], n=128)
+    bw0 = dve("bw", 8, [], lambda q: q.memset(T.BW[:, 0:16], 0.0))
     bw = []
     for i in range(8):
         def f(q, e, o, i=i):
-            out = T.BW[:, 128 * i:128 * i + 128]
+            out = T.BW[:, 16 + 128 * i:144 + 128 * i]
             if e == "dve":
                 return [q.tensor_scalar(out, T.EW[:], T.MK[:, i:i + 1], None, A.mult)]
             return [q.activation(out, T.EW[:], AF.Identity, scale=T.MK[:, i:i + 1])]
@@ -304,9 +309,9 @@ def build(t, T, topo, core):
     one = dve("one", 128, [], lambda q: q.memset(T.ONE[:], 1.0))
     ac0 = dve("ac0", 24, [], lambda q: q.memset(T.AC[:], 0.0))
     ec0 = dve("ec0", 24, [], lambda q: q.memset(T.EC[:], 0.0))
-    cast = {tt: ts("cast%d" % tt, T.M16[:, 256 * tt:256 * tt + 256], T.M[:, tt, :], -2048.0, None, A.add, None, [ml[tt], lam, pad], n=256)
+    cast = {tt: ts("cast%d" % tt, T.M16[:, 256 * tt:256 * tt + 256], T.M[:, tt, :], -2048.0, None, A.add, None, [ml[tt], lam, pad, pad2], n=256)
             for tt in (t ^ 1, t ^ 3, t ^ 2, t)}
-    near, far = helpers(topo, core)
+    near, far, far2 = helpers(topo, core)
     up = topo.engines(core, near)
     up = up[len(up) // 2:]
     h = len(up) // 2
@@ -321,7 +326,7 @@ def build(t, T, topo, core):
             RemoteDMATransfer(dst_ids=[dst(far)], dma_engine_mask=bits(up[h:]), remote_sem=T.sem.hs0, src=T.FS[:, Q:2 * Q], dst=T.FS[:, Q:2 * Q])],
             local_sem=T.sem.lsem)
         return []
-    sends = []
+    gq.append(remote("h0", f_h0, 2 * h, [fs[1], fs[3]], after=gq[-1:]))
     for d in (1, 3, 2):
         tt = t ^ d
 
@@ -331,11 +336,9 @@ def build(t, T, topo, core):
             return []
         o = remote("sm%d" % d, f, len(topo.engines(core, cores[tt])), [cast[tt]], after=gq[-1:], boost=300.0)
         gq.append(o)
-        if d == 1:
-            gq.append(remote("h0", f_h0, 2 * h, [fs[1], fs[3]], after=gq[-1:]))
 
     def f_h1(q):
-        r, p, _ = topo.addr(far)
+        r, p, _ = topo.addr(far2)
         q.remote_dma(T.FS[:, 2 * Q:3 * Q], T.FS[:, 2 * Q:3 * Q], T.sem.hs1, T.sem.lsem, p, r, bits(up))
         return []
     gq.append(remote("h1", f_h1, len(up), [fs[2]], after=gq[-1:], boost=300.0))
@@ -346,7 +349,7 @@ def build(t, T, topo, core):
             rows = [T.ft[32 * t + 16 * l:32 * t + 16 * l + 16, :] for l in range(2)]
             qr = [[T.ft[32 * t + 16 * l:32 * t + 16 * l + 16, Q * q:Q * q + Q] for q in range(4)] for l in range(2)]
         else:
-            snd = helpers(topo, cores[a])[0 if a ^ t == 1 else 1]
+            snd = helpers(topo, cores[a])[(1, 3, 2).index(a ^ t)]
             dep = [arrive("fa%d" % a, "fa%d" % a, len(topo.engines(snd, core)), ARR_FT[a ^ t])]
             rows = [T.FD[a, 64 * l:64 * l + 64, :] for l in range(2)]
             qr = [[T.FD[a, 64 * l + q:64 * l + 64:4, :] for q in range(4)] for l in range(2)]
@@ -360,17 +363,24 @@ def build(t, T, topo, core):
             za[a], zs[a] = cast[t], T.M16
         else:
             za[a], zs[a] = arrive("ma%d" % a, "ma%d" % a, len(topo.engines(cores[a], core)), ARR_MAP[a ^ t]), T.Z16
-    win = {}
+    win, zz = {}, {}
     for a in (t, t ^ 1, t ^ 3, t ^ 2):
         s = slice(256 * a, 256 * a + 256)
         hi = ts("hi%d" % a, T.HI[:, s], zs[a][:, s], 1.0 / 32, 192.0 - 31.0 / 64, A.mult, A.add, [za[a]], n=128)
         t1 = ts("t1%d" % a, T.T1[:, s], T.HI[:, s], -32.0, 6144.0, A.mult, A.add, [hi], n=128)
         lo = dve("lo%d" % a, 512, [t1], lambda q, s=s, a=a: q.tensor_tensor(T.LO[:, s], zs[a][:, s], T.T1[:, s], A.add))
         z2 = dma("z%d" % a, [(T.Z2[0:64, 512 * a:512 * a + 512], T.HI[:, s]), (T.Z2[64:128, 512 * a:512 * a + 512], T.LO[:, s])], 130e3, [lo])
+        zz[a] = z2
+    for da, db in PASSES:
+        a, b = t ^ da, (None if db is None else t ^ db)
         win[a] = []
         for j in range(8):
-            p = pe("wp%d_%d" % (a, j), 512, [z2, bw[j]],
-                   lambda q, e, o, j=j, a=a: [q.matmul(pv(o, 0, 512), T.BW[:, 128 * j:128 * j + 128], T.Z2[:, 512 * a:512 * a + 512], True, True)], 3)
+            def wp(q, e, o, j=j, a=a, b=b):
+                r = [q.matmul(pv(o, 0, 512), T.BW[:, 16 + 128 * j:144 + 128 * j], T.Z2[:, 512 * a:512 * a + 512], True, b is None)]
+                if b is not None:
+                    r.append(q.matmul(pv(o, 0, 512), T.BW[:, 8 + 128 * j:136 + 128 * j], T.Z2[:, 512 * b:512 * b + 512], False, True))
+                return r
+            p = pe("wp%d_%d" % (a, j), 512 if b is None else 1024, [zz[a], zz.get(b), bw0, bw[j]] + bw[max(j - 1, 0):j], wp, 3)
 
             def cp(q, e, o, j=j, a=a, p=p):
                 r = []
@@ -380,6 +390,10 @@ def build(t, T, topo, core):
                     r.append(q.tensor_copy(out, pv(p, 256 * x, 256 * x + 256)) if e == "dve" else q.activation(out, pv(p, 256 * x, 256 * x + 256), AF.Copy))
                 return r
             win[a].append(op("wc%d_%d" % (a, j), {"dve": 612 * CY, "act": 680 * CY}, [], cp, uses=p))
+        if b is None:
+            continue
+        win[b] = [dma("mv%d" % b, [(T.MW[0:120, V * b:V * b + V], T.MW[8:128, V * a:V * a + V]),
+                                   (T.MW[120:128, V * b:V * b + V], T.MW[0:8, V * a:V * a + V])], 1050e3, win[a])]
 
     col = {}
     for p, (r, j) in enumerate(PAIRS):
@@ -455,7 +469,7 @@ def build(t, T, topo, core):
         prev = None
         if want_u:
             ul[key] = prev = dve("u" + name, 64, [], lambda q: q.tensor_scalar(U(key), pv(p, 0, 64), -4096.0, None, A.add), uses=p)
-            ln[key] = dve("n" + name, 64, [prev], lambda q: q.tensor_scalar(LN(key), pv(p, 0, 64), -4096.0, None, A.add), uses=p)
+            ln[key] = addc("n" + name, LN(key), lambda: pv(p, 0, 64), -4096, [prev], uses=p)
         else:
             ln[key] = addc("n" + name, LN(key), lambda: pv(p, 0, 64), -4096, [], uses=p)
         return gth, None
@@ -607,20 +621,25 @@ def build(t, T, topo, core):
     ab = {(p, 0): evaluate(p, 0) for p in range(6)}
     G = []
     for name, a, b, x, key, wu in (("C011", 2, 1, "02", (0, 1), True), ("C012", 3, 1, "03", (0, 2), True), ("C231", 0, 3, "20", (1, 1), True),
-                                   ("C232", 1, 3, "21", (1, 2), True), ("IC", 2, 0, "12", "IC", False)):
+                                   ("C232", 1, 3, "21", (1, 2), True)):
         G.append(mapg(name, U(x), [ul[x]] + win[a], a, b, key, wu)[0])
     for p in (0, 1):
         for c in (1, 2):
             ab[(p, c)] = evaluate(p, c)
-    fill4 = [dve("m4%d" % x, 512, [], lambda q, x=x: q.memset(T.MW[:, 4 * V + Q * x:4 * V + Q * x + Q], 0.0)) for x in range(4)]
+    def zero(q, e, o, x):
+        out = T.MW[:, 4 * V + Q * x:4 * V + Q * x + Q]
+        return [q.memset(out, 0.0) if e == "dve" else q.activation(out, T.FS[:, 0:Q], AF.Copy, scale=0.0)]
+    fill4 = [op("m4%d" % x, {"act": 1100 * CY}, [fs[1]], lambda q, e, o, x=x: zero(q, e, o, x)) for x in range(4)]
+    for o in fill4:
+        o["boost"] = 250.0
     nw0 = renew("nw0", [("C011", 1, 1), ("C012", 4, 1), ("C231", 3, 3), ("C232", 4, 3)], G + allwin + fill4)
     of0 = decide(0, [ab[(0, c)] for c in range(3)], 2)
     of1 = decide(1, [ab[(1, c)] for c in range(3)], 3)
     G = []
     cu, lst = chosen(0, of0)
     G.append(mapg("C021", lst, [cu, nw0], 1, 2, (2, 1), True)[0])
-    s0, l0 = select(0, of0, [[(0, "10"), (0, "IC"), (1, "id")], [(1, "id"), (2, "12"), (3, "13")]])
-    s1, l1 = select(1, of1, [[(3, "03"), (0, "id"), (1, (0, 2))], [(2, "12"), (0, "IC"), (1, "id")], [(3, "id"), (0, "30"), (1, "31")]])
+    s0, l0 = select(0, of0, [[(0, "10"), (3, "12"), (1, "id")], [(1, "id"), (2, "12"), (3, "13")]])
+    s1, l1 = select(1, of1, [[(3, "03"), (0, "id"), (1, (0, 2))], [(2, "12"), (3, "12"), (1, "id")], [(3, "id"), (0, "30"), (1, "31")]])
     G.append(mapg("C131", l0[0], [s0, nw0], None, 3, (3, 1), True)[0])
     G.append(mapg("C022", l1[0], [s1, nw0], None, 2, (2, 2), True)[0])
     G.append(mapg("C132", l1[1], [s1, nw0], None, 3, (3, 2), True)[0])
@@ -661,17 +680,19 @@ def build(t, T, topo, core):
     o21 = mapg("W21", l5[0], [s5, nw2], None, 1, None, False, out_to=T.OUT[:, 64 * 10:64 * 11])[1]
     chosen(4, of4, "W03")
     chosen(5, of5, "W12")
-    o3 = turn("3", "W03", 128, 512, [ln["W03"], ln["W12"]])
+    o03 = turn("03", "W03", 64, 512, [ln["W03"]])
+    o12 = turn("12", "W12", 64, 576, [ln["W12"]])
+    o3 = [o03, o12, o21, o30]
     x1 = ship("x1", 1, [0, 1, 2, 3], [o1], [nw1])
     x2 = ship("x2", 2, [0, 1, 2, 3], [o2], [nw2])
-    x3 = ship("x3", 3, [0, 1], [o3], [])
-    x4 = ship("x4", 3, [2, 3], [o30, o21], [])
-    for d, mine, late in ((1, o1, [nw2]), (2, o2, [of4]), (3, o3 if t < 2 else o21, [])):
+    for a in (1, 2, 0, 3):
+        ship("x3%d" % a, 3, [a], [o3[a]], [])
+    for d, mine, late in ((1, o1, [nw2]), (2, o2, [of5]), (3, o3[t], [])):
         for s in range(4):
             if s == t:
                 continue
             ne = len(topo.engines(cores[s], core))
-            grp = [a for a in ([0, 1, 2, 3] if d < 3 else ([0, 1] if t < 2 else [2, 3])) if a != s]
+            grp = [a for a in ([0, 1, 2, 3] if d < 3 else [t]) if a != s]
             k = 3 * s + d - 1
             ar = arrive("oa%d" % k, "oa%d" % k, {1: ne, 2: ne // 2, 3: ne // 4}[len(grp)], 0.0, [mine])
             ar["tail"] = 4.0
@@ -684,11 +705,11 @@ def rank_program(g, core, T, topo):
     rank = T.rank_of(core)
     if rank is None:
         for a, c in enumerate(T.cores):
-            near, far = helpers(topo, c)
-            if core not in (near, far):
+            hs = helpers(topo, c)
+            if core not in hs:
                 continue
-            up = len(topo.engines(c, near)) // 2
-            jobs = [(0, 1, "hs0", up // 2)] if core == near else [(1, 3, "hs0", up // 2), (2, 2, "hs1", up)]
+            up = len(topo.engines(c, core)) // 2
+            jobs = [((0, 1, "hs0", up // 2), (1, 3, "hs0", up // 2), (2, 2, "hs1", up))[hs.index(core)]]
             n = 0
             for k, d, s, v in jobs:
                 to = T.cores[a ^ d]

@@ -2,99 +2,121 @@ import numpy as np
 from concourse.bass import DstId, RemoteDMATransfer
 from concourse.mybir import AluOpType as A, AxisListType, ActivationFunctionType as AF
 
-N, V, Q = 4, 4096, 1024
-ACT_H = False
-PASSES = ((0, None), (1, None), (2, 3))
-SEEDS = [[31, 80725, 3044, 65945, 8560, 61206, 57262, 25811, 67318], [124, 32876, 9405, 79899, 72206, 46818, 85960, 86616, 93005, 57730, 59866, 79372],
-         [122, 85383, 56362, 13238, 89976, 4429, 99622, 36666, 16093, 78920, 94701, 79383, 30889],
-         [122, 91852, 30353, 45049, 14138, 61100, 45163, 44008, 12483, 39688]]
-PAIRS = [(0, 1), (2, 3), (0, 2), (1, 3), (0, 3), (1, 2)]
-EXTRA = ["10", "20", "21", "30", "31", "id"]
-NR, NTB = 18, 11
-LN_X = 6 * 192
-LN_W = LN_X + 64 * len(EXTRA)
-LN_END = LN_W + 256 + 256 + 128
+N, V, HF, Q, L = 4, 4096, 2048, 1024, 128
+CUT = 66
+SEEDS = [[0], [0], [0], [0]]
+SENDS = (1, "h0", 3, 2, "h1")
+LOADS = ("mp1", "mp3", "mp2", "fs2", "mp0", "fs1", "fs3")
+ONE, SHARE, TWICE = False, 1, (0,)
+LATER = "id k7 k9 k0 oh"
+ORDER = {"dve": "N0 N4 N8 N12 S2a S3a S4a h00a h01b h01a h02a ne10 ne20 h02b h10b h10a h12a h12b h11a h11b ne11 ab110 ne21 ab111 h20b h22a h21a ne12 ne22 h21b ab210 h22b S9a S8a",
+         "act": "S1a S1b S2b wc1 S3b S4b h00b ab000 ab001 ab011 e01 e00 ab010 ab020 e02 ab021 S5a S5b ab100 ab101 ab120 ab121 S6a e10 S6b e11 e12 h20a "
+                "S7b pk3 ab200 S7a ab201 e20 e21 e22 S8b ab220 S9b ab211 ab221",
+         "pe": "cvg5 cv1 cv2 cv3 cv4 df000 df001 df011 df010 df020 df021 sc0 df100 cvr2 df101 cvr1 df120 df121 cvx df110 df111 cvy sc1 cvz "
+               "df200 df201 df210 cv7 df220 df211 df221 cv9 sc2 cv8"}
+RAW, LONG, ABS, SHORT, PASSES = -0.9, 0.4, 1.0, 2.0, 1
+DIRECT, HOLD, CUT2 = 3, 7, 86
+EARLY = {1: 2, 3: 2, 2: 2}
+LEFT = ((0, 2), (0, 1), (1, 0))
+STAGE = ({"10": 1, "12": 3, "13": 5, "21": 2, "20": 4, "23": 6}, {"01": 1, "03": 3, "02": 5, "30": 2, "31": 4, "32": 6})
+HOME = ((0, 0, 1), (1, 1, 0), (1, 1, 1), (0, 0, 0))
+T1, T2, T3, TZ, T4, TW, O2, O1, O3, LT_END = [L * x for x in (0, 3, 6, 9, 13, 16, 17, 21, 22, 23)]
 
 SCRATCH = {
     "M": ("sbuf", [128, 4, 256], "int32"),
+    "MA": ("sbuf", [128, 256], "int32"),
+    "DS": ("sbuf", [128, 512], "bfloat16"),
     "M16": ("sbuf", [128, 1024], "float16"),
     "Z16": ("sbuf", [128, 1024], "float16"),
-    "T1": ("sbuf", [128, 1024], "float16"),
-    "HI": ("sbuf", [128, 1024], "bfloat16"),
-    "LO": ("sbuf", [128, 1024], "bfloat16"),
-    "Z2": ("sbuf", [128, 4 * 512], "bfloat16"),
-    "MW": ("sbuf", [128, 5 * V], "bfloat16"),
-    "FW1": ("sbuf", [128, V], "bfloat16"),
-    "FW2": ("sbuf", [128, V], "bfloat16"),
-    "FW3": ("sbuf", [128, V], "bfloat16"),
-    "FR": ("sbuf", [128, 3 * Q], "bfloat16"),
+    "TA": ("sbuf", [128, 1024], "float16"),
+    "TB": ("sbuf", [128, 1024], "float16"),
+    "DG": ("sbuf", [128, 8 * 256], "bfloat16"),
+    "WD": ("sbuf", [128, 32], "float16"),
+    "ST": ("sbuf", [128, V + L], "bfloat16"),
+    "MW": ("sbuf", [128, 2 * V], "bfloat16"),
+    "FW": ("sbuf", [128, 2 * V], "bfloat16"),
+    "FR": ("sbuf", [128, 3 * HF], "bfloat16"),
     "FS": ("sbuf", [128, 3 * Q], "bfloat16"),
     "FD": ("dram", [4, 128, Q], "bfloat16"),
-    "H": ("sbuf", [128, 18 * Q], "bfloat16"),
-    "R": ("sbuf", [128, NR * Q], "bfloat16"),
+    "FE": ("dram", [2, 128, Q // 2], "bfloat16"),
+    "H": ("sbuf", [128, 9 * HF], "bfloat16"),
+    "R": ("sbuf", [128, 10 * HF], "bfloat16"),
     "JK": ("sbuf", [128, 2 * Q], "bfloat16"),
-    "JS": ("sbuf", [128, 18 * 64], "float32"),
-    "LN": ("sbuf", [128, LN_END], "float32"),
-    "U": ("sbuf", [128, LN_W], "uint16"),
-    "US": ("sbuf", [128, 64 * 16], "uint16"),
-    "TB": ("sbuf", [128, NTB * 192], "float32"),
-    "NE": ("sbuf", [128, 6 * 256], "bfloat16"),
-    "AC": ("sbuf", [128, 24], "float32"),
-    "EC": ("sbuf", [128, 24], "float32"),
-    "FL": ("sbuf", [128, 28], "float32"),
+    "JS": ("sbuf", [128, 9 * L], "float32"),
+    "LT": ("sbuf", [128, LT_END], "float32"),
+    "U": ("sbuf", [128, 22 * L], "uint16"),
+    "NE": ("sbuf", [128, 9 * L], "bfloat16"),
+    "AC": ("sbuf", [128, 36], "float32"),
+    "FL": ("sbuf", [128, 32], "float32"),
     "WC": ("sbuf", [128, 12], "float32"),
-    "OF": ("sbuf", [128, 6 * 16], "uint16"),
-    "OUT": ("sbuf", [128, 12 * 64], "float32"),
-    "YL": ("sbuf", [128, 12 * 64], "float32"),
-    "IOT": ("sbuf", [128, 192], "float32"),
-    "IOT2": ("sbuf", [128, 128], "float32"),
-    "IOT3": ("sbuf", [128, 16], "float32"),
+    "OF": ("sbuf", [128, 80], "uint16"),
+    "MK": ("sbuf", [128, 96], "float32"),
+    "YL": ("sbuf", [128, 12 * L], "float32"),
+    "YU": ("sbuf", [128, 4 * L], "uint16"),
+    "IOT": ("sbuf", [128, 160], "float32"),
     "KI": ("sbuf", [128, 2], "int32"),
-    "CI": ("sbuf", [128, 10], "int32"),
-    "CF": ("sbuf", [128, 10], "float32"),
-    "CD": ("sbuf", [128, 16], "float32"),
-    "WB": ("sbuf", [128, 12], "float32"),
-    "MB": ("sbuf", [128, 4], "float32"),
-    "MK": ("sbuf", [128, 8], "float32"),
-    "PC": ("sbuf", [128, 16], "float32"),
-    "EW": ("sbuf", [128, 128], "bfloat16"),
-    "BW": ("sbuf", [128, 1040], "bfloat16"),
-    "BC": ("sbuf", [128, 4 * 144], "bfloat16"),
-    "BO": ("sbuf", [128, 2 * 192], "bfloat16"),
-    "BL": ("sbuf", [128, 4 * 176], "float16"),
-    "OH": ("sbuf", [128, 3 * 128], "float16"),
+    "CI": ("sbuf", [128, 9], "int32"),
+    "CF": ("sbuf", [128, 9], "float32"),
+    "MB": ("sbuf", [128, 12], "float32"),
+    "CD": ("sbuf", [128, 48], "float32"),
+    "PC": ("sbuf", [128, 32], "float32"),
+    "BC": ("sbuf", [128, 13 * 144], "bfloat16"),
+    "BP": ("sbuf", [128, 11 * 160], "bfloat16"),
+    "OH": ("sbuf", [128, 192], "float16"),
     "ID": ("sbuf", [128, 4 * 128], "bfloat16"),
-    "PM": ("sbuf", [128, 128], "float32"),
-    "ONE": ("sbuf", [128, 128], "float32"),
+    "SW": ("sbuf", [128, 320], "float32"),
     "E0": ("psum", [128, 1024], "float32"),
     "E1": ("psum", [128, 1024], "float32"),
-    "P4": ("psum", [128, 512], "float32"),
-    "P5": ("psum", [128, 512], "float32"),
-    "P6": ("psum", [128, 512], "float32"),
-    "P7": ("psum", [128, 512], "float32"),
+    "E2": ("psum", [128, 1024], "float32"),
+    "E3": ("psum", [128, 1024], "float32"),
 }
 SEMAPHORES = (["pe", "dve", "act", "pool", "lsem", "hs0", "hs1"] + ["ma%d" % a for a in range(4)] + ["fa%d" % a for a in range(4)]
-              + ["oa%d" % k for k in range(12)] + ["d%d" % k for k in range(48)])
+              + ["oa%d" % k for k in range(12)] + ["d%d" % k for k in range(72)])
 
-CY, PCY, GA, LAT = 0.92e-3, 0.48e-3, 1.5, 0.12
-ARR_MAP = {1: 9.5, 3: 11.0, 2: 12.5}
-ARR_FT = {1: 14.5, 3: 16.5, 2: 20.0}
-ISSUE, DLAT, DRATE = 0.08, 2.0, 250e3
+CY, PCY, GA, LAT = 1.0e-3, 0.5e-3, 1.5, 0.1
+ARR_MAP = {1: 7.9, 3: 8.6, 2: 9.9}
+ARR_FT = {1: 16.5, 3: 16.5, 2: 19.0}
+ISSUE, DLAT, DRATE, DROW = 0.1, 1.8, 600e3, 0.012 / 16
+WIDE = 2
 
 
 def helpers(topo, core):
     near = [c for c in topo.cores_of(core) if c != core and topo.die(c) == topo.die(core)]
     far = [c for c in topo.cores_of(core) if topo.die(c) != topo.die(core)]
-    return near[0], far[0], far[1]
+    return near[0], far[0], far[1], near[1]
 
 
 def bits(es):
     return sum(1 << e for e in es)
 
 
-def plan(ops, seed):
+def backwards(order):
+    need, free = {}, {}
+    for o in sorted(order, key=lambda x: -x["end"]):
+        e = o["eng"]
+        after = need.get(o["n"], 0.0) + o["tail"] + o["move"]
+        need[o["n"]] = max(max(after, free.get(e, 0.0) if e in ("dve", "act", "pe") else 0.0) + o["dur"][e], o["boost"])
+        if not o["boost"]:
+            free[e] = need[o["n"]]
+        for d in o["deps"] + o["ord"]:
+            need[d["n"]] = max(need.get(d["n"], 0.0), need[o["n"]] + LAT)
+    return need
+
+
+def arrange(make, seed):
+    best, late = None, None
+    for _ in range(PASSES):
+        order = plan(make(), seed, late)
+        end = max(o["end"] for o in order)
+        if best is None or end < best[0]:
+            best = (end, order)
+        late = backwards(order)
+    return best[1]
+
+
+def plan(ops, seed, late=None):
     rng = np.random.RandomState(seed[0])
-    slack, pen = float(rng.uniform(0.0, 0.3)), float(rng.uniform(0.0, 1.5))
+    beta, pen = float(rng.uniform(2.0, 8.0)), float(rng.uniform(0.0, 0.3))
     dp, de = np.zeros(len(ops)), np.zeros(len(ops))
     for s in seed[1:]:
         rng = np.random.RandomState(s)
@@ -106,10 +128,15 @@ def plan(ops, seed):
         o["open"] = len(o["deps"] + o["ord"])
         for d in o["deps"] + o["ord"]:
             succ[d["n"]].append(o)
-    for o in reversed(ops):
-        o["path"] = min(o["dur"].values()) + o["tail"] + LAT + max([s["path"] for s in succ[o["n"]]] + [o.get("boost", 0.0)])
-        o["prio"] = o["path"] + float(dp[o["n"]])
-        o["pen"] = max(-0.9, (-0.5 if "twice" in o else pen) + float(de[o["n"]]))
+    line, wait = [o for o in ops if o["open"] == 0], {o["n"]: o["open"] for o in ops}
+    for o in line:
+        for s in succ[o["n"]]:
+            wait[s["n"]] -= 1
+            line += [s] if wait[s["n"]] == 0 else []
+    for o in reversed(line):
+        o["path"] = min(o["dur"].values()) + o["tail"] + o["move"] + LAT + max([s["path"] for s in succ[o["n"]]] + [o["boost"]])
+        o["prio"] = (o["path"] if late is None else late[o["n"]]) + float(dp[o["n"]])
+        o["pen"] = max(-0.9, (RAW if "twice" in o else LONG if o["name"][0] == "S" else ABS if o["name"][:2] == "ab" else SHORT + pen) + float(de[o["n"]]))
     free = {}
     holder = [None] * 8
     left = [o for o in ops if o["open"] == 0]
@@ -131,7 +158,7 @@ def plan(ops, seed):
             rdy = o["rdy"]
             bk = None
             if o["psum"]:
-                sets = [(0, 1), (2, 3)] if o["psum"] == 2 else ([(4,), (5,), (6,), (7,)] if o["psum"] == 1 else [(b,) for b in (4, 5, 6, 0, 1, 2, 3)])
+                sets = [(b, b + 1) for b in range(0, 2 * WIDE, 2)] if o["psum"] == 2 else [(b,) for b in range(2 * WIDE, 8)]
                 best = None
                 for s in sets:
                     ts = [bank_at(b) for b in s]
@@ -143,14 +170,26 @@ def plan(ops, seed):
                 if best is None:
                     continue
                 rdy, bk = best
-            e = min(o["dur"], key=lambda x: max(rdy, free.get(x, 0.0)) + o["dur"][x] * (1.0 + (o["pen"] if x == "dve" else 0.0)))
-            cand.append((max(rdy, free.get(e, 0.0)), o, e, bk))
-        t0 = min(c[0] for c in cand)
-        st, o, e, bk = max([c for c in cand if c[0] <= t0 + slack], key=lambda c: c[1]["prio"])
+            last = o["uses"].get("read") if "uses" in o else None
+            at = {x: max(rdy, free.get(x, 0.0), last["end"] + LAT if last is not None and last["eng"] != x else 0.0) for x in o["dur"]}
+            e = min(o["dur"], key=lambda x: at[x] + o["dur"][x] * (1.0 + (o["pen"] if x == "dve" else 0.0)))
+            cand.append((at[e], o, e, bk))
+        t0, e0 = min((c[0], c[2]) for c in cand)
+        mine = [c for c in cand if c[2] == e0]
+        top = max(mine, key=lambda c: c[1]["prio"] - beta * (c[0] - t0))
+        fit = [c for c in mine if c[0] + c[1]["dur"][e0] <= top[0] + 0.02]
+        st, o, e, bk = max(fit, key=lambda c: c[1]["prio"]) if fit else top
         o["eng"], o["start"] = e, st
+        if "uses" in o:
+            o["deps"] = o["deps"] + [c for c in o["uses"]["cons"] if c.get("eng", e) != e]
+            o["uses"]["read"] = o
         if e != "arr":
             free[e] = st + o["dur"][e]
         o["end"] = st + o["dur"][e] + o["tail"]
+        if o["move"]:
+            free["dma"] = max(max(free.get("dma", 0.0), st + DLAT - 0.5) + o["move"], st + o["dur"][e] + DLAT - 0.5)
+            if o["sem"]:
+                o["end"] = free["dma"] + 0.5
         if bk:
             o["bank"] = bk
             for b in bk:
@@ -158,7 +197,8 @@ def plan(ops, seed):
                     o["deps"] = o["deps"] + holder[b]["cons"]
                 holder[b] = o
         if e == "act" and "twice" in o:
-            o["twice"]["dur"] = {"pe": 2 * o["twice"]["dur"]["pe"]}
+            for x in o["twice"]:
+                x["dur"] = {"pe": 2 * x["base"]}
         left = [x for x in left if x is not o]
         for s in succ[o["n"]]:
             s["open"] -= 1
@@ -172,532 +212,584 @@ def build(t, T, topo, core):
     ops = []
     nd = [0]
 
-    def op(name, dur, deps, fn, psum=0, tail=0.0, at=0.0, after=(), sem=None, uses=None):
+    def op(name, dur, deps, fn, psum=0, tail=0.0, at=0.0, after=(), sem=None, uses=None, move=0.0, boost=0.0):
         o = {"n": len(ops), "name": name, "dur": dur, "deps": [d for d in deps if d is not None], "ord": list(after), "fn": fn,
-             "psum": psum, "tail": tail, "at": at, "sem": sem, "cons": []}
+             "psum": psum, "tail": tail, "at": at, "sem": sem, "cons": [], "move": move, "boost": boost}
         if uses is not None:
-            uses["cons"].append(o)
             o["deps"].append(uses)
+            o["uses"] = uses
+            uses["cons"].append(o)
         ops.append(o)
         return o
 
-    def ps(o):
-        b = o["bank"]
-        if len(b) == 2:
-            return T["E%d" % (b[0] // 2)], 0
-        return (T["E%d" % (b[0] // 2)], 512 * (b[0] % 2)) if b[0] < 4 else (T["P%d" % b[0]], 0)
-
-    def pv(o, a, b):
-        buf, c = ps(o)
-        return buf[:, c + a:c + b]
+    def pv(o, a, b, p=slice(0, 128)):
+        k = o["bank"]
+        c = 512 * (k[0] % 2)
+        return T["E%d" % (k[0] // 2)][p, c + a:c + b]
 
     def dve(name, n, deps, f, **k):
-        return op(name, {"dve": (max(n, 64) + 50) * CY}, deps, lambda q, e, o: [f(q)], **k)
+        return op(name, {"dve": (max(n, 64) + 35) * CY}, deps, lambda q, e, o: [f(q)], **k)
 
     def ts(name, out, in0, s1, s2, o0, o1, deps, n=64, **k):
         if o1 is None:
             return dve(name, n, deps, lambda q: q.tensor_scalar(out, in0, s1, None, o0), **k)
         return dve(name, n, deps, lambda q: q.tensor_scalar(out, in0, s1, s2, o0, o1), **k)
 
-    def addc(name, out, src, c, deps, n=64, **k):
+    def addc(name, out, src, c, deps, n=L, **k):
         def f(q, e, o):
-            s = src() if not isinstance(src, tuple) else src[0]
-            if isinstance(c, tuple):
-                return [q.tensor_scalar(out, s, c[0], None, A.add) if e == "dve" else q.activation(out, s, AF.Identity, bias=c[0])]
-            if e == "dve":
-                return [q.tensor_scalar(out, s, float(c), None, A.add)]
-            return [q.activation(out, s, AF.Copy, bias=float(c))]
-        return op(name, {"dve": (n + 50) * CY, "act": (n + 110) * CY}, deps, f, **k)
+            return [q.tensor_scalar(out, src(), float(c), None, A.add) if e == "dve" else q.activation(out, src(), AF.Copy, bias=float(c))]
+        return op(name, {"dve": (n + 35) * CY, "act": (n + 80) * CY}, deps, f, **k)
 
-    def dma(name, pairs, nbytes, deps, queues=("sp",), **k):
+    def dma(name, pairs, nbytes, rows, deps, queues=("sp",), **k):
         s = "d%d" % nd[0]
         nd[0] += 1
         return op(name, {x: ISSUE * len(pairs) for x in queues}, deps, lambda q, e, o: [q.dma_start(a, b) for a, b in pairs],
-                  tail=DLAT + nbytes / DRATE, sem=s, **k)
+                  tail=DLAT, move=nbytes / DRATE + rows * DROW, sem=s, **k)
 
     def pe(name, cyc, deps, f, psum):
-        return op(name, {"pe": cyc * PCY + 0.05}, deps, f, psum=psum, tail=0.1)
+        return op(name, {"pe": cyc * PCY + 0.02}, deps, f, psum=psum, tail=0.05)
 
     def arrive(name, sem, val, at, deps=()):
         o = op(name, {"arr": 0.0}, list(deps), None, at=at)
         o["tok"] = (sem, val)
         return o
 
-    def remote(name, f, n, deps, after=(), boost=6.0):
-        o = op(name, {"g": 0.8}, deps, lambda q, e, o: f(q), after=after)
-        o["lsem"], o["boost"] = n, boost
+    def remote(name, f, n, deps, after=(), boost=6.0, move=0.0):
+        o = op(name, {"g": 0.6}, deps, lambda q, e, o: f(q), after=after, boost=boost, move=move)
+        o["lsem"] = n
         return o
 
     cores = T.cores
-    a0 = t
-    pad = dve("pad", 16, [], lambda q: q.memset(T.M[32 * a0:32 * a0 + 32, :, 0:4], 2048))
-    ml = {}
-    for tt in (t ^ 1, t ^ 3, t ^ 2, t):
-        prs = [(T.M[32 * b:32 * b + 32, tt, :], T.mp[32 * tt:32 * tt + 32, 256 * ((a0 ^ b) - 1):256 * (a0 ^ b)]) for b in range(4) if b != a0]
-        ml[tt] = dma("mp%d" % tt, prs, 200e3, [], queues=("sp", "act"))
-    lam = dma("lam", [(T.M[32 * a0:32 * a0 + 1, :, 0:3], T.lam[:])], 0, [pad], queues=("sp", "act"))
-    fs = {}
-    for k, d in enumerate((1, 3, 2)):
+    both = ("sp", "act")
+    pad = dve("pad", 16, [], lambda q: q.memset(T.M[32 * t:32 * t + 32, :, 0:4], 0), boost=400.0)
+    ml, fs, ld = {}, {}, []
+    lam = dve("pad2", 1008, [], lambda q: q.memset(T.M[32 * t:32 * t + 32, :, 4:256], 0), boost=370.0, after=[pad])
+    lam = [lam, dma("lam2", [(T.M[32 * t:32 * t + 1, :, 0:3], T.lam[:])], 0, 4, [pad], queues=("act",), boost=400.0)]
+    for x in LOADS:
+        d = int(x[2])
         tt = t ^ d
-        fs[d] = dma("fs%d" % d, [(T.FS[:, Q * k:Q * k + Q], T.ft[32 * tt:32 * tt + 32, :])], 262e3 * (k + 1) + 300e3, [], queues=("sp", "act"))
+        if x[0] == "m":
+            prs = [(T.M[32 * b:32 * b + 32, tt, :], T.mp[32 * tt:32 * tt + 32, 256 * ((t ^ b) - 1):256 * (t ^ b)]) for b in range(4) if b != t]
+            ml[tt] = dma(x, prs, 98e3, 96, [], boost=400.0, after=ld[-1:])
+            ld.append(ml[tt])
+        else:
+            k = (1, 3, 2).index(d)
+            n = 2 if d == 2 and DIRECT == 3 else 1
+            fs[d] = dma(x, [(T.FS[:, Q * k + Q // n * y:Q * k + Q // n * (y + 1)], T.ft[32 * tt:32 * tt + 32, V // n * y:V // n * (y + 1)]) for y in range(n)],
+                        262e3, 128 * n, [], boost=400.0, after=ld[-1:])
+            ld.append(fs[d])
     gq = []
 
     def gop(name, n, f):
         o = op(name, {"g": 0.13 + 2 * n * CY}, [], lambda q, e, o: [f(q)], after=gq[-1:])
         gq.append(o)
         return o
-    ki = gop("ki", 2, lambda q: q.iota(T.KI[:], [[48, 2]], 0, 1))
-    iot = gop("iot", 192, lambda q: q.iota(T.IOT[:], [[1, 192]], 0, 0, allow_small_or_imprecise_dtypes=True))
-    iot2 = gop("iot2", 128, lambda q: q.iota(T.IOT2[:], [[64, 2], [0, 4], [1, 16]], 0, 0, allow_small_or_imprecise_dtypes=True))
-    iot3 = gop("iot3", 16, lambda q: q.iota(T.IOT3[:], [[192, 4], [16, 4]], 0, 0, allow_small_or_imprecise_dtypes=True))
-    pad2 = gop("pad2", 1008, lambda q: q.iota(T.M[32 * a0:32 * a0 + 32, :, 4:256], [[0, 1008]], 2048, 0))
-    pad2["deps"].append(iot3)
+    ki = gop("ki", 1, lambda q: q.iota(T.KI[:], [[0, 2]], 0, 1))
+    iot = gop("iot", 160, lambda q: q.iota(T.IOT[:], [[1, 160]], 0, 0, allow_small_or_imprecise_dtypes=True))
     k0 = T.KI[:, 0:1]
-    ci = [ts("c0", T.CI[:, 0:1], k0, 15, None, A.bitwise_and, None, [ki]),
-          ts("c1", T.CI[:, 1:2], k0, 112, None, A.bitwise_and, None, [ki]),
-          ts("c2", T.CI[:, 2:3], k0, 64, None, A.bitwise_and, None, [ki]),
-          ts("c3", T.CI[:, 3:4], k0, 4, 3, A.arith_shift_right, A.bitwise_and, [ki]),
-          ts("c4", T.CI[:, 4:5], k0, 4, 1, A.arith_shift_right, A.bitwise_and, [ki]),
-          ts("c5", T.CI[:, 5:6], k0, 5, None, A.arith_shift_right, None, [ki]),
-          ts("c6", T.CI[:, 6:7], T.KI[:, 1:2], 63, None, A.bitwise_and, None, [ki]),
-          ts("c7", T.CI[:, 7:8], k0, 127, None, A.bitwise_and, None, [ki]),
-          ts("c8", T.CI[:, 8:9], k0, 3, 1, A.arith_shift_right, A.bitwise_and, [ki]),
-          ts("c9", T.CI[:, 9:10], k0, 7, None, A.bitwise_and, None, [ki])]
-    cf = dve("cf", 10, ci, lambda q: q.tensor_copy(T.CF[:], T.CI[:]))
+    ci = [ts("c%d" % n, T.CI[:, n:n + 1], k0, m, None, A.bitwise_and, None, [ki]) for n, m in enumerate((127, 15, 112, 64, 32, 7, 8, 31, 96))]
+    cf = dve("cf", 8, ci, lambda q: q.tensor_copy(T.CF[:], T.CI[:]), boost=320.0)
+    P, I16, G16, S64, H32, SL, D8, P32, B96 = [T.CF[:, j:j + 1] for j in range(9)]
+    nc = [0]
 
-    def C(j):
-        return T.CF[:, j:j + 1]
+    def newcol():
+        nc[0] += 1
+        return T.CD[:, nc[0] - 1:nc[0]]
 
-    def D(j):
-        return T.CD[:, j:j + 1]
-    d0 = ts("d0", D(0), C(1), 15.0, None, A.add, None, [cf])
-    d1 = ts("d1", D(1), C(2), C(3), 60.0, A.add, A.add, [cf])
-    d2a = ts("d2a", D(8), C(0), 4.0, C(2), A.mult, A.add, [cf])
-    d2 = ts("d2", D(2), D(8), C(3), None, A.add, None, [d2a])
-    d3a = ts("d3a", D(9), C(4), 64.0, C(0), A.mult, A.add, [cf])
-    d3 = ts("d3", D(3), D(9), 48.0, None, A.add, None, [d3a])
-    d4a = ts("d4a", D(10), C(2), 1.0 / 16, C(3), A.mult, A.add, [cf])
-    d4 = ts("d4", D(4), C(8), 64.0, D(10), A.mult, A.add, [d4a])
-    d5 = ts("d5", D(5), C(2), C(6), None, A.add, None, [cf])
-    d6 = ts("d6", D(6), C(3), 1024.0, C(0), A.mult, A.add, [cf])
-    dm = ts("dm", T.CD[:, 12:15], T.IOT[:, 0:96:32], C(7), None, A.is_equal, None, [cf, iot])
-    wa = ts("wa", T.WB[:, 4:8], T.IOT[:, 0:4], C(0), 32.0, A.is_equal, A.mult, [cf, iot])
-    wb_ = ts("wb", T.WB[:, 8:12], T.IOT[:, 4:8], C(0), None, A.is_equal, None, [cf, iot])
-    wc = dve("wc", 8, [wa, wb_], lambda q: q.tensor_tensor(T.WB[:, 0:4], T.WB[:, 4:8], T.WB[:, 8:12], A.add))
-    mb = ts("mb", T.MB[:], T.IOT[:, 0:4], C(5), None, A.is_equal, None, [cf, iot])
-    mk = ts("mk", T.MK[:], T.IOT[:, 0:8], C(9), None, A.is_equal, None, [cf, iot])
-    pc = ts("pc", T.PC[:], T.IOT3[:], C(0), None, A.add, None, [cf, iot3])
-    ew = ts("ew", T.EW[:], T.IOT2[:], D(4), None, A.is_equal, None, [d4, iot2], n=128)
-    bw0 = dve("bw", 8, [], lambda q: q.memset(T.BW[:, 0:16], 0.0))
-    bw = []
-    for i in range(8):
-        def f(q, e, o, i=i):
-            out = T.BW[:, 16 + 128 * i:144 + 128 * i]
-            if e == "dve":
-                return [q.tensor_scalar(out, T.EW[:], T.MK[:, i:i + 1], None, A.mult)]
-            return [q.activation(out, T.EW[:], AF.Identity, scale=T.MK[:, i:i + 1])]
-        bw.append(op("bw%d" % i, {"dve": 114 * CY, "act": 240 * CY}, [ew, mk], f))
-    bc = [ts("bc%d" % b, T.BC[:, 144 * b:144 * b + 144], T.IOT[:, 0:144], D(0), T.WB[:, b:b + 1], A.is_equal, A.mult, [d0, wc], n=144) for b in range(4)]
-    bo = [ts("bo%d" % b, T.BO[:, 192 * b:192 * b + 192], T.IOT[:], D(1), T.WB[:, b:b + 1], A.is_equal, A.mult, [d1, wc], n=192) for b in range(2)]
-    bl = [ts("bl%d" % b, T.BL[:, 176 * b:176 * b + 176], T.IOT[:, 0:176], D(3), T.MB[:, b:b + 1], A.is_equal, A.mult, [d3, mb], n=176) for b in range(4)]
-    oh = [ts("oh%d" % b, T.OH[:, 128 * b:128 * b + 128], T.IOT[:, 0:128], 0.0, D(12 + b), A.mult, A.add, [dm], n=128) for b in range(3)]
-    idm = [ts("id0", T.ID[:, 0:128], T.IOT[:, 0:128], C(7), None, A.is_equal, None, [cf, iot], n=128),
-           ts("id1", T.ID[:, 128:256], T.IOT[:, 0:128], C(7), -1.0, A.is_equal, A.mult, [cf, iot], n=128),
-           ts("id2", T.ID[:, 256:384], T.IOT[:, 0:128], D(5), -1.0, A.is_equal, A.mult, [d5, iot], n=128),
-           ts("id3", T.ID[:, 384:512], T.IOT[:, 0:128], D(5), None, A.is_equal, None, [d5, iot], n=128)]
-    pm = ts("pm", T.PM[:], T.IOT[:, 0:128], D(2), None, A.is_equal, None, [d2, iot], n=128)
-    one = dve("one", 128, [], lambda q: q.memset(T.ONE[:], 1.0))
-    ac0 = dve("ac0", 24, [], lambda q: q.memset(T.AC[:], 0.0))
-    ec0 = dve("ec0", 24, [], lambda q: q.memset(T.EC[:], 0.0))
-    cast = {tt: ts("cast%d" % tt, T.M16[:, 256 * tt:256 * tt + 256], T.M[:, tt, :], -2048.0, None, A.add, None, [ml[tt], lam, pad, pad2], n=256)
-            for tt in (t ^ 1, t ^ 3, t ^ 2, t)}
-    near, far, far2 = helpers(topo, core)
+    def col(name, in0, s1, s2, o0, o1, deps):
+        c = newcol()
+        if o0 == A.is_equal:
+            return c, ts(name, c, in0, s1, s2, o0, o1, deps)
+        return c, lin(name, c, in0, *((s1, 0.0 if s2 is None else s2) if o0 == A.mult else (1.0, s1)), deps)
+
+    def lin(name, out, in0, a, b, deps):
+        return op(name, {"act": 140 * CY}, deps, lambda q, e, o: [q.activation(out, in0, AF.Copy if isinstance(b, float) else AF.Identity, bias=b, scale=a)])
+
+    def scaled(name, out, in0, m, n, deps):
+        return op(name, {"dve": (max(n // 2, 64) + 35) * CY, "act": (n + 80) * CY}, deps,
+                  lambda q, e, o: [q.tensor_scalar(out, in0, m, None, A.mult) if e == "dve" else q.activation(out, in0, AF.Identity, scale=m)])
+    calm = [len(ops)]
+    sg, osg = col("sg", S64, -2.0, 79.0, A.mult, A.add, [cf])
+    at = {"s": col("bs", G16, 15.0, None, A.add, None, [cf]), "x": col("bx", G16, sg, None, A.add, None, [osg])}
+    WT, owt = col("wt", D8, 15.0 / 8, 1.0, A.mult, A.add, [cf])
+    sl, part = {0: col("sl0", SL, 128.0, None, A.mult, None, [cf])}, {}
+    for n, a, b, x, y in (("d", 128.0, -768.0, 5.0, 384.0), ("n", -128.0, 128.0, 7.0, 1024.0)):
+        part[n] = col("sa" + n, SL, x, y, A.is_equal, A.mult, [cf]), col("sc" + n, SL, a, b, A.mult, A.add, [cf])
+    for n in "dn":
+        sl[n] = col("sl" + n, part[n][1][0], part[n][0][0], None, A.add, None, [part[n][0][1], part[n][1][1]])
+    trio = T.CD[:, nc[0] - 1:nc[0] + 2]
+    for n, b in (("f", -128.0), ("g", -192.0)):
+        sl[n] = col("sl" + n, SL, 64.0, b, A.mult, A.add, [cf])
+    b93, ob93 = newcol(), None
+    ob93 = op("b93", {"act": 140 * CY}, [cf], lambda q, e, o: [q.activation(b93, B96, AF.Abs, bias=-48.0)])
+    b94, ob94 = col("b94", b93, 2.0, P32, A.mult, A.add, [ob93])
+    b96, ob96 = b94, ob94
+    hx, ohx = col("hx", H32, -2.0, 32.0, A.mult, A.add, [cf])
+    px, opx = col("px", P, hx, None, A.add, None, [ohx])
+    sh, osh = col("sh", H32, -4.0, 128.0, A.mult, A.add, [cf])
+    sb, osb = col("sb", S64, 6.0, None, A.mult, None, [cf])
+    sa, osa = col("sa", S64, -6.0, 384.0, A.mult, A.add, [cf])
+
+    def mask(name, out, slot, deps):
+        if isinstance(slot, tuple):
+            return ts(name, out, slot[0], slot[1], WT, A.is_equal, A.mult, deps + [owt])
+        return ts(name, out, SL, float(slot), WT, A.is_equal, A.mult, deps + [owt])
+
+    def sided(name, out, a, b):
+        c, o = col(name + "c", S64, 2.0 * (b - a), 128.0 * a, A.mult, A.add, [cf])
+        return mask(name, out, (sl[0][0], c), [o, sl[0][1]])
+    bc = {way: (n, ts("bc" + way, T.BC[:, 144 * n:144 * n + 144], T.IOT[:, 0:144], at[way][0], None, A.is_equal, None, [at[way][1], iot], n=144)) for n, way in enumerate("sx")}
+
+    def matrix(name, way, m, deps):
+        n, w = len(bc), bc[way][0]
+        bc[name] = (n, scaled("bc" + name, T.BC[:, 144 * n:144 * n + 144], T.BC[:, 144 * w:144 * w + 144], m, 144, deps + [bc[way][1]]))
+    for slot, ways in ((3, "s"), (5, "x"), (2, "sx"), (4, "x")):
+        c = newcol()
+        o = mask("m%d" % slot, c, slot, [cf])
+        for way in ways:
+            matrix("%d%s" % (slot, way), way, c, [o])
+    bp, bp0 = {}, ts("bp", T.BP[:, 0:160], T.IOT[:], b96, None, A.is_equal, None, [ob96, iot], n=160)
+    for n, w in enumerate((256, 1, 16)):
+        o = ts("mb%d" % w, T.MB[:, 4 * n:4 * n + 4], T.IOT[:, 0:128:32], B96, float(w), A.is_equal, A.mult, [cf, iot])
+        for b in range(2 if w == 256 else 4):
+            c = 160 * (len(bp) + 1)
+            bp[(b, w)] = (c, scaled("bp%d_%d" % (b, w), T.BP[:, c:c + 160], T.BP[:, 0:160], T.MB[:, 4 * n + b:4 * n + b + 1], 160, [bp0, o]))
+    o1 = dve("oh", 64, [], lambda q: q.memset(T.OH[0:1, :], 0.0))
+    oh = [dve("oh1", 32, [o1], lambda q: q.memset(T.OH[0:1, 64:128], -1.0))]
+    idm = [ts("id%d" % n, T.ID[:, 128 * n:128 * n + 128], T.IOT[:, 0:128], c, w, A.is_equal, A.mult, [cf, opx, iot], n=128)
+           for n, (c, w) in enumerate(((P, 1.0), (P, -1.0), (px, -1.0), (px, 1.0)))]
+
+    pc0 = lin("pc0", T.PC[:, 0:8], T.IOT[:, 0:8], 16.0, I16, [cf, iot])
+    pcb = lin("pcb", T.PC[:, 8:16], T.PC[:, 0:8], 1.0, sb, [pc0, osb])
+    pca = lin("pca", T.PC[:, 16:24], T.PC[:, 0:8], 1.0, sa, [pc0, osa])
+    pc3 = lin("pc3", T.PC[:, 24:32], T.PC[:, 0:8], 1.0, 384.0, [pc0])
+    mk = [sided("k70", T.MK[:, 2:3], 6, 4), mask("k72", T.MK[:, 4:5], 2, [cf]), sided("k90", T.MK[:, 5:6], 5, 7), mask("k92", T.MK[:, 7:8], 3, [cf]),
+          dve("k0", 2, [], lambda q: q.memset(T.MK[:, 1:2], 0.0))]
+    calm.append(len(ops))
+    nu = [0]
+
+    def ulist(n=1):
+        nu[0] += n
+        return L * (nu[0] - n)
+    edge = [dve("edge%d" % c, 64, [], lambda q, c=c: q.memset(T.ST[:, c:c + L], 0.0), boost=330.0) for c in (0, V)]
+    spare = [dma("zst", [(T.ST[r:128:8, L:V], T.FS[0:64, 2 * Q:2 * Q + 992]) for r in (0, 7)], 256e3, 128, [fs[2]], queues=("act",), boost=300.0),
+             dma("zmw", [(T.MW[r:128:8, V:2 * V], T.FS[0:64, 2 * Q:3 * Q]) for r in (1, 3)], 256e3, 128, [fs[2]], queues=("act",), boost=290.0)]
+    cast = {tt: ts("cast%d" % tt, T.M16[:, 256 * tt:256 * tt + 256], T.M[:, tt, :], -2048.0, None, A.add, None, [ml[tt], pad] + lam, n=256 , boost=300.0)
+            for tt in (t ^ 1, t ^ 3, t)}
+    dep, tt = [ml[t ^ 2], pad] + lam, t ^ 2
+    ma = ts("ma", T.MA[:], T.M[:, tt, :], 15, None, A.bitwise_and, None, dep, n=256, boost=290.0)
+    ta = ts("ta", T.TA[:, 256 * tt:256 * tt + 256], T.M[:, tt, :], 1.0 / 16, 1280.0 - 15.0 / 32, A.mult, A.add, dep, n=256, boost=290.0)
+    made = [dve("da", 256, [ma], lambda q: q.tensor_copy(T.DS[:, 0:256], T.MA[:]), boost=290.0),
+            ts("db", T.DS[:, 256:512], T.TA[:, 256 * tt:256 * tt + 256], -1280.0, None, A.add, None, [ta], n=128, boost=290.0)]
+    near, far, far2, near2 = helpers(topo, core)
     up = topo.engines(core, near)
-    up = up[len(up) // 2:]
-    h = len(up) // 2
+    up = up[len(up) - len(up) // SHARE:]
+    hh = len(up) // 2
 
     def dst(c):
         r, p, _ = topo.addr(c)
         return DstId(rid=r, pnc=p)
 
+    def f_h2(q):
+        r, p, _ = topo.addr(cores[t ^ 1])
+        q.remote_dma(T.FD[t], T.FS[:, 0:Q], T.sem["fa%d" % t], T.sem.lsem, p, r, topo.mask(core, cores[t ^ 1]))
+        return []
+
     def f_h0(q):
+        if DIRECT == 2:
+            r, p, _ = topo.addr(far)
+            q.remote_dma(T.FS[:, Q:2 * Q], T.FS[:, Q:2 * Q], T.sem.hs0, T.sem.lsem, p, r, bits(up[hh:]))
+            return []
         q.remote_dma_fused([
-            RemoteDMATransfer(dst_ids=[dst(near)], dma_engine_mask=bits(up[:h]), remote_sem=T.sem.hs0, src=T.FS[:, 0:Q], dst=T.FS[:, 0:Q]),
-            RemoteDMATransfer(dst_ids=[dst(far)], dma_engine_mask=bits(up[h:]), remote_sem=T.sem.hs0, src=T.FS[:, Q:2 * Q], dst=T.FS[:, Q:2 * Q])],
+            RemoteDMATransfer(dst_ids=[dst(near)], dma_engine_mask=bits(up[:hh]), remote_sem=T.sem.hs0, src=T.FS[:, 0:Q], dst=T.FS[:, 0:Q]),
+            RemoteDMATransfer(dst_ids=[dst(far)], dma_engine_mask=bits(up[hh:]), remote_sem=T.sem.hs0, src=T.FS[:, Q:2 * Q], dst=T.FS[:, Q:2 * Q])],
             local_sem=T.sem.lsem)
         return []
-    gq.append(remote("h0", f_h0, 2 * h, [fs[1], fs[3]], after=gq[-1:]))
-    for d in (1, 3, 2):
-        tt = t ^ d
 
-        def f(q, tt=tt):
-            r, p, _ = topo.addr(cores[tt])
-            q.remote_dma(T.Z16[:, 256 * a0:256 * a0 + 256], T.M16[:, 256 * tt:256 * tt + 256], T.sem["ma%d" % a0], T.sem.lsem, p, r, topo.mask(core, cores[tt]))
-            return []
-        o = remote("sm%d" % d, f, len(topo.engines(core, cores[tt])), [cast[tt]], after=gq[-1:], boost=300.0)
-        gq.append(o)
+    def f_sm(q, tt):
+        r, p, _ = topo.addr(cores[tt])
+        out, src = (T.DG[:, 512 * t:512 * t + 512], T.DS[:]) if tt == t ^ 2 else (T.Z16[:, 256 * t:256 * t + 256], T.M16[:, 256 * tt:256 * tt + 256])
+        q.remote_dma(out, src, T.sem["ma%d" % t], T.sem.lsem, p, r, topo.mask(core, cores[tt]))
+        return []
 
     def f_h1(q):
+        if DIRECT == 3:
+            q.remote_dma_fused([RemoteDMATransfer(dst_ids=[dst(c)], dma_engine_mask=bits(up[hh * y:hh * y + hh]), remote_sem=T.sem.hs1,
+                                                  src=T.FS[:, 2 * Q + 512 * y:2 * Q + 512 * y + 512], dst=T.FS[:, 2 * Q + 512 * y:2 * Q + 512 * y + 512])
+                                for y, c in enumerate((near2, far2))], local_sem=T.sem.lsem)
+            return []
+        if DIRECT:
+            r, p, _ = topo.addr(cores[t ^ 2])
+            q.remote_dma(T.FD[t], T.FS[:, 2 * Q:3 * Q], T.sem["fa%d" % t], T.sem.lsem, p, r, topo.mask(core, cores[t ^ 2]))
+            return []
         r, p, _ = topo.addr(far2)
         q.remote_dma(T.FS[:, 2 * Q:3 * Q], T.FS[:, 2 * Q:3 * Q], T.sem.hs1, T.sem.lsem, p, r, bits(up))
         return []
-    gq.append(remote("h1", f_h1, len(up), [fs[2]], after=gq[-1:], boost=300.0))
-    fw, fr = {}, {}
+    for x in SENDS:
+        if x == "h0":
+            gq.append(remote("h0", f_h0, hh if DIRECT == 2 else 2 * hh, [fs[1], fs[3]], after=gq[-1:], boost=300.0, move=1.2))
+        elif x == "h1":
+            gq.append(remote("h1", f_h1, len(topo.engines(core, cores[t ^ 2]) if DIRECT in (1, 2) else up), [fs[2]], after=gq[-1:], boost=300.0, move=0.6))
+        else:
+            gq.append(remote("sm%d" % x, lambda q, tt=t ^ x: f_sm(q, tt), len(topo.engines(core, cores[t ^ x])), made if x == 2 else [cast[t ^ x]], after=gq[-1:], boost=300.0, move=0.3))
+    small = {"allow_small_or_imprecise_dtypes": True}
+    ac0 = gop("ac0", 36, lambda q: q.iota(T.AC[:], [[0, 36]], 0, 0, **small))
+    sw = []
+    for n, (p, a, b, v) in enumerate(((0, 0, 128, 1), (0, 128, 256, 0), (0, 256, 320, 1), (64, 0, 128, 0), (64, 128, 256, 1), (64, 256, 320, 0))):
+        sw.append(gop("sw%d" % n, b - a, lambda q, p=p, a=a, b=b, v=v: q.iota(T.SW[p:p + 64, a:b], [[0, b - a]], v, 0, **small)))
+        sw[-1]["deps"] += [ac0] if n == 0 else sw[n - 1:n] if n == 3 else []
+    fa = {}
     for a in range(4):
         if a == t:
-            dep = [fs[2]]
-            rows = [T.ft[32 * t + 16 * l:32 * t + 16 * l + 16, :] for l in range(2)]
-            qr = [[T.ft[32 * t + 16 * l:32 * t + 16 * l + 16, Q * q:Q * q + Q] for q in range(4)] for l in range(2)]
+            fa[a] = fs[2]
         else:
             snd = helpers(topo, cores[a])[(1, 3, 2).index(a ^ t)]
-            dep = [arrive("fa%d" % a, "fa%d" % a, len(topo.engines(snd, core)), ARR_FT[a ^ t])]
-            rows = [T.FD[a, 64 * l:64 * l + 64, :] for l in range(2)]
-            qr = [[T.FD[a, 64 * l + q:64 * l + 64:4, :] for q in range(4)] for l in range(2)]
-        if a > 0:
-            fw[a] = dma("fw%d" % a, [(T["FW%d" % a][64 * l + 16 * q:64 * l + 16 * q + 16, :], rows[l]) for l in range(2) for q in range(4)], 1050e3, dep)
-        if a < 3:
-            fr[a] = dma("fr%d" % a, [(T.FR[64 * l + 16 * q:64 * l + 16 * q + 16, Q * a:Q * a + Q], qr[l][q]) for l in range(2) for q in range(4)], 262e3, dep)
-    za, zs = {}, {}
-    for a in range(4):
+            fa[a] = arrive("fa%d" % a, "fa%d" % a, len(topo.engines(snd, core)) * (2 if DIRECT == 3 and a ^ t == 2 else 1), ARR_FT[a ^ t])
+
+    def fwin(k, s, a, after):
+        src = T.ft[32 * t:32 * t + 32, :] if a == t else T.FD[a]
+        if DIRECT == 3 and a ^ t == 2:
+            return dma("fw%d%d" % (k, s), [(T.FW[64 * s + 32 * h:64 * s + 32 * h + 32, V * k + HF * y:V * k + HF * y + HF], T.FE[y]) for h in range(2) for y in range(2)],
+                       524e3, 128, [fa[a]], after=after)
+        return dma("fw%d%d" % (k, s), [(T.FW[64 * s + 32 * h:64 * s + 32 * h + 32, V * k:V * k + V], src) for h in range(2)], 524e3, 128, [fa[a]], after=after)
+
+    def fleft(k, s, a, after):
         if a == t:
-            za[a], zs[a] = cast[t], T.M16
+            prs = [(T.FR[64 * s + 32 * h:64 * s + 32 * h + 32, HF * k:HF * k + HF], T.ft[32 * t:32 * t + 32, HF * h:HF * h + HF]) for h in range(2)]
+        elif DIRECT == 3 and a ^ t == 2:
+            prs = [(T.FR[64 * s + 32 * h:64 * s + 32 * h + 32, HF * k:HF * k + HF], T.FE[h]) for h in range(2)]
         else:
-            za[a], zs[a] = arrive("ma%d" % a, "ma%d" % a, len(topo.engines(cores[a], core)), ARR_MAP[a ^ t]), T.Z16
-    win, zz = {}, {}
+            prs = [(T.FR[64 * s + 32 * (x // 2):64 * s + 32 * (x // 2) + 32, HF * k + Q * (x % 2):HF * k + Q * (x % 2) + Q], T.FD[a, x:128:4, :]) for x in range(4)]
+        return dma("fr%d%d" % (k, s), prs, 262e3, 128, [fa[a]], after=after)
+    za, stg, zl, wl, seq = {}, [], {}, {}, []
     for a in (t, t ^ 1, t ^ 3, t ^ 2):
-        s = slice(256 * a, 256 * a + 256)
-        hi = ts("hi%d" % a, T.HI[:, s], zs[a][:, s], 1.0 / 32, 192.0 - 31.0 / 64, A.mult, A.add, [za[a]], n=128)
-        t1 = ts("t1%d" % a, T.T1[:, s], T.HI[:, s], -32.0, 6144.0, A.mult, A.add, [hi], n=128)
-        lo = dve("lo%d" % a, 512, [t1], lambda q, s=s, a=a: q.tensor_tensor(T.LO[:, s], zs[a][:, s], T.T1[:, s], A.add))
-        z2 = dma("z%d" % a, [(T.Z2[0:64, 512 * a:512 * a + 512], T.HI[:, s]), (T.Z2[64:128, 512 * a:512 * a + 512], T.LO[:, s])], 130e3, [lo])
-        zz[a] = z2
-    for da, db in PASSES:
-        a, b = t ^ da, (None if db is None else t ^ db)
-        win[a] = []
-        for j in range(8):
-            def wp(q, e, o, j=j, a=a, b=b):
-                r = [q.matmul(pv(o, 0, 512), T.BW[:, 16 + 128 * j:144 + 128 * j], T.Z2[:, 512 * a:512 * a + 512], True, b is None)]
-                if b is not None:
-                    r.append(q.matmul(pv(o, 0, 512), T.BW[:, 8 + 128 * j:136 + 128 * j], T.Z2[:, 512 * b:512 * b + 512], False, True))
-                return r
-            p = pe("wp%d_%d" % (a, j), 512 if b is None else 1024, [zz[a], zz.get(b), bw0, bw[j]] + bw[max(j - 1, 0):j], wp, 3)
+        za[a] = cast[t] if a == t else arrive("ma%d" % a, "ma%d" % a, len(topo.engines(cores[a], core)), ARR_MAP[a ^ t])
+        c, s = slice(256 * a, 256 * a + 256), 0 if a in (1, 2) else 1
+        Z = (T.M16 if a == t else T.Z16)[:, c]
+        zl[a] = [za[a], za[a]]
+        if a != t ^ 2:
+            ta = ts("ta%d" % a, T.TA[:, c], Z, 1.0 / 16, 1408.0 - 15.0 / 32, A.mult, A.add, [za[a]], n=128, after=seq[-1:], boost=200.0)
+            tb = ts("tb%d" % a, T.TB[:, c], T.TA[:, c], -16.0, 22528.0, A.mult, A.add, [ta], n=128, boost=200.0)
+            db = ts("db%d" % a, T.DG[:, 512 * a + 256:512 * a + 512], T.TA[:, c], -1280.0, None, A.add, None, [ta], n=128, after=[tb], boost=200.0)
+            zl[a] = [dve("da%d" % a, 512, [tb], lambda q, a=a, c=c, Z=Z: q.tensor_tensor(T.DG[:, 512 * a:512 * a + 256], Z, T.TB[:, c], A.add), after=[db], boost=200.0), db]
+            seq.append(zl[a][0])
+        for g in (1, 0):
+            prs = []
+            for b in range(4):
+                for h in range(0 if b == a else 1 if a ^ t in TWICE else 2):
+                    r = 64 * s + 32 * h + STAGE[s]["%d%d" % (a, b)] + 8 * g
+                    prs.append((T.ST[r:r + 17:16, L - L * h:V + L - L * h], T.DG[32 * b:32 * b + 32, 512 * a + 256 * g:512 * a + 256 * g + 256]))
+            stg.append(dma("st%d%d" % (a, g), prs, 16e3 * len(prs), 32 * len(prs), [zl[a][g]] + edge, queues=both[g:g + 1], after=stg[-2:-1], boost=200.0))
+    for n, d in enumerate(TWICE):
+        a = t ^ d
+        s = 0 if a in (1, 2) else 1
+        rs = [64 * s + STAGE[s]["%d%d" % (a, b)] for b in range(4) if b != a]
+        stg.append(dma("sd%d" % a, [(T.ST[r + 32:r + 57:8, 0:V], T.ST[r:r + 25:8, L:V + L]) for r in rs], 98e3, 48, stg[2 * n:2 * n + 2], boost=200.0))
+    for o in ops[calm[0]:calm[1]]:
+        o["boost"] = 70.0
+        if o["name"][:2] in LATER.split():
+            o["ord"].append(seq[-1])
+    if DIRECT == 2:
+        gq.append(remote("h2", f_h2, len(topo.engines(core, cores[t ^ 1])), [fs[1], stg[HOLD]], after=gq[-1:], boost=300.0, move=0.6))
+    if "h1" not in SENDS:
+        gq.append(remote("h1", f_h1, len(topo.engines(core, cores[t ^ 2]) if DIRECT else up), [fs[2], stg[HOLD]], after=gq[-1:], boost=300.0, move=0.6))
+    for a in (t, t ^ 1, t ^ 3):
+        wl[a] = dma("wl%d" % a, [(T.WD[0:1, 8 * a:8 * a + 4], (T.M16 if a == t else T.Z16)[32 * a:32 * a + 1, 256 * a:256 * a + 4])], 0, 1, [za[a]], after=stg)
 
-            def cp(q, e, o, j=j, a=a, p=p):
-                r = []
-                for x in range(2):
-                    i = 2 * j + x
-                    out = T.MW[:, V * a + i:V * a + V:16]
-                    r.append(q.tensor_copy(out, pv(p, 256 * x, 256 * x + 256)) if e == "dve" else q.activation(out, pv(p, 256 * x, 256 * x + 256), AF.Copy))
-                return r
-            win[a].append(op("wc%d_%d" % (a, j), {"dve": 612 * CY, "act": 680 * CY}, [], cp, uses=p))
-        if b is None:
-            continue
-        win[b] = [dma("mv%d" % b, [(T.MW[0:120, V * b:V * b + V], T.MW[8:128, V * a:V * a + V]),
-                                   (T.MW[120:128, V * b:V * b + V], T.MW[0:8, V * a:V * a + V])], 1050e3, win[a])]
+    def LT(c, n=L, p=slice(0, 128)):
+        return T.LT[p, c:c + n]
 
-    col = {}
-    for p, (r, j) in enumerate(PAIRS):
-        for c in range(3):
-            col[(p, c)] = 192 * p + 64 * c
-        col["%d%d" % (r, j)] = 192 * p
-    for k, x in enumerate(EXTRA):
-        col[x] = LN_X + 64 * k
-    for a in range(4):
-        col["W%d%d" % (a, a ^ 1)] = LN_W + 64 * a
-        col["W%d%d" % (a, a ^ 2)] = LN_W + 256 + 64 * a
-    col["W03"], col["W12"] = LN_W + 512, LN_W + 576
+    def U(c, n=L):
+        return T.U[:, c:c + n]
 
-    def LN(x, n=64):
-        return T.LN[:, col[x]:col[x] + n]
-
-    def U(x):
-        return T.U[:, col[x]:col[x] + 64]
-    ln, ul = {}, {}
-    ln["id"] = ts("idl", LN("id"), T.IOT[:, 0:64], 16.0, D(6), A.mult, A.add, [d6, iot])
-    wgt = {}
-    needu = ("01", "23", "02", "13", "03", "12", "20", "21")
-    for a in (t, t ^ 1, t ^ 3, t ^ 2):
-        bs = [b for b in range(4) if b != a and (a, b) != (3, 2)]
-
-        def f(q, e, o, a=a, bs=bs):
-            r = []
-            for n, b in enumerate(bs):
-                for x in range(4):
-                    r.append(q.matmul(pv(o, 64 * n, 64 * n + 64), T.BL[:, 176 * b + 48 - 16 * x:176 * b + 176 - 16 * x],
-                                      zs[a][:, 256 * a + 64 * x:256 * a + 64 * x + 64], x == 0, x == 3))
-            if a < 3:
-                r.append(q.matmul(pv(o, 192, 196), T.OH[:, 128 * a:128 * a + 128], zs[a][:, 256 * a:256 * a + 4], True, True))
-            return r
-        p = pe("lp%d" % a, 832, [za[a]] + [bl[b] for b in bs] + oh[a:a + 1], f, 1)
-        prev = None
-        for n, b in enumerate(bs):
-            x = "%d%d" % (a, b)
-            if x in needu:
-                ul[x] = prev = dve("u" + x, 64, [prev], lambda q, p=p, n=n, x=x: q.tensor_scalar(U(x), pv(p, 64 * n, 64 * n + 64), 2048.0, None, A.add), uses=p)
-            ln[x] = prev = dve("n" + x, 64, [prev], lambda q, p=p, n=n, x=x: q.tensor_scalar(LN(x), pv(p, 64 * n, 64 * n + 64), 2048.0, None, A.add), uses=p)
-        if a < 3:
-            wgt[a] = dve("w%d" % a, 4, [prev], lambda q, p=p, a=a: q.tensor_scalar(T.WC[:, 4 * a:4 * a + 4], pv(p, 192, 196), 2048.0, -1.0, A.add, A.mult), uses=p)
-    for p, (r, j) in enumerate(PAIRS):
-        ln[(p, 0)], ul[(p, 0)] = ln["%d%d" % (r, j)], ul["%d%d" % (r, j)]
-
-    nr = [0]
-    rrow = {}
-
-    def mapg(name, lst, dep, a, b, key, want_u, out_to=None):
-        k = nr[0]
-        nr[0] += 1
-        Rk = T.R[:, Q * k:Q * k + Q]
-        w = T.MW[:, V * a:V * a + V] if a is not None else T.MW[:, 0:5 * V]
+    def given(name, pair, ws):
+        use = [(int(x[0]), bp[(int(x[1]), w)], g) for x in pair for g, w in enumerate(ws)]
 
         def f(q, e, o):
-            return [q.tensor_copy(Rk, w.indirect(lst)) if e == "dve" else q.activation(Rk, w.indirect(lst), AF.Copy)]
-        dur = {"dve": (Q * GA + 60) * CY, "act": (Q * GA + 80) * CY}
-        if out_to is not None:
-            dur.pop("dve" if b else "act")
-        gth = op("g" + name, dur, dep, f)
-        rrow[name] = k
+            mm = [(T.BP[:, m[0] + 32 - 32 * h:m[0] + 160 - 32 * h], T.DG[:, 512 * a + 256 * g + L * h:512 * a + 256 * g + L * h + L]) for a, m, g in use for h in range(2)]
+            return [q.matmul(pv(o, 0, L), l, r, n == 0, n == len(mm) - 1) for n, (l, r) in enumerate(mm)]
+        return pe("l" + name, 8 * L, sum([zl[a] + [m[1]] for a, m, g in use], []), f, 1)
 
-        def cv(q, e, o):
-            r = []
-            for i in range(16):
-                lt = T.BC[:, 144 * b + 15 - i:144 * b + 143 - i] if out_to is None else T.BO[:, 192 * b + 60 - 4 * i:192 * b + 188 - 4 * i]
-                r.append(q.matmul(pv(o, 0, 64), lt, T.R[:, Q * k + i:Q * k + Q:16], i == 0, i == 15))
-            return r
-        p = pe("cv" + name, 1024, [gth, bc[b] if out_to is None else bo[b]], cv, 1)
-        if out_to is not None:
-            return gth, addc("o" + name, out_to, lambda: pv(p, 0, 64), -4096, [], uses=p)
-        prev = None
-        if want_u:
-            ul[key] = prev = dve("u" + name, 64, [], lambda q: q.tensor_scalar(U(key), pv(p, 0, 64), -4096.0, None, A.add), uses=p)
-            ln[key] = addc("n" + name, LN(key), lambda: pv(p, 0, 64), -4096, [prev], uses=p)
-        else:
-            ln[key] = addc("n" + name, LN(key), lambda: pv(p, 0, 64), -4096, [], uses=p)
-        return gth, None
+    def tou(name, p, shift=None):
+        u = ulist()
+        if shift:
+            return u, dve("u" + name, L, [shift[1]], lambda q: q.tensor_scalar(U(u), pv(p, 0, L), shift[0], None, A.add), uses=p)
+        return u, dve("u" + name, L, [], lambda q: q.tensor_copy(U(u), pv(p, 0, L)), uses=p)
+
+    def tof(name, p, c0, part=slice(0, 128)):
+        return addc("n" + name, LT(c0, L, part), lambda: pv(p, 0, L, part), 0, [], uses=p)
+    lu, lf = {}, {}
+    for name, pair in (("p1", ("31", "20")), ("p2", ("21", "30"))):
+        lu[name] = tou(name, given(name, pair, (256, 1)), (sh, osh))
+
+    def fwt(q, e, o):
+        who = [[a if a in wl else a ^ (k + 1) for a in LEFT[k]] for k in range(3)]
+        return [q.matmul(pv(o, 4 * k, 4 * k + 4), T.OH[0:1, 64 - 64 * s:192 - 64 * s], T.WD[0:1, 8 * who[k][s]:8 * who[k][s] + 4], s == 0, s == 1)
+                for k in range(3) for s in range(2)]
+    wp = pe("wp", 400, list(wl.values()) + oh, fwt, 1)
+    wgt = addc("wgt", T.WC[:], lambda: pv(wp, 0, 12), -2048, [], n=64, uses=wp)
+
+    parts = ((0, CUT), (CUT, L))
+
+    def compose(k, win, lst, deps, cut=CUT):
+        res = []
+        for x, (a, b) in enumerate(((0, cut), (cut, L))):
+            def f(q, e, o, a=a, b=b):
+                out, w = T.R[:, HF * k + 16 * a:HF * k + 16 * b], win.indirect(U(lst[0] + a, b - a))
+                return [q.tensor_copy(out, w) if e == "dve" else q.activation(out, w, AF.Copy)]
+            n = 16 * (b - a) * GA
+            res.append(op("S%d%s" % (k, "ab"[x]), {"dve": (n + 60) * CY, "act": (n + 75) * CY}, deps + [lst[1]], f))
+        return res
+
+    def tolist(name, k, m, deps):
+        def f(q, e, o):
+            n = bc[m][0]
+            return [q.matmul(pv(o, 0, L), T.BC[:, 144 * n + 15 - i:144 * n + 143 - i],
+                             T.R[:, HF * k + i:HF * k + HF:16] if k else T.ST[:, L + 256 * i:2 * L + 256 * i], i == 0, i == 15) for i in range(16)]
+        return pe("cv" + name, 16 * L, deps + [bc[m][1]], f, 1)
+
+    def renew(name, moves, deps, step=8, **kw):
+        prs = []
+        for k, s, slot, s2, blk, slot2 in moves:
+            for h in range(2):
+                for h2 in range(2):
+                    r, r2 = 64 * s + 32 * h + slot, 64 * s2 + 32 * h2 + slot2
+                    prs.append((T.MW[r2:r2 + 33 - step:step, V * blk + HF * h:V * blk + HF * h + HF], T.R[r:r + 33 - step:step, HF * k:HF * k + HF]))
+        return dma(name, prs, 131e3 / step * len(prs), 16 * len(prs), deps, **kw)
 
     junk = [None, None]
     nj = [0]
 
-    def evaluate(p, c):
-        r, j = PAIRS[p]
-        k = 3 * p + c
-        h0 = Q * k
-        w = T["FW%d" % j][:, 0:V].indirect(U((p, c)))
+    def evaluate(k, c, lst):
+        h0 = HF * (3 * k + c)
+        z0 = HF * k
+        wk = min(k, 1)
+        hg = []
+        for x, (a, b) in enumerate(parts):
+            def fh(q, e, o, a=a, b=b):
+                out, w = T.H[:, h0 + 16 * a:h0 + 16 * b], T.FW[:, V * wk:V * wk + V].indirect(U(lst[0] + a, b - a))
+                if e == "dve":
+                    return [q.tensor_tensor(out, w, T.FR[:, z0 + 16 * a:z0 + 16 * b], A.subtract)]
+                return [q.activation(out, w, AF.Copy)]
+            n = 16 * (b - a) * GA
+            hg.append(op("h%d%d%s" % (k, c, "ab"[x]), {"dve": (n + 60) * CY, "act": (n + 75) * CY}, fw[wk] + fr[k] + [lst[1]], fh))
+        res = []
+        for x in range(2):
+            def f(q, e, o, x=x):
+                I, NI, NS, S = [T.ID[:, 128 * y:128 * y + 128] for y in range(4)]
+                raw = [g["eng"] == "act" for g in hg]
+                mm = []
+                for y in range(2):
+                    j0, j1 = Q * x + 512 * y, Q * x + 512 * y + 512
+                    tm = [(I, T.H, h0, 0, j0, j1), (NI, T.H, h0, 1, j0, min(j1, HF - 1))]
+                    for g, (a, b) in enumerate(parts):
+                        if raw[g]:
+                            tm += [(NI, T.FR, z0, 0, max(j0, 16 * a), min(j1, 16 * b)), (I, T.FR, z0, 1, max(j0, 16 * a - 1), min(j1, 16 * b - 1))]
+                    if j1 == HF:
+                        tm += [(NS, T.H, h0, 1 - HF, HF - 1, HF)] + ([(S, T.FR, z0, 1 - HF, HF - 1, HF)] if raw[0] else [])
+                    tm = [m for m in tm if m[5] > m[4]]
+                    mm += [q.matmul(pv(o, u - Q * x, v - Q * x), W, B[:, z + u + sh:z + v + sh], n == 0, n == len(tm) - 1) for n, (W, B, z, sh, u, v) in enumerate(tm)]
+                return mm
+            df = pe("df%d%d%d" % (k, c, x), 2112, hg[:x + 1] + fr[k] + idm, f, 2)
+            df["base"] = df["dur"]["pe"]
+            hg[x]["twice"] = [df]
+            acc = T.AC[:, 12 * k + 4 * x + c:12 * k + 4 * x + c + 1]
 
-        def fh(q, e, o):
-            if e == "dve":
-                return [q.tensor_tensor(T.H[:, h0:h0 + Q], w, T.FR[:, Q * r:Q * r + Q], A.subtract)]
-            return [q.activation(T.H[:, h0:h0 + Q], w, AF.Copy)]
-        hd = {"dve": (Q * GA + 60) * CY}
-        if ACT_H:
-            hd["act"] = (Q * GA + 80) * CY
-        hg = op("h%d%d" % (p, c), hd, [fw[j], fr[r], ul[(p, c)]], fh)
+            def ab(q, e, o, df=df, acc=acc):
+                if e == "dve":
+                    return [q.tensor_reduce(acc, pv(df, 0, Q), AxisListType.X, A.add, apply_absolute_value=True)]
+                y = nj[0] % 2
+                nj[0] += 1
+                if junk[y] is not None:
+                    o["wait"](junk[y])
+                junk[y] = o
+                return [q.activation(T.JK[:, Q * y:Q * y + Q], pv(df, 0, Q), AF.Abs, accum_out=acc)]
+            res.append(op("ab%d%d%d" % (k, c, x), {"dve": (Q + 35) * CY, "act": (Q + 100) * CY}, [ac0], ab, uses=df))
+        return res
 
-        def f(q, e, o):
-            I, NI, NS, S = [T.ID[:, 128 * x:128 * x + 128] for x in range(4)]
-            terms = [(T.H, h0, I, NI, NS)] + ([(T.FR, Q * r, NI, I, S)] if hg["eng"] == "act" else [])
-            res = []
-            for n, (B, z, P, M, W) in enumerate(terms):
-                res += [q.matmul(pv(o, 0, 512), P, B[:, z:z + 512], n == 0, False),
-                        q.matmul(pv(o, 0, 512), M, B[:, z + 1:z + 513], False, n == len(terms) - 1)]
-            for n, (B, z, P, M, W) in enumerate(terms):
-                res += [q.matmul(pv(o, 512, 1024), P, B[:, z + 512:z + Q], n == 0, False),
-                        q.matmul(pv(o, 512, 1023), M, B[:, z + 513:z + Q], False, False),
-                        q.matmul(pv(o, 1023, 1024), W, B[:, z:z + 1], False, n == len(terms) - 1)]
-            return res
-        df = pe("df%d%d" % (p, c), 2112, [hg, fr[r]] + idm, f, 2)
-        hg["twice"] = df
-        acc = T.AC[:, 4 * p + c:4 * p + c + 1]
-
-        def ab(q, e, o):
-            if e == "dve":
-                return [q.tensor_reduce(acc, pv(df, 0, Q), AxisListType.X, A.add, apply_absolute_value=True)]
-            x = nj[0] % 2
-            nj[0] += 1
-            if junk[x] is not None:
-                o["wait"](junk[x])
-            junk[x] = o
-            return [q.activation(T.JK[:, Q * x:Q * x + Q], pv(df, 0, Q), AF.Abs, accum_out=acc)]
-        return op("ab%d%d" % (p, c), {"dve": (Q + 60) * CY, "act": (Q + 110) * CY}, [ac0], ab, uses=df)
-
-    base = {}
-
-    def decide(p, abs_, nsel):
-        r, j = PAIRS[p]
-        n0 = 256 * p
-        L = [ln[(p, c)] for c in range(3)]
-        c0 = col[(p, 0)]
-        n1 = dve("ne1%d" % p, 256, L, lambda q: q.tensor_tensor(T.NE[:, n0:n0 + 128], T.LN[:, c0:c0 + 128], T.LN[:, c0 + 64:c0 + 192], A.not_equal))
-        n2 = dve("ne2%d" % p, 128, L, lambda q: q.tensor_tensor(T.NE[:, n0 + 128:n0 + 192], T.LN[:, c0 + 128:c0 + 192], T.LN[:, c0:c0 + 64], A.not_equal))
-        wcol = T.WC[:, 4 * r + (r ^ j) - 1:4 * r + (r ^ j)]
+    def decide(k, c0, lists, abs_):
+        n0 = 3 * L * k
+        n1 = dve("ne1%d" % k, 4 * L, lists, lambda q: q.tensor_tensor(T.NE[:, n0:n0 + 2 * L], LT(c0, 2 * L), LT(c0 + L, 2 * L), A.not_equal))
+        n2 = dve("ne2%d" % k, 2 * L, lists, lambda q: q.tensor_tensor(T.NE[:, n0 + 2 * L:n0 + 3 * L], LT(c0 + 2 * L), LT(c0), A.not_equal))
+        wcol = T.WC[:, 5 * k:5 * k + 1]
         es = []
         for c in range(3):
-            s = n0 + 64 * ((c + 1) % 3)
-            es.append(op("e%d%d" % (p, c), {"act": 180 * CY}, [n1, n2, wgt[r], ec0],
-                         lambda q, e, o, s=s, c=c: [q.activation(T.JS[:, 64 * (3 * p + c):64 * (3 * p + c) + 64], T.NE[:, s:s + 64], AF.Identity,
-                                                                 scale=wcol, accum_out=T.EC[:, 4 * p + c:4 * p + c + 1])]))
-        sc = pe("sc%d" % p, 512, es + abs_ + [one],
-                lambda q, e, o: [q.matmul(pv(o, 0, 4), T.ONE[:], T.EC[:, 4 * p:4 * p + 4], True, False),
-                                 q.matmul(pv(o, 0, 4), T.ONE[:], T.AC[:, 4 * p:4 * p + 4], False, True)], 1)
-        F = [T.FL[:, 4 * p + x:4 * p + x + 1] for x in range(3)]
-        f2 = dve("f2%d" % p, 1, [], lambda q: q.tensor_scalar(F[2], pv(sc, 0, 1), pv(sc, 1, 2), pv(sc, 2, 3), A.min, A.is_gt), uses=sc)
-        f1 = dve("f1%d" % p, 1, [], lambda q: q.tensor_scalar(F[1], pv(sc, 0, 1), pv(sc, 1, 2), 64.0, A.is_gt, A.mult), uses=sc)
-        fw_ = ts("fw%d" % p, F[0], F[2], 128.0, F[1], A.mult, A.max, [f1, f2])
-        if p == 0:
-            b1 = ts("b1", T.FL[:, 26:27], F[0], 64.0, None, A.mult, None, [fw_])
-            base["X01"] = (T.FL[:, 24:25], ts("b01", T.FL[:, 24:25], F[2], 2.0 * V, T.FL[:, 26:27], A.mult, A.add, [b1]))
-        if p == 1:
-            base["X23"] = (T.FL[:, 25:26], ts("b23", T.FL[:, 25:26], F[0], 64.0, 2.0 * V, A.mult, A.add, [fw_]))
-        return ts("of%d" % p, T.OF[:, 16 * p:16 * p + 4 * nsel], T.PC[:, 0:4 * nsel], F[0], None, A.add, None, [fw_, pc])
+            s = n0 + L * ((c + 1) % 3)
+            es.append(op("e%d%d" % (k, c), {"act": (L + 100) * CY}, [n2 if c == 1 else n1, wgt, ac0],
+                         lambda q, e, o, s=s, c=c: [q.activation(T.JS[:, n0 + L * c:n0 + L * c + L], T.NE[:, s:s + L], AF.Identity,
+                                                                 scale=wcol, accum_out=T.AC[:, 12 * k + 8 + c:12 * k + 9 + c])]))
+        ways = (0, 128) if k == 0 else (64, 192)
+        pre = dve("pre%d" % k, 4, es + abs_[0::2], lambda q: q.tensor_tensor(T.AC[:, 12 * k + 8:12 * k + 12], T.AC[:, 12 * k + 8:12 * k + 12], T.AC[:, 12 * k:12 * k + 4], A.add))
+        sc = pe("sc%d" % k, 4 * 256, [pre] + abs_ + sw,
+                lambda q, e, o: [q.matmul(pv(o, 4 * x, 4 * x + 4), T.SW[:, ways[x]:ways[x] + 128], T.AC[:, 12 * k + 4 * j:12 * k + 4 * j + 4], j == 2, j == 1)
+                                 for x in range(2) for j in (2, 1)], 1)
+        res = []
+        for x in range(2):
+            F = [T.FL[:, 8 * k + 2 * y + x:8 * k + 2 * y + x + 1] for y in range(3)]
+            f2 = dve("f2%d%d" % (k, x), 1, [], lambda q, F=F, x=x: q.tensor_scalar(F[2], pv(sc, 4 * x, 4 * x + 1), pv(sc, 4 * x + 1, 4 * x + 2), pv(sc, 4 * x + 2, 4 * x + 3), A.min, A.is_gt), uses=sc)
+            f1 = dve("f1%d%d" % (k, x), 1, [], lambda q, F=F, x=x: q.tensor_scalar(F[1], pv(sc, 4 * x, 4 * x + 1), pv(sc, 4 * x + 1, 4 * x + 2), 128.0, A.is_gt, A.mult), uses=sc)
+            res.append((F[0], ts("fw%d%d" % (k, x), F[0], F[2], 256.0, F[1], A.mult, A.max, [f1, f2])))
+        return res
+    no = [0]
 
-    ntb, nus = [0], [0]
+    def offs(name, base, F, how, deps):
+        c = 8 * no[0]
+        no[0] += 1
+        return c, ts("of" + name, T.OF[:, c:c + 8], base, F[0], None, how, None, deps + [F[1]])
 
-    def select(p, of, tables):
-        b0 = 192 * ntb[0]
-        ntb[0] += len(tables)
-        fill = []
-        for k, tb in enumerate(tables):
-            for c, (a, x) in enumerate(tb):
-                o0 = b0 + 192 * k + 64 * c
-                if a in base:
-                    fill.append(addc("tb%d%d%d" % (p, k, c), T.TB[:, o0:o0 + 64], (LN(x),), base[a][:1], [ln[x], base[a][1]]))
-                else:
-                    fill.append(addc("tb%d%d%d" % (p, k, c), T.TB[:, o0:o0 + 64], (LN(x),), V * a, [ln[x]]))
-        n = len(tables)
-        u0 = 64 * nus[0]
-        nus[0] += n
-        s = dve("sl%d" % p, 64 * n * GA, fill + [of],
-                lambda q: q.tensor_copy(T.US[:, u0:u0 + 64 * n], T.TB[:, b0:b0 + 192 * n].indirect(T.OF[:, 16 * p:16 * p + 4 * n])))
-        return s, [T.US[:, u0 + 64 * k:u0 + 64 * k + 64] for k in range(n)]
+    def pick(name, to, c0, n, of, k, deps):
+        w = LT(c0, n * L).indirect(T.OF[:, of:of + 8 * k])
+        dur = {"dve": (L * k * GA + 60) * CY}
+        if to is None:
+            u = ulist(k)
+            return u, op("pu" + name, dur, deps, lambda q, e, o: [q.tensor_copy(U(u, k * L), w)])
+        dur["act"] = (L * k * GA + 75) * CY
+        return op("pk" + name, dur, deps, lambda q, e, o: [q.tensor_copy(LT(to, k * L), w) if e == "dve" else q.activation(LT(to, k * L), w, AF.Copy)])
 
-    def chosen(p, of, key=None, at=None):
-        c0 = col[(p, 0)]
-        w = T.LN[:, c0:c0 + 192].indirect(T.OF[:, 16 * p:16 * p + 4])
-        dep = [of] + [ln[(p, c)] for c in range(3)]
-        if key is not None:
-            ln[key] = dve("ch" + key, 100, dep, lambda q: q.tensor_copy(LN(key), w))
-            return None
-        u0 = 64 * nus[0]
-        nus[0] += 1
-        if at is not None:
-            return (dve("cu%d" % p, 100, dep + [base[at][1]], lambda q: q.tensor_scalar(T.US[:, u0:u0 + 64], w, base[at][0], None, A.add)),
-                    T.US[:, u0:u0 + 64])
-        return dve("cu%d" % p, 100, dep, lambda q: q.tensor_copy(T.US[:, u0:u0 + 64], w)), T.US[:, u0:u0 + 64]
-
-    def renew(name, maps, dep):
-        prs = []
-        for x, a, b in maps:
-            k = rrow[x]
-            for dg in range(2):
-                r = 4 * dg + b
-                for q in range(4):
-                    prs.append((T.MW[16 * q + r:128:64, V * a:V * a + V], T.R[r:128:16, Q * k:Q * k + Q]))
-        return dma(name, prs, 16e3 * len(prs), dep)
-
-    outs = []
-
-    def ship(name, d, dests, dep, late):
-        far_ = [a for a in dests if a != t]
-        if t in dests:
-            outs.append(dma("y%d%d" % (t, d), [(T.ym[32 * t:32 * t + 32, 256 * (d - 1):256 * d], T.OUT[:, 64 * (4 * (d - 1) + t):64 * (4 * (d - 1) + t) + 64])],
-                            32e3, dep + late))
-        if not far_:
-            return
-        es = topo.engines(core, cores[far_[0]])
-        per = {1: len(es), 2: len(es) // 2, 3: len(es) // 4}[len(far_)]
+    def ship(name, d, items, late):
+        away = [(a, c0) for a, c0, dep in items if a != t]
+        k = 3 * t + d - 1
+        for a, c0, dep in items:
+            if a == t and d < 3:
+                home(t, d, T.LT, c0, [dep] + late)
+            elif a == t:
+                home(t, d, T.YL, L * k, [widen(t, U(c0), [dep])])
+        es = topo.engines(core, cores[away[0][0]])
+        per = {1: len(es), 2: len(es) // 2, 3: len(es) // 4}[len(away)]
 
         def f(q):
-            q.remote_dma_fused([RemoteDMATransfer(dst_ids=[dst(cores[a])], dma_engine_mask=bits(es[per * n:per * n + per]), remote_sem=T.sem["oa%d" % (3 * t + d - 1)],
-                                                  src=T.OUT[:, 64 * (4 * (d - 1) + a):64 * (4 * (d - 1) + a) + 64],
-                                                  dst=T.YL[:, 64 * (3 * t + d - 1):64 * (3 * t + d - 1) + 64]) for n, a in enumerate(far_)], local_sem=T.sem.lsem)
+            q.remote_dma_fused([RemoteDMATransfer(dst_ids=[dst(cores[a])], dma_engine_mask=bits(es[per * n:per * n + per]), remote_sem=T.sem["oa%d" % k],
+                                                  src=LT(c0) if d < 3 else U(c0), dst=T.YL[:, L * k:L * k + L] if d < 3 else T.YU[:, L * t:L * t + L])
+                                for n, (a, c0) in enumerate(away)], local_sem=T.sem.lsem)
             return []
-        gq.append(remote(name, f, per * len(far_), dep, after=gq[-1:], boost=(30.0, 14.0, 6.5)[d - 1]))
-        return gq[-1]
+        gq.append(remote(name, f, per * len(away), [dep for a, c0, dep in items if a != t], after=gq[-1:], boost=(30.0, 14.0, 6.5)[d - 1]))
 
-    def turn(name, key, n, o0, dep):
-        p = pe("tp" + name, 4 * n, dep + [pm], lambda q, e, o: [q.matmul(pv(o, 0, n), T.PM[:], LN(key, n), True, True)], 1)
-        return addc("to" + name, T.OUT[:, o0:o0 + n], lambda: pv(p, 0, n), 0, [], n=n, uses=p)
+    def widen(s, src, deps):
+        return dve("wi%d" % s, L, deps, lambda q: q.tensor_copy(T.YL[:, L * (3 * s + 2):L * (3 * s + 3)], src))
 
-    allwin = win[0] + win[1] + win[2] + win[3]
-    ab = {(p, 0): evaluate(p, 0) for p in range(6)}
-    G = []
-    for name, a, b, x, key, wu in (("C011", 2, 1, "02", (0, 1), True), ("C012", 3, 1, "03", (0, 2), True), ("C231", 0, 3, "20", (1, 1), True),
-                                   ("C232", 1, 3, "21", (1, 2), True)):
-        G.append(mapg(name, U(x), [ul[x]] + win[a], a, b, key, wu)[0])
-    for p in (0, 1):
-        for c in (1, 2):
-            ab[(p, c)] = evaluate(p, c)
-    def zero(q, e, o, x):
-        out = T.MW[:, 4 * V + Q * x:4 * V + Q * x + Q]
-        return [q.memset(out, 0.0) if e == "dve" else q.activation(out, T.FS[:, 0:Q], AF.Copy, scale=0.0)]
-    fill4 = [op("m4%d" % x, {"act": 1100 * CY}, [fs[1]], lambda q, e, o, x=x: zero(q, e, o, x)) for x in range(4)]
-    for o in fill4:
-        o["boost"] = 250.0
-    nw0 = renew("nw0", [("C011", 1, 1), ("C012", 4, 1), ("C231", 3, 3), ("C232", 4, 3)], G + allwin + fill4)
-    of0 = decide(0, [ab[(0, c)] for c in range(3)], 2)
-    of1 = decide(1, [ab[(1, c)] for c in range(3)], 3)
-    G = []
-    cu, lst = chosen(0, of0)
-    G.append(mapg("C021", lst, [cu, nw0], 1, 2, (2, 1), True)[0])
-    s0, l0 = select(0, of0, [[(0, "10"), (3, "12"), (1, "id")], [(1, "id"), (2, "12"), (3, "13")]])
-    s1, l1 = select(1, of1, [[(3, "03"), (0, "id"), (1, (0, 2))], [(2, "12"), (3, "12"), (1, "id")], [(3, "id"), (0, "30"), (1, "31")]])
-    G.append(mapg("C131", l0[0], [s0, nw0], None, 3, (3, 1), True)[0])
-    G.append(mapg("C022", l1[0], [s1, nw0], None, 2, (2, 2), True)[0])
-    G.append(mapg("C132", l1[1], [s1, nw0], None, 3, (3, 2), True)[0])
-    G.append(mapg("W10", l0[1], [s0, nw0], None, 0, "W10", False)[0])
-    G.append(mapg("W32", l1[2], [s1, nw0], None, 2, "W32", False)[0])
-    nw1 = renew("nw1", [("W32", 3, 2), ("W10", 1, 0)], G)
-    chosen(0, of0, "W01")
-    chosen(1, of1, "W23")
-    o1 = turn("1", "W01", 256, 0, [ln[x] for x in ("W01", "W10", "W23", "W32")])
-    for p in (2, 3):
-        for c in (1, 2):
-            ab[(p, c)] = evaluate(p, c)
-    of2 = decide(2, [ab[(2, c)] for c in range(3)], 2)
-    of3 = decide(3, [ab[(3, c)] for c in range(3)], 2)
-    G = []
-    cu2, lst2 = chosen(2, of2, at="X23")
-    cu3, lst3 = chosen(3, of3)
-    s2, l2 = select(2, of2, [[(0, "W10"), (1, "id"), (3, (3, 1))], [(2, "id"), (1, "21"), (3, "W23")]])
-    s3, l3 = select(3, of3, [[(1, "W01"), (0, "id"), ("X23", (2, 1))], [(3, "id"), ("X01", "30"), (2, "W32")]])
-    G.append(mapg("C032", lst2, [cu2, nw1], None, 3, (4, 2), True)[0])
-    G.append(mapg("C121", l2[0], [s2, nw1], None, 2, (5, 1), True)[0])
-    G.append(mapg("C031", l3[0], [s3, nw1], None, 3, (4, 1), True)[0])
-    G.append(mapg("C122", lst3, [cu3, nw1], 3, 2, (5, 2), True)[0])
-    G.append(mapg("W20", l2[1], [s2, nw1], None, 0, "W20", False)[0])
-    G.append(mapg("W31", l3[1], [s3, nw1], None, 1, "W31", False)[0])
-    nw2 = renew("nw2", [("W20", 2, 0), ("W31", 3, 1)], G)
-    chosen(2, of2, "W02")
-    chosen(3, of3, "W13")
-    o2 = turn("2", "W02", 256, 256, [ln[x] for x in ("W02", "W13", "W20", "W31")])
-    for p in (4, 5):
-        for c in (1, 2):
-            ab[(p, c)] = evaluate(p, c)
-    of4 = decide(4, [ab[(4, c)] for c in range(3)], 1)
-    of5 = decide(5, [ab[(5, c)] for c in range(3)], 1)
-    s4, l4 = select(4, of4, [[(3, "id"), (1, "W31"), (2, "W32")]])
-    s5, l5 = select(5, of5, [[(2, "id"), ("X01", "W20"), (3, "W23")]])
-    o30 = mapg("W30", l4[0], [s4, nw2], None, 0, None, False, out_to=T.OUT[:, 64 * 11:64 * 12])[1]
-    o21 = mapg("W21", l5[0], [s5, nw2], None, 1, None, False, out_to=T.OUT[:, 64 * 10:64 * 11])[1]
-    chosen(4, of4, "W03")
-    chosen(5, of5, "W12")
-    o03 = turn("03", "W03", 64, 512, [ln["W03"]])
-    o12 = turn("12", "W12", 64, 576, [ln["W12"]])
-    o3 = [o03, o12, o21, o30]
-    x1 = ship("x1", 1, [0, 1, 2, 3], [o1], [nw1])
-    x2 = ship("x2", 2, [0, 1, 2, 3], [o2], [nw2])
-    for a in (1, 2, 0, 3):
-        ship("x3%d" % a, 3, [a], [o3[a]], [])
-    for d, mine, late in ((1, o1, [nw2]), (2, o2, [of5]), (3, o3[t], [])):
+    def home(s, d, B, c0, deps):
+        r = 64 * HOME[t][d - 1]
+        dma("y%d%d" % (s, d), [(T.ym[32 * s:32 * s + 32, 256 * (d - 1) + L * h:256 * (d - 1) + L * h + L], B[r + 32 * h:r + 32 * h + 32, c0:c0 + L]) for h in range(2)],
+            32e3, 64, deps, queues=both if d == 3 else ("sp",))
+
+    B0, B1, BB = T.MW[:, 0:V], T.MW[:, V:2 * V], T.MW[:, 0:2 * V]
+    SA, SB = slice(0, 64), slice(64, 128)
+    stg = stg + spare[:1]
+
+    def order(q, e, i0):
+        prs = [(T.R[:, i:HF:16], T.ST[:, L + 256 * i:2 * L + 256 * i]) for i in range(i0, i0 + 4)]
+        return [q.tensor_copy(a, b) if e == "dve" else q.activation(a, b, AF.Copy) for a, b in prs]
+    S0 = [op("N%d" % i0, {"dve": 4 * 100 * CY, "act": 4 * 210 * CY}, stg, lambda q, e, o, i0=i0: order(q, e, i0)) for i0 in range(0, 16, 4)]
+    S1 = compose(1, T.ST[:, 0:V + L], lu["p1"], stg)
+    S2 = compose(2, T.ST[:, 0:V + L], lu["p2"], stg, CUT2)
+    wa = [renew("wa", [(0, s, 0, s, 1, 0) for s in range(2)], S0, 2)]
+    w1 = wa + [renew("wb", [(1, 0, 3, 1, 1, 5), (1, 1, 3, 0, 1, 7)], S1)]
+    w1 += [renew("wc%d" % s, [(2, s, 5, s, 1, (5, 7)[s])], S2, queues=both[s:s + 1]) for s in range(2)]
+    behind = {a: stg if a == t else (wa, w1[:2], w1)[EARLY[a ^ t]] for a in range(4)}
+    w1 = w1 + spare[1:]
+    fw = [[fwin(0, 0, 1, behind[1]), fwin(0, 1, 3, behind[3])]]
+    fr = [[fleft(0, s, LEFT[0][s], behind[LEFT[0][s]]) for s in range(2)]]
+    fr += [[fleft(k, s, LEFT[k][s], w1 + fw[0] + fr[0]) for s in range(2)] for k in (1, 2)]
+    fw.append([fwin(1, 0, 2, w1 + fw[0] + fr[0]), fwin(1, 1, 3, w1 + fw[0] + fr[0])])
+    w0 = [renew("wd", [(0, s, 1, s, 0, 1) for s in range(2)], S0, 2, after=fw[1] + fr[1]),
+          renew("wh", [(0, s, 1, 1 - s, 0, 2) for s in range(2)], S0, after=fw[1] + fr[1])]
+    for name, pair, places, wu in (("1", ("02", "13"), [T3], 1), ("2", ("12", "03"), [T4, TZ + L], 1), ("0", ("01", "23"), [T1], 1), ("3", ("32", "10"), [T2], 0),
+                                   ("5", None, [TW + 2 * L], 0)):
+        p = given(name, pair, (1, 16)) if pair else tolist("g" + name, 0, "2x", stg)
+        if wu:
+            lu[name] = tou(name, p)
+        for n, c0 in enumerate(places):
+            lf[c0] = [tof("%s%d" % (name, n), p, c0)]
+    ab = {(k, 0): evaluate(k, 0, lu[str(k)]) for k in range(3)}
+    S3 = compose(3, B1, lu["1"], w1)
+    S4 = compose(4, B1, lu["2"], w1)
+    w0 += [renew("we", [(3, 0, 2, 1, 0, 0), (3, 0, 2, 0, 0, 4), (3, 1, 2, 0, 0, 7), (3, 1, 2, 1, 0, 6)], S3 + w0[:1]),
+           renew("wf", [(4, 0, 4, 0, 0, 0), (4, 0, 4, 1, 0, 4), (4, 1, 4, 1, 0, 7), (4, 1, 4, 0, 0, 6)], S4 + w0[:1])]
+    for name, k, m, S, ca, cb in (("1", 1, "3s", S1, T2 + 2 * L, T1 + L), ("2", 2, "5x", S2, T2 + L, T1 + 2 * L),
+                                  ("3", 3, "2s", S3, T1 + L, T2 + 2 * L), ("4", 4, "4x", S4, T1 + 2 * L, T2 + L)):
+        p = tolist(name, k, m, S)
+        for c0, part in sorted(((ca, SA), (cb, SB)), key=lambda z: z[0]):
+            lf.setdefault(c0, []).append(tof("c%s%d" % (name, c0 // L), p, c0, part))
+    for c in (1, 2):
+        u = ulist()
+        ab[(0, c)] = evaluate(0, c, (u, dve("uc%d" % c, L, lf[T1 + c * L], lambda q, u=u, c=c: q.tensor_copy(U(u), LT(T1 + c * L)))))
+    t1 = lf[T1] + lf[T1 + L] + lf[T1 + 2 * L]
+    t12 = t1 + lf[T2] + lf[T2 + L] + lf[T2 + 2 * L]
+    FA, FB = decide(0, T1, t1, ab[(0, 0)] + ab[(0, 1)] + ab[(0, 2)])
+    matrix("dx", "x", T.MK[:, 72:73], [mask("mdx", T.MK[:, 72:73], (sl["d"][0], FB[0]), [sl["d"][1], FB[1]])])
+    of5, o = offs("5", T.PC[:, 8:16], FA, A.add, [pcb])
+    S5 = compose(5, B0, pick("5", None, T1, 6, of5, 1, t12 + [o]), w0)
+    r1 = pick("o1", O1, T1, 6, of5, 1, t12 + [o])
+    of6, o = offs("6", T.PC[:, 16:24], FB, A.add, [pca])
+    r2 = pick("o2", O2, T1, 6, of6, 1, t12 + [o])
+    u = ulist()
+    lu["v"] = u, dve("uv", L, [r2], lambda q, u=u: q.tensor_copy(U(u), LT(O2)))
+    mk1 = [mask("k1", T.MK[:, 0:7:3], (trio, FA[0]), [sl[n][1] for n in "nfg"] + [FA[1]])]
+    ship("x1", 1, [(0, O1, r1), (1, O1, r1), (2, O2, r2), (3, O2, r2)], [])
+    for c, k, m, S in ((2, 4, "dx", S4), (1, 5, "3s", S5)):
+        p = tolist("r%d" % c, k, m, S)
+        lu["r"] = tou("r%d" % c, p)
+        ab[(1, c)] = evaluate(1, c, lu["r"])
+        lf[T3 + c * L] = [tof("r%d" % c, p, T3 + c * L)]
+    S6 = compose(6, B1, lu["r"], w1)
+    for name, k, m, S, c0 in (("y", 3, "dx", S3, TZ + 3 * L), ("x", 5, "5x", S5, TZ), ("z", 6, "dx", S6, TZ + 2 * L)):
+        lf[c0] = [tof(name, tolist(name, k, m, S), c0)]
+    t3 = lf[T3] + lf[T3 + L] + lf[T3 + 2 * L]
+    FO, FX = decide(1, T3, t3, ab[(1, 0)] + ab[(1, 1)] + ab[(1, 2)])
+    tz = sum([lf[TZ + n * L] for n in range(4)], [])
+    ofa, oa = offs("a", T.PC[:, 0:8], FO, A.add, [pc0])
+    ofb, ob = offs("b", T.PC[:, 24:32], FX, A.subtract, [pc3])
+    u3, o3 = pick("3", None, TZ, 4, ofa, 2, tz + [oa, ob])
+    lf[T4 + L] = [pick("3", T4 + L, TZ, 4, ofa, 2, tz + [oa, ob])]
+    r3 = pick("o3", O3, T3, 3, ofa, 1, t3 + [oa])
+    g7 = ts("g7", T.FL[:, 30:31], FX[0], 256.0, 128.0, A.is_lt, A.mult, [FX[1]])
+    g8 = ts("g8", T.FL[:, 31:32], FX[0], 256.0, float(V), A.is_equal, A.mult, [FX[1]])
+    of7, o = offs("7", T.PC[:, 0:8], (T.FL[:, 30:31], g7), A.add, [pc0])
+    u = ulist()
+    S7 = compose(7, BB, (u, dve("pu7", L * GA + 25, [r2, o, g8] + lf[TW + 2 * L], lambda q, u=u: q.tensor_scalar(
+        U(u), LT(O2, 2 * L).indirect(T.OF[:, of7:of7 + 8]), T.FL[:, 31:32], None, A.add))), w0 + w1)
+    du = [ts("du%d" % x, T.OF[:, 72 + x:73 + x], F[0], 1.0 / 128, c, A.mult, A.add, [F[1]]) for x, F, c in ((0, FO, 5.0), (1, FX, 2.0))]
+    pm = dve("pm", 48, mk + mk1 + du, lambda q: q.tensor_copy(T.MK[:, 16:48], T.MK[:, 0:8].indirect(T.OF[:, 72:74])))
+    matrix("7", "s", T.MK[:, 32:33], [pm])
+    matrix("8", "s", T.MK[:, 0:1], mk1)
+    matrix("9", "s", T.MK[:, 16:17], [pm])
+    p = tolist("7", 7, "7", S7)
+    r4 = tof("7", p, TW)
+    w2 = renew("wg", [(7, s, 0, 1 - s, 1, 1) for s in range(2)], S7 + S6, 2)
+    ship("x2", 2, [(0, O3, r3), (1, O3, r3)], [w2])
+    ship("x5", 2, [(2, TW, r4), (3, TW, r4)], [w2])
+    for c in (1, 2):
+        ab[(2, c)] = evaluate(2, c, (u3 + L * (c - 1), o3))
+    t4 = lf[T4] + lf[T4 + L]
+    GO, GX = decide(2, T4, t4, ab[(2, 0)] + ab[(2, 1)] + ab[(2, 2)])
+    inv = [tof("8", tolist("8", 8, "8", compose(8, B0, tou("8", p), w0)), TW + 3 * L),
+           tof("9", tolist("9", 9, "9", compose(9, B1, lu["v"], [w2])), TW + 4 * L)]
+    of8, o = offs("8", T.PC[:, 0:8], GX, A.add, [pc0])
+    u6, r6 = pick("o6", None, TW + 2 * L, 3, of8, 1, lf[TW + 2 * L] + inv + [o])
+    of9, o = offs("9", T.PC[:, 0:8], GO, A.add, [pc0])
+    u5, r5 = pick("o5", None, T4, 3, of9, 1, t4 + [o])
+    last = [[(0, u5, r5), (1, u5, r5)], [(2, u6, r6), (3, u6, r6)]]
+    if ONE:
+        ship("x3", 3, last[0] + last[1], [])
+    else:
+        ship("x3", 3, last[0], [])
+        ship("x4", 3, last[1], [])
+    for d, mine, late in ((1, r2, [w2]), (2, r4, [GO[1]]), (3, r5 if t < 2 else r6, [])):
         for s in range(4):
             if s == t:
                 continue
             ne = len(topo.engines(cores[s], core))
-            grp = [a for a in ([0, 1, 2, 3] if d < 3 else [t]) if a != s]
+            grp = [a for a in ([0, 1, 2, 3] if d < 2 or ONE else [t & 2, (t & 2) + 1]) if a != s]
             k = 3 * s + d - 1
             ar = arrive("oa%d" % k, "oa%d" % k, {1: ne, 2: ne // 2, 3: ne // 4}[len(grp)], 0.0, [mine])
             ar["tail"] = 4.0
-            outs.append(dma("y%d%d" % (s, d), [(T.ym[32 * s:32 * s + 32, 256 * (d - 1):256 * d], T.YL[:, 64 * k:64 * k + 64])], 32e3, [ar] + late,
-                            queues=("sp", "act") if d == 3 else ("sp",)))
+            home(s, d, T.YL, L * k, [ar] + late if d < 3 else [widen(s, T.YU[:, L * s:L * s + L], [ar])])
+    named = {o["name"]: o for o in ops}
+    for e, names in ORDER.items():
+        row = [named[x] for x in names.split()]
+        for a, b in zip([None] + row, row):
+            b["dur"] = {e: b["dur"][e]}
+            b["ord"] += [a] if a else []
     return ops
 
 
@@ -706,20 +798,21 @@ def rank_program(g, core, T, topo):
     if rank is None:
         for a, c in enumerate(T.cores):
             hs = helpers(topo, c)
-            if core not in hs:
+            if core not in (hs[:3], hs[:2], hs[1:2], hs)[DIRECT]:
                 continue
-            up = len(topo.engines(c, core)) // 2
-            jobs = [((0, 1, "hs0", up // 2), (1, 3, "hs0", up // 2), (2, 2, "hs1", up))[hs.index(core)]]
-            n = 0
-            for k, d, s, v in jobs:
-                to = T.cores[a ^ d]
-                r, p, _ = topo.addr(to)
-                g.wait_ge(T.sem[s], v)
-                g.remote_dma(T.FD[a], T.FS[:, Q * k:Q * k + Q], T.sem["fa%d" % a], T.sem.lsem, p, r, topo.mask(core, to))
-                n += len(topo.engines(core, to))
-            g.wait_ge(T.sem.lsem, n)
+            up = len(topo.engines(c, core)) // SHARE
+            k, d, s, v = ((0, 1, "hs0", up // 2), (1, 3, "hs0", up // 2), (2, 2, "hs1", up // 2 if DIRECT else up), (2, 2, "hs1", up // 2))[hs.index(core)]
+            to = T.cores[a ^ d]
+            r, p, _ = topo.addr(to)
+            g.wait_ge(T.sem[s], v)
+            out, src = T.FD[a], T.FS[:, Q * k:Q * k + Q]
+            if DIRECT == 3 and k == 2:
+                y = 3 - hs.index(core)
+                out, src = T.FE[y], T.FS[:, 2 * Q + 512 * y:2 * Q + 512 * y + 512]
+            g.remote_dma(out, src, T.sem["fa%d" % a], T.sem.lsem, p, r, topo.mask(core, to))
+            g.wait_ge(T.sem.lsem, len(topo.engines(core, to)))
         return
-    order = plan(build(rank, T, topo, core), SEEDS[rank])
+    order = arrange(lambda: build(rank, T, topo, core), SEEDS[rank])
     queue = {"pe": g.tensor, "dve": g.vector, "act": g.scalar, "sp": g.sync, "g": g}
     own = {"pe": "pe", "dve": "dve", "act": "act", "g": "pool"}
     count = {}

import numpy as np
from concourse.bass import DstId, RemoteDMATransfer
from concourse.mybir import AluOpType as A, AxisListType, ActivationFunctionType as AF

N, V, HF, Q, L = 4, 4096, 2048, 1024, 128
CUT = 66
SEEDS = [[0], [0], [0], [0]]
SENDS = (1, "h0", 3, 2, "h1")
LOADS = ("mp1", "mp3", "mp2", "fs2", "mp0", "fs1", "fs3")
ONE, SHARE, TWICE = False, 1, (0,)
LATER = "id k7 k9 k0 oh"
ORDER = {"dve": "N0 N4 N8 N12 S2a S3a S4a h00a h01b h01a h02a ne10 ne20 h02b h10b h10a h12a h12b h11a h11b ne11 ab110 ne21 ab111 h20b h22a h21a ne12 ne22 h21b ab210 h22b S9a S8a",
         "act": "S1a S1b S2b wc1 S3b S4b h00b ab000 ab001 ab011 e01 e00 ab010 ab020 e02 ab021 S5a S5b ab100 ab101 ab120 ab121 S6a e10 S6b e11 e12 h20a "
                "S7b pk3 ab200 S7a ab201 e20 e21 e22 S8b ab220 S9b ab211 ab221",
         "pe": "cvg5 cv1 cv2 cv3 cv4 df000 df001 df011 df010 df020 df021 sc0 df100 cvr2 df101 cvr1 df120 df121 cvx df110 df111 cvy sc1 cvz "
               "df200 df201 df210 cv7 df220 df211 df221 cv9 sc2 cv8"}
RAW, LONG, ABS, SHORT, PASSES = -0.9, 0.4, 1.0, 2.0, 1
DIRECT, HOLD, CUT2 = 3, 7, 86
EARLY = {1: 2, 3: 2, 2: 2}
LEFT = ((0, 2), (0, 1), (1, 0))
STAGE = ({"10": 1, "12": 3, "13": 5, "21": 2, "20": 4, "23": 6}, {"01": 1, "03": 3, "02": 5, "30": 2, "31": 4, "32": 6})
HOME = ((0, 0, 1), (1, 1, 0), (1, 1, 1), (0, 0, 0))
T1, T2, T3, TZ, T4, TW, O2, O1, O3, LT_END = [L * x for x in (0, 3, 6, 9, 13, 16, 17, 21, 22, 23)]

SCRATCH = {
    "M": ("sbuf", [128, 4, 256], "int32"),
    "MA": ("sbuf", [128, 256], "int32"),
    "DS": ("sbuf", [128, 512], "bfloat16"),
    "M16": ("sbuf", [128, 1024], "float16"),
    "Z16": ("sbuf", [128, 1024], "float16"),
    "TA": ("sbuf", [128, 1024], "float16"),
    "TB": ("sbuf", [128, 1024], "float16"),
    "DG": ("sbuf", [128, 8 * 256], "bfloat16"),
    "WD": ("sbuf", [128, 32], "float16"),
    "ST": ("sbuf", [128, V + L], "bfloat16"),
    "MW": ("sbuf", [128, 2 * V], "bfloat16"),
    "FW": ("sbuf", [128, 2 * V], "bfloat16"),
    "FR": ("sbuf", [128, 3 * HF], "bfloat16"),
    "FS": ("sbuf", [128, 3 * Q], "bfloat16"),
    "FD": ("dram", [4, 128, Q], "bfloat16"),
    "FE": ("dram", [2, 128, Q // 2], "bfloat16"),
    "H": ("sbuf", [128, 9 * HF], "bfloat16"),
    "R": ("sbuf", [128, 10 * HF], "bfloat16"),
    "JK": ("sbuf", [128, 2 * Q], "bfloat16"),
    "JS": ("sbuf", [128, 9 * L], "float32"),
    "LT": ("sbuf", [128, LT_END], "float32"),
    "U": ("sbuf", [128, 22 * L], "uint16"),
    "NE": ("sbuf", [128, 9 * L], "bfloat16"),
    "AC": ("sbuf", [128, 36], "float32"),
    "FL": ("sbuf", [128, 32], "float32"),
    "WC": ("sbuf", [128, 12], "float32"),
    "OF": ("sbuf", [128, 80], "uint16"),
    "MK": ("sbuf", [128, 96], "float32"),
    "YL": ("sbuf", [128, 12 * L], "float32"),
    "YU": ("sbuf", [128, 4 * L], "uint16"),
    "IOT": ("sbuf", [128, 160], "float32"),
    "KI": ("sbuf", [128, 2], "int32"),
    "CI": ("sbuf", [128, 9], "int32"),
    "CF": ("sbuf", [128, 9], "float32"),
    "MB": ("sbuf", [128, 12], "float32"),
    "CD": ("sbuf", [128, 48], "float32"),
    "PC": ("sbuf", [128, 32], "float32"),
    "BC": ("sbuf", [128, 13 * 144], "bfloat16"),
    "BP": ("sbuf", [128, 11 * 160], "bfloat16"),
    "OH": ("sbuf", [128, 192], "float16"),
    "ID": ("sbuf", [128, 4 * 128], "bfloat16"),
    "SW": ("sbuf", [128, 320], "float32"),
    "E0": ("psum", [128, 1024], "float32"),
    "E1": ("psum", [128, 1024], "float32"),
    "E2": ("psum", [128, 1024], "float32"),
    "E3": ("psum", [128, 1024], "float32"),
}
SEMAPHORES = (["pe", "dve", "act", "pool", "lsem", "hs0", "hs1"] + ["ma%d" % a for a in range(4)] + ["fa%d" % a for a in range(4)]
              + ["oa%d" % k for k in range(12)] + ["d%d" % k for k in range(72)])

CY, PCY, GA, LAT = 1.0e-3, 0.5e-3, 1.5, 0.1
ARR_MAP = {1: 7.9, 3: 8.6, 2: 9.9}
ARR_FT = {1: 16.5, 3: 16.5, 2: 19.0}
ISSUE, DLAT, DRATE, DROW = 0.1, 1.8, 600e3, 0.012 / 16
WIDE = 2


def helpers(topo, core):
    near = [c for c in topo.cores_of(core) if c != core and topo.die(c) == topo.die(core)]
    far = [c for c in topo.cores_of(core) if topo.die(c) != topo.die(core)]
    return near[0], far[0], far[1], near[1]


def bits(es):
    return sum(1 << e for e in es)


def backwards(order):
    need, free = {}, {}
    for o in sorted(order, key=lambda x: -x["end"]):
        e = o["eng"]
        after = need.get(o["n"], 0.0) + o["tail"] + o["move"]
        need[o["n"]] = max(max(after, free.get(e, 0.0) if e in ("dve", "act", "pe") else 0.0) + o["dur"][e], o["boost"])
        if not o["boost"]:
            free[e] = need[o["n"]]
        for d in o["deps"] + o["ord"]:
            need[d["n"]] = max(need.get(d["n"], 0.0), need[o["n"]] + LAT)
    return need


def arrange(make, seed):
    best, late = None, None
    for _ in range(PASSES):
        order = plan(make(), seed, late)
        end = max(o["end"] for o in order)
        if best is None or end < best[0]:
            best = (end, order)
        late = backwards(order)
    return best[1]


def plan(ops, seed, late=None):
    rng = np.random.RandomState(seed[0])
    beta, pen = float(rng.uniform(2.0, 8.0)), float(rng.uniform(0.0, 0.3))
    dp, de = np.zeros(len(ops)), np.zeros(len(ops))
    for s in seed[1:]:
        rng = np.random.RandomState(s)
        part = (0.005, 0.015, 0.04)[s % 3]
        dp = dp + (rng.uniform(size=len(ops)) < part) * rng.normal(0.0, 5.0, size=len(ops))
        de = de + (rng.uniform(size=len(ops)) < part) * rng.normal(0.0, 1.0, size=len(ops))
    succ = [[] for _ in ops]
    for o in ops:
        o["open"] = len(o["deps"] + o["ord"])
        for d in o["deps"] + o["ord"]:
            succ[d["n"]].append(o)
    line, wait = [o for o in ops if o["open"] == 0], {o["n"]: o["open"] for o in ops}
    for o in line:
        for s in succ[o["n"]]:
            wait[s["n"]] -= 1
            line += [s] if wait[s["n"]] == 0 else []
    for o in reversed(line):
        o["path"] = min(o["dur"].values()) + o["tail"] + o["move"] + LAT + max([s["path"] for s in succ[o["n"]]] + [o["boost"]])
        o["prio"] = (o["path"] if late is None else late[o["n"]]) + float(dp[o["n"]])
        o["pen"] = max(-0.9, (RAW if "twice" in o else LONG if o["name"][0] == "S" else ABS if o["name"][:2] == "ab" else SHORT + pen) + float(de[o["n"]]))
    free = {}
    holder = [None] * 8
    left = [o for o in ops if o["open"] == 0]
    order = []

    def bank_at(b):
        h = holder[b]
        if h is None:
            return 0.0
        if any("end" not in c for c in h["cons"]):
            return None
        return max(c["end"] for c in h["cons"]) + LAT

    while left:
        cand = []
        for o in left:
            if "rdy" not in o:
                o["rdy"] = max([d["end"] + LAT for d in o["deps"]] + [o["at"]])
            rdy = o["rdy"]
            bk = None
            if o["psum"]:
                sets = [(b, b + 1) for b in range(0, 2 * WIDE, 2)] if o["psum"] == 2 else [(b,) for b in range(2 * WIDE, 8)]
                best = None
                for s in sets:
                    ts = [bank_at(b) for b in s]
                    if None in ts:
                        continue
                    tm = max(max(ts), rdy, free.get("pe", 0.0))
                    if best is None or tm < best[0]:
                        best = (tm, s)
                if best is None:
                    continue
                rdy, bk = best
            last = o["uses"].get("read") if "uses" in o else None
            at = {x: max(rdy, free.get(x, 0.0), last["end"] + LAT if last is not None and last["eng"] != x else 0.0) for x in o["dur"]}
            e = min(o["dur"], key=lambda x: at[x] + o["dur"][x] * (1.0 + (o["pen"] if x == "dve" else 0.0)))
            cand.append((at[e], o, e, bk))
        t0, e0 = min((c[0], c[2]) for c in cand)
        mine = [c for c in cand if c[2] == e0]
        top = max(mine, key=lambda c: c[1]["prio"] - beta * (c[0] - t0))
        fit = [c for c in mine if c[0] + c[1]["dur"][e0] <= top[0] + 0.02]
        st, o, e, bk = max(fit, key=lambda c: c[1]["prio"]) if fit else top
        o["eng"], o["start"] = e, st
        if "uses" in o:
            o["deps"] = o["deps"] + [c for c in o["uses"]["cons"] if c.get("eng", e) != e]
            o["uses"]["read"] = o
        if e != "arr":
            free[e] = st + o["dur"][e]
        o["end"] = st + o["dur"][e] + o["tail"]
        if o["move"]:
            free["dma"] = max(max(free.get("dma", 0.0), st + DLAT - 0.5) + o["move"], st + o["dur"][e] + DLAT - 0.5)
            if o["sem"]:
                o["end"] = free["dma"] + 0.5
        if bk:
            o["bank"] = bk
            for b in bk:
                if holder[b] is not None:
                    o["deps"] = o["deps"] + holder[b]["cons"]
                holder[b] = o
        if e == "act" and "twice" in o:
            for x in o["twice"]:
                x["dur"] = {"pe": 2 * x["base"]}
        left = [x for x in left if x is not o]
        for s in succ[o["n"]]:
            s["open"] -= 1
            if s["open"] == 0:
                left.append(s)
        order.append(o)
    return order


def build(t, T, topo, core):
    ops = []
    nd = [0]

    def op(name, dur, deps, fn, psum=0, tail=0.0, at=0.0, after=(), sem=None, uses=None, move=0.0, boost=0.0):
        o = {"n": len(ops), "name": name, "dur": dur, "deps": [d for d in deps if d is not None], "ord": list(after), "fn": fn,
             "psum": psum, "tail": tail, "at": at, "sem": sem, "cons": [], "move": move, "boost": boost}
        if uses is not None:
            o["deps"].append(uses)
            o["uses"] = uses
            uses["cons"].append(o)
        ops.append(o)
        return o

    def pv(o, a, b, p=slice(0, 128)):
        k = o["bank"]
        c = 512 * (k[0] % 2)
        return T["E%d" % (k[0] // 2)][p, c + a:c + b]

    def dve(name, n, deps, f, **k):
        return op(name, {"dve": (max(n, 64) + 35) * CY}, deps, lambda q, e, o: [f(q)], **k)

    def ts(name, out, in0, s1, s2, o0, o1, deps, n=64, **k):
        if o1 is None:
            return dve(name, n, deps, lambda q: q.tensor_scalar(out, in0, s1, None, o0), **k)
        return dve(name, n, deps, lambda q: q.tensor_scalar(out, in0, s1, s2, o0, o1), **k)

    def addc(name, out, src, c, deps, n=L, **k):
        def f(q, e, o):
            return [q.tensor_scalar(out, src(), float(c), None, A.add) if e == "dve" else q.activation(out, src(), AF.Copy, bias=float(c))]
        return op(name, {"dve": (n + 35) * CY, "act": (n + 80) * CY}, deps, f, **k)

    def dma(name, pairs, nbytes, rows, deps, queues=("sp",), **k):
        s = "d%d" % nd[0]
        nd[0] += 1
        return op(name, {x: ISSUE * len(pairs) for x in queues}, deps, lambda q, e, o: [q.dma_start(a, b) for a, b in pairs],
                  tail=DLAT, move=nbytes / DRATE + rows * DROW, sem=s, **k)

    def pe(name, cyc, deps, f, psum):
        return op(name, {"pe": cyc * PCY + 0.02}, deps, f, psum=psum, tail=0.05)

    def arrive(name, sem, val, at, deps=()):
        o = op(name, {"arr": 0.0}, list(deps), None, at=at)
        o["tok"] = (sem, val)
        return o

    def remote(name, f, n, deps, after=(), boost=6.0, move=0.0):
        o = op(name, {"g": 0.6}, deps, lambda q, e, o: f(q), after=after, boost=boost, move=move)
        o["lsem"] = n
        return o

    cores = T.cores
    both = ("sp", "act")
    pad = dve("pad", 16, [], lambda q: q.memset(T.M[32 * t:32 * t + 32, :, 0:4], 0), boost=400.0)
    ml, fs, ld = {}, {}, []
    lam = dve("pad2", 1008, [], lambda q: q.memset(T.M[32 * t:32 * t + 32, :, 4:256], 0), boost=370.0, after=[pad])
    lam = [lam, dma("lam2", [(T.M[32 * t:32 * t + 1, :, 0:3], T.lam[:])], 0, 4, [pad], queues=("act",), boost=400.0)]
    for x in LOADS:
        d = int(x[2])
        tt = t ^ d
        if x[0] == "m":
            prs = [(T.M[32 * b:32 * b + 32, tt, :], T.mp[32 * tt:32 * tt + 32, 256 * ((t ^ b) - 1):256 * (t ^ b)]) for b in range(4) if b != t]
            ml[tt] = dma(x, prs, 98e3, 96, [], boost=400.0, after=ld[-1:])
            ld.append(ml[tt])
        else:
            k = (1, 3, 2).index(d)
            n = 2 if d == 2 and DIRECT == 3 else 1
            fs[d] = dma(x, [(T.FS[:, Q * k + Q // n * y:Q * k + Q // n * (y + 1)], T.ft[32 * tt:32 * tt + 32, V // n * y:V // n * (y + 1)]) for y in range(n)],
                        262e3, 128 * n, [], boost=400.0, after=ld[-1:])
            ld.append(fs[d])
    gq = []

    def gop(name, n, f):
        o = op(name, {"g": 0.13 + 2 * n * CY}, [], lambda q, e, o: [f(q)], after=gq[-1:])
        gq.append(o)
        return o
    ki = gop("ki", 1, lambda q: q.iota(T.KI[:], [[0, 2]], 0, 1))
    iot = gop("iot", 160, lambda q: q.iota(T.IOT[:], [[1, 160]], 0, 0, allow_small_or_imprecise_dtypes=True))
    k0 = T.KI[:, 0:1]
    ci = [ts("c%d" % n, T.CI[:, n:n + 1], k0, m, None, A.bitwise_and, None, [ki]) for n, m in enumerate((127, 15, 112, 64, 32, 7, 8, 31, 96))]
    cf = dve("cf", 8, ci, lambda q: q.tensor_copy(T.CF[:], T.CI[:]), boost=320.0)
    P, I16, G16, S64, H32, SL, D8, P32, B96 = [T.CF[:, j:j + 1] for j in range(9)]
    nc = [0]

    def newcol():
        nc[0] += 1
        return T.CD[:, nc[0] - 1:nc[0]]

    def col(name, in0, s1, s2, o0, o1, deps):
        c = newcol()
        if o0 == A.is_equal:
            return c, ts(name, c, in0, s1, s2, o0, o1, deps)
        return c, lin(name, c, in0, *((s1, 0.0 if s2 is None else s2) if o0 == A.mult else (1.0, s1)), deps)

    def lin(name, out, in0, a, b, deps):
        return op(name, {"act": 140 * CY}, deps, lambda q, e, o: [q.activation(out, in0, AF.Copy if isinstance(b, float) else AF.Identity, bias=b, scale=a)])

    def scaled(name, out, in0, m, n, deps):
        return op(name, {"dve": (max(n // 2, 64) + 35) * CY, "act": (n + 80) * CY}, deps,
                  lambda q, e, o: [q.tensor_scalar(out, in0, m, None, A.mult) if e == "dve" else q.activation(out, in0, AF.Identity, scale=m)])
    calm = [len(ops)]
    sg, osg = col("sg", S64, -2.0, 79.0, A.mult, A.add, [cf])
    at = {"s": col("bs", G16, 15.0, None, A.add, None, [cf]), "x": col("bx", G16, sg, None, A.add, None, [osg])}
    WT, owt = col("wt", D8, 15.0 / 8, 1.0, A.mult, A.add, [cf])
    sl, part = {0: col("sl0", SL, 128.0, None, A.mult, None, [cf])}, {}
    for n, a, b, x, y in (("d", 128.0, -768.0, 5.0, 384.0), ("n", -128.0, 128.0, 7.0, 1024.0)):
        part[n] = col("sa" + n, SL, x, y, A.is_equal, A.mult, [cf]), col("sc" + n, SL, a, b, A.mult, A.add, [cf])
    for n in "dn":
        sl[n] = col("sl" + n, part[n][1][0], part[n][0][0], None, A.add, None, [part[n][0][1], part[n][1][1]])
    trio = T.CD[:, nc[0] - 1:nc[0] + 2]
    for n, b in (("f", -128.0), ("g", -192.0)):
        sl[n] = col("sl" + n, SL, 64.0, b, A.mult, A.add, [cf])
    b93, ob93 = newcol(), None
    ob93 = op("b93", {"act": 140 * CY}, [cf], lambda q, e, o: [q.activation(b93, B96, AF.Abs, bias=-48.0)])
    b94, ob94 = col("b94", b93, 2.0, P32, A.mult, A.add, [ob93])
    b96, ob96 = b94, ob94
    hx, ohx = col("hx", H32, -2.0, 32.0, A.mult, A.add, [cf])
    px, opx = col("px", P, hx, None, A.add, None, [ohx])
    sh, osh = col("sh", H32, -4.0, 128.0, A.mult, A.add, [cf])
    sb, osb = col("sb", S64, 6.0, None, A.mult, None, [cf])
    sa, osa = col("sa", S64, -6.0, 384.0, A.mult, A.add, [cf])

    def mask(name, out, slot, deps):
        if isinstance(slot, tuple):
            return ts(name, out, slot[0], slot[1], WT, A.is_equal, A.mult, deps + [owt])
        return ts(name, out, SL, float(slot), WT, A.is_equal, A.mult, deps + [owt])

    def sided(name, out, a, b):
        c, o = col(name + "c", S64, 2.0 * (b - a), 128.0 * a, A.mult, A.add, [cf])
        return mask(name, out, (sl[0][0], c), [o, sl[0][1]])
    bc = {way: (n, ts("bc" + way, T.BC[:, 144 * n:144 * n + 144], T.IOT[:, 0:144], at[way][0], None, A.is_equal, None, [at[way][1], iot], n=144)) for n, way in enumerate("sx")}

    def matrix(name, way, m, deps):
        n, w = len(bc), bc[way][0]
        bc[name] = (n, scaled("bc" + name, T.BC[:, 144 * n:144 * n + 144], T.BC[:, 144 * w:144 * w + 144], m, 144, deps + [bc[way][1]]))
    for slot, ways in ((3, "s"), (5, "x"), (2, "sx"), (4, "x")):
        c = newcol()
        o = mask("m%d" % slot, c, slot, [cf])
        for way in ways:
            matrix("%d%s" % (slot, way), way, c, [o])
    bp, bp0 = {}, ts("bp", T.BP[:, 0:160], T.IOT[:], b96, None, A.is_equal, None, [ob96, iot], n=160)
    for n, w in enumerate((256, 1, 16)):
        o = ts("mb%d" % w, T.MB[:, 4 * n:4 * n + 4], T.IOT[:, 0:128:32], B96, float(w), A.is_equal, A.mult, [cf, iot])
        for b in range(2 if w == 256 else 4):
            c = 160 * (len(bp) + 1)
            bp[(b, w)] = (c, scaled("bp%d_%d" % (b, w), T.BP[:, c:c + 160], T.BP[:, 0:160], T.MB[:, 4 * n + b:4 * n + b + 1], 160, [bp0, o]))
    o1 = dve("oh", 64, [], lambda q: q.memset(T.OH[0:1, :], 0.0))
    oh = [dve("oh1", 32, [o1], lambda q: q.memset(T.OH[0:1, 64:128], -1.0))]
    idm = [ts("id%d" % n, T.ID[:, 128 * n:128 * n + 128], T.IOT[:, 0:128], c, w, A.is_equal, A.mult, [cf, opx, iot], n=128)
           for n, (c, w) in enumerate(((P, 1.0), (P, -1.0), (px, -1.0), (px, 1.0)))]

    pc0 = lin("pc0", T.PC[:, 0:8], T.IOT[:, 0:8], 16.0, I16, [cf, iot])
    pcb = lin("pcb", T.PC[:, 8:16], T.PC[:, 0:8], 1.0, sb, [pc0, osb])
    pca = lin("pca", T.PC[:, 16:24], T.PC[:, 0:8], 1.0, sa, [pc0, osa])
    pc3 = lin("pc3", T.PC[:, 24:32], T.PC[:, 0:8], 1.0, 384.0, [pc0])
    mk = [sided("k70", T.MK[:, 2:3], 6, 4), mask("k72", T.MK[:, 4:5], 2, [cf]), sided("k90", T.MK[:, 5:6], 5, 7), mask("k92", T.MK[:, 7:8], 3, [cf]),
          dve("k0", 2, [], lambda q: q.memset(T.MK[:, 1:2], 0.0))]
    calm.append(len(ops))
    nu = [0]

    def ulist(n=1):
        nu[0] += n
        return L * (nu[0] - n)
    edge = [dve("edge%d" % c, 64, [], lambda q, c=c: q.memset(T.ST[:, c:c + L], 0.0), boost=330.0) for c in (0, V)]
    spare = [dma("zst", [(T.ST[r:128:8, L:V], T.FS[0:64, 2 * Q:2 * Q + 992]) for r in (0, 7)], 256e3, 128, [fs[2]], queues=("act",), boost=300.0),
             dma("zmw", [(T.MW[r:128:8, V:2 * V], T.FS[0:64, 2 * Q:3 * Q]) for r in (1, 3)], 256e3, 128, [fs[2]], queues=("act",), boost=290.0)]
    cast = {tt: ts("cast%d" % tt, T.M16[:, 256 * tt:256 * tt + 256], T.M[:, tt, :], -2048.0, None, A.add, None, [ml[tt], pad] + lam, n=256 , boost=300.0)
            for tt in (t ^ 1, t ^ 3, t)}
    dep, tt = [ml[t ^ 2], pad] + lam, t ^ 2
    ma = ts("ma", T.MA[:], T.M[:, tt, :], 15, None, A.bitwise_and, None, dep, n=256, boost=290.0)
    ta = ts("ta", T.TA[:, 256 * tt:256 * tt + 256], T.M[:, tt, :], 1.0 / 16, 1280.0 - 15.0 / 32, A.mult, A.add, dep, n=256, boost=290.0)
    made = [dve("da", 256, [ma], lambda q: q.tensor_copy(T.DS[:, 0:256], T.MA[:]), boost=290.0),
            ts("db", T.DS[:, 256:512], T.TA[:, 256 * tt:256 * tt + 256], -1280.0, None, A.add, None, [ta], n=128, boost=290.0)]
    near, far, far2, near2 = helpers(topo, core)
    up = topo.engines(core, near)
    up = up[len(up) - len(up) // SHARE:]
    hh = len(up) // 2

    def dst(c):
        r, p, _ = topo.addr(c)
        return DstId(rid=r, pnc=p)

    def f_h2(q):
        r, p, _ = topo.addr(cores[t ^ 1])
        q.remote_dma(T.FD[t], T.FS[:, 0:Q], T.sem["fa%d" % t], T.sem.lsem, p, r, topo.mask(core, cores[t ^ 1]))
        return []

    def f_h0(q):
        if DIRECT == 2:
            r, p, _ = topo.addr(far)
            q.remote_dma(T.FS[:, Q:2 * Q], T.FS[:, Q:2 * Q], T.sem.hs0, T.sem.lsem, p, r, bits(up[hh:]))
            return []
        q.remote_dma_fused([
            RemoteDMATransfer(dst_ids=[dst(near)], dma_engine_mask=bits(up[:hh]), remote_sem=T.sem.hs0, src=T.FS[:, 0:Q], dst=T.FS[:, 0:Q]),
            RemoteDMATransfer(dst_ids=[dst(far)], dma_engine_mask=bits(up[hh:]), remote_sem=T.sem.hs0, src=T.FS[:, Q:2 * Q], dst=T.FS[:, Q:2 * Q])],
            local_sem=T.sem.lsem)
        return []

    def f_sm(q, tt):
        r, p, _ = topo.addr(cores[tt])
        out, src = (T.DG[:, 512 * t:512 * t + 512], T.DS[:]) if tt == t ^ 2 else (T.Z16[:, 256 * t:256 * t + 256], T.M16[:, 256 * tt:256 * tt + 256])
        q.remote_dma(out, src, T.sem["ma%d" % t], T.sem.lsem, p, r, topo.mask(core, cores[tt]))
        return []

    def f_h1(q):
        if DIRECT == 3:
            q.remote_dma_fused([RemoteDMATransfer(dst_ids=[dst(c)], dma_engine_mask=bits(up[hh * y:hh * y + hh]), remote_sem=T.sem.hs1,
                                                  src=T.FS[:, 2 * Q + 512 * y:2 * Q + 512 * y + 512], dst=T.FS[:, 2 * Q + 512 * y:2 * Q + 512 * y + 512])
                                for y, c in enumerate((near2, far2))], local_sem=T.sem.lsem)
            return []
        if DIRECT:
            r, p, _ = topo.addr(cores[t ^ 2])
            q.remote_dma(T.FD[t], T.FS[:, 2 * Q:3 * Q], T.sem["fa%d" % t], T.sem.lsem, p, r, topo.mask(core, cores[t ^ 2]))
            return []
        r, p, _ = topo.addr(far2)
        q.remote_dma(T.FS[:, 2 * Q:3 * Q], T.FS[:, 2 * Q:3 * Q], T.sem.hs1, T.sem.lsem, p, r, bits(up))
        return []
    for x in SENDS:
        if x == "h0":
            gq.append(remote("h0", f_h0, hh if DIRECT == 2 else 2 * hh, [fs[1], fs[3]], after=gq[-1:], boost=300.0, move=1.2))
        elif x == "h1":
            gq.append(remote("h1", f_h1, len(topo.engines(core, cores[t ^ 2]) if DIRECT in (1, 2) else up), [fs[2]], after=gq[-1:], boost=300.0, move=0.6))
        else:
            gq.append(remote("sm%d" % x, lambda q, tt=t ^ x: f_sm(q, tt), len(topo.engines(core, cores[t ^ x])), made if x == 2 else [cast[t ^ x]], after=gq[-1:], boost=300.0, move=0.3))
    small = {"allow_small_or_imprecise_dtypes": True}
    ac0 = gop("ac0", 36, lambda q: q.iota(T.AC[:], [[0, 36]], 0, 0, **small))
    sw = []
    for n, (p, a, b, v) in enumerate(((0, 0, 128, 1), (0, 128, 256, 0), (0, 256, 320, 1), (64, 0, 128, 0), (64, 128, 256, 1), (64, 256, 320, 0))):
        sw.append(gop("sw%d" % n, b - a, lambda q, p=p, a=a, b=b, v=v: q.iota(T.SW[p:p + 64, a:b], [[0, b - a]], v, 0, **small)))
        sw[-1]["deps"] += [ac0] if n == 0 else sw[n - 1:n] if n == 3 else []
    fa = {}
    for a in range(4):
        if a == t:
            fa[a] = fs[2]
        else:
            snd = helpers(topo, cores[a])[(1, 3, 2).index(a ^ t)]
            fa[a] = arrive("fa%d" % a, "fa%d" % a, len(topo.engines(snd, core)) * (2 if DIRECT == 3 and a ^ t == 2 else 1), ARR_FT[a ^ t])

    def fwin(k, s, a, after):
        src = T.ft[32 * t:32 * t + 32, :] if a == t else T.FD[a]
        if DIRECT == 3 and a ^ t == 2:
            return dma("fw%d%d" % (k, s), [(T.FW[64 * s + 32 * h:64 * s + 32 * h + 32, V * k + HF * y:V * k + HF * y + HF], T.FE[y]) for h in range(2) for y in range(2)],
                       524e3, 128, [fa[a]], after=after)
        return dma("fw%d%d" % (k, s), [(T.FW[64 * s + 32 * h:64 * s + 32 * h + 32, V * k:V * k + V], src) for h in range(2)], 524e3, 128, [fa[a]], after=after)

    def fleft(k, s, a, after):
        if a == t:
            prs = [(T.FR[64 * s + 32 * h:64 * s + 32 * h + 32, HF * k:HF * k + HF], T.ft[32 * t:32 * t + 32, HF * h:HF * h + HF]) for h in range(2)]
        elif DIRECT == 3 and a ^ t == 2:
            prs = [(T.FR[64 * s + 32 * h:64 * s + 32 * h + 32, HF * k:HF * k + HF], T.FE[h]) for h in range(2)]
        else:
            prs = [(T.FR[64 * s + 32 * (x // 2):64 * s + 32 * (x // 2) + 32, HF * k + Q * (x % 2):HF * k + Q * (x % 2) + Q], T.FD[a, x:128:4, :]) for x in range(4)]
        return dma("fr%d%d" % (k, s), prs, 262e3, 128, [fa[a]], after=after)
    za, stg, zl, wl, seq = {}, [], {}, {}, []
    for a in (t, t ^ 1, t ^ 3, t ^ 2):
        za[a] = cast[t] if a == t else arrive("ma%d" % a, "ma%d" % a, len(topo.engines(cores[a], core)), ARR_MAP[a ^ t])
        c, s = slice(256 * a, 256 * a + 256), 0 if a in (1, 2) else 1
        Z = (T.M16 if a == t else T.Z16)[:, c]
        zl[a] = [za[a], za[a]]
        if a != t ^ 2:
            ta = ts("ta%d" % a, T.TA[:, c], Z, 1.0 / 16, 1408.0 - 15.0 / 32, A.mult, A.add, [za[a]], n=128, after=seq[-1:], boost=200.0)
            tb = ts("tb%d" % a, T.TB[:, c], T.TA[:, c], -16.0, 22528.0, A.mult, A.add, [ta], n=128, boost=200.0)
            db = ts("db%d" % a, T.DG[:, 512 * a + 256:512 * a + 512], T.TA[:, c], -1280.0, None, A.add, None, [ta], n=128, after=[tb], boost=200.0)
            zl[a] = [dve("da%d" % a, 512, [tb], lambda q, a=a, c=c, Z=Z: q.tensor_tensor(T.DG[:, 512 * a:512 * a + 256], Z, T.TB[:, c], A.add), after=[db], boost=200.0), db]
            seq.append(zl[a][0])
        for g in (1, 0):
            prs = []
            for b in range(4):
                for h in range(0 if b == a else 1 if a ^ t in TWICE else 2):
                    r = 64 * s + 32 * h + STAGE[s]["%d%d" % (a, b)] + 8 * g
                    prs.append((T.ST[r:r + 17:16, L - L * h:V + L - L * h], T.DG[32 * b:32 * b + 32, 512 * a + 256 * g:512 * a + 256 * g + 256]))
            stg.append(dma("st%d%d" % (a, g), prs, 16e3 * len(prs), 32 * len(prs), [zl[a][g]] + edge, queues=both[g:g + 1], after=stg[-2:-1], boost=200.0))
    for n, d in enumerate(TWICE):
        a = t ^ d
        s = 0 if a in (1, 2) else 1
        rs = [64 * s + STAGE[s]["%d%d" % (a, b)] for b in range(4) if b != a]
        stg.append(dma("sd%d" % a, [(T.ST[r + 32:r + 57:8, 0:V], T.ST[r:r + 25:8, L:V + L]) for r in rs], 98e3, 48, stg[2 * n:2 * n + 2], boost=200.0))
    for o in ops[calm[0]:calm[1]]:
        o["boost"] = 70.0
        if o["name"][:2] in LATER.split():
            o["ord"].append(seq[-1])
    if DIRECT == 2:
        gq.append(remote("h2", f_h2, len(topo.engines(core, cores[t ^ 1])), [fs[1], stg[HOLD]], after=gq[-1:], boost=300.0, move=0.6))
    if "h1" not in SENDS:
        gq.append(remote("h1", f_h1, len(topo.engines(core, cores[t ^ 2]) if DIRECT else up), [fs[2], stg[HOLD]], after=gq[-1:], boost=300.0, move=0.6))
    for a in (t, t ^ 1, t ^ 3):
        wl[a] = dma("wl%d" % a, [(T.WD[0:1, 8 * a:8 * a + 4], (T.M16 if a == t else T.Z16)[32 * a:32 * a + 1, 256 * a:256 * a + 4])], 0, 1, [za[a]], after=stg)

    def LT(c, n=L, p=slice(0, 128)):
        return T.LT[p, c:c + n]

    def U(c, n=L):
        return T.U[:, c:c + n]

    def given(name, pair, ws):
        use = [(int(x[0]), bp[(int(x[1]), w)], g) for x in pair for g, w in enumerate(ws)]

        def f(q, e, o):
            mm = [(T.BP[:, m[0] + 32 - 32 * h:m[0] + 160 - 32 * h], T.DG[:, 512 * a + 256 * g + L * h:512 * a + 256 * g + L * h + L]) for a, m, g in use for h in range(2)]
            return [q.matmul(pv(o, 0, L), l, r, n == 0, n == len(mm) - 1) for n, (l, r) in enumerate(mm)]
        return pe("l" + name, 8 * L, sum([zl[a] + [m[1]] for a, m, g in use], []), f, 1)

    def tou(name, p, shift=None):
        u = ulist()
        if shift:
            return u, dve("u" + name, L, [shift[1]], lambda q: q.tensor_scalar(U(u), pv(p, 0, L), shift[0], None, A.add), uses=p)
        return u, dve("u" + name, L, [], lambda q: q.tensor_copy(U(u), pv(p, 0, L)), uses=p)

    def tof(name, p, c0, part=slice(0, 128)):
        return addc("n" + name, LT(c0, L, part), lambda: pv(p, 0, L, part), 0, [], uses=p)
    lu, lf = {}, {}
    for name, pair in (("p1", ("31", "20")), ("p2", ("21", "30"))):
        lu[name] = tou(name, given(name, pair, (256, 1)), (sh, osh))

    def fwt(q, e, o):
        who = [[a if a in wl else a ^ (k + 1) for a in LEFT[k]] for k in range(3)]
        return [q.matmul(pv(o, 4 * k, 4 * k + 4), T.OH[0:1, 64 - 64 * s:192 - 64 * s], T.WD[0:1, 8 * who[k][s]:8 * who[k][s] + 4], s == 0, s == 1)
                for k in range(3) for s in range(2)]
    wp = pe("wp", 400, list(wl.values()) + oh, fwt, 1)
    wgt = addc("wgt", T.WC[:], lambda: pv(wp, 0, 12), -2048, [], n=64, uses=wp)

    parts = ((0, CUT), (CUT, L))

    def compose(k, win, lst, deps, cut=CUT):
        res = []
        for x, (a, b) in enumerate(((0, cut), (cut, L))):
            def f(q, e, o, a=a, b=b):
                out, w = T.R[:, HF * k + 16 * a:HF * k + 16 * b], win.indirect(U(lst[0] + a, b - a))
                return [q.tensor_copy(out, w) if e == "dve" else q.activation(out, w, AF.Copy)]
            n = 16 * (b - a) * GA
            res.append(op("S%d%s" % (k, "ab"[x]), {"dve": (n + 60) * CY, "act": (n + 75) * CY}, deps + [lst[1]], f))
        return res

    def tolist(name, k, m, deps):
        def f(q, e, o):
            n = bc[m][0]
            return [q.matmul(pv(o, 0, L), T.BC[:, 144 * n + 15 - i:144 * n + 143 - i],
                             T.R[:, HF * k + i:HF * k + HF:16] if k else T.ST[:, L + 256 * i:2 * L + 256 * i], i == 0, i == 15) for i in range(16)]
        return pe("cv" + name, 16 * L, deps + [bc[m][1]], f, 1)

    def renew(name, moves, deps, step=8, **kw):
        prs = []
        for k, s, slot, s2, blk, slot2 in moves:
            for h in range(2):
                for h2 in range(2):
                    r, r2 = 64 * s + 32 * h + slot, 64 * s2 + 32 * h2 + slot2
                    prs.append((T.MW[r2:r2 + 33 - step:step, V * blk + HF * h:V * blk + HF * h + HF], T.R[r:r + 33 - step:step, HF * k:HF * k + HF]))
        return dma(name, prs, 131e3 / step * len(prs), 16 * len(prs), deps, **kw)

    junk = [None, None]
    nj = [0]

    def evaluate(k, c, lst):
        h0 = HF * (3 * k + c)
        z0 = HF * k
        wk = min(k, 1)
        hg = []
        for x, (a, b) in enumerate(parts):
            def fh(q, e, o, a=a, b=b):
                out, w = T.H[:, h0 + 16 * a:h0 + 16 * b], T.FW[:, V * wk:V * wk + V].indirect(U(lst[0] + a, b - a))
                if e == "dve":
                    return [q.tensor_tensor(out, w, T.FR[:, z0 + 16 * a:z0 + 16 * b], A.subtract)]
                return [q.activation(out, w, AF.Copy)]
            n = 16 * (b - a) * GA
            hg.append(op("h%d%d%s" % (k, c, "ab"[x]), {"dve": (n + 60) * CY, "act": (n + 75) * CY}, fw[wk] + fr[k] + [lst[1]], fh))
        res = []
        for x in range(2):
            def f(q, e, o, x=x):
                I, NI, NS, S = [T.ID[:, 128 * y:128 * y + 128] for y in range(4)]
                raw = [g["eng"] == "act" for g in hg]
                mm = []
                for y in range(2):
                    j0, j1 = Q * x + 512 * y, Q * x + 512 * y + 512
                    tm = [(I, T.H, h0, 0, j0, j1), (NI, T.H, h0, 1, j0, min(j1, HF - 1))]
                    for g, (a, b) in enumerate(parts):
                        if raw[g]:
                            tm += [(NI, T.FR, z0, 0, max(j0, 16 * a), min(j1, 16 * b)), (I, T.FR, z0, 1, max(j0, 16 * a - 1), min(j1, 16 * b - 1))]
                    if j1 == HF:
                        tm += [(NS, T.H, h0, 1 - HF, HF - 1, HF)] + ([(S, T.FR, z0, 1 - HF, HF - 1, HF)] if raw[0] else [])
                    tm = [m for m in tm if m[5] > m[4]]
                    mm += [q.matmul(pv(o, u - Q * x, v - Q * x), W, B[:, z + u + sh:z + v + sh], n == 0, n == len(tm) - 1) for n, (W, B, z, sh, u, v) in enumerate(tm)]
                return mm
            df = pe("df%d%d%d" % (k, c, x), 2112, hg[:x + 1] + fr[k] + idm, f, 2)
            df["base"] = df["dur"]["pe"]
            hg[x]["twice"] = [df]
            acc = T.AC[:, 12 * k + 4 * x + c:12 * k + 4 * x + c + 1]

            def ab(q, e, o, df=df, acc=acc):
                if e == "dve":
                    return [q.tensor_reduce(acc, pv(df, 0, Q), AxisListType.X, A.add, apply_absolute_value=True)]
                y = nj[0] % 2
                nj[0] += 1
                if junk[y] is not None:
                    o["wait"](junk[y])
                junk[y] = o
                return [q.activation(T.JK[:, Q * y:Q * y + Q], pv(df, 0, Q), AF.Abs, accum_out=acc)]
            res.append(op("ab%d%d%d" % (k, c, x), {"dve": (Q + 35) * CY, "act": (Q + 100) * CY}, [ac0], ab, uses=df))
        return res

    def decide(k, c0, lists, abs_):
        n0 = 3 * L * k
        n1 = dve("ne1%d" % k, 4 * L, lists, lambda q: q.tensor_tensor(T.NE[:, n0:n0 + 2 * L], LT(c0, 2 * L), LT(c0 + L, 2 * L), A.not_equal))
        n2 = dve("ne2%d" % k, 2 * L, lists, lambda q: q.tensor_tensor(T.NE[:, n0 + 2 * L:n0 + 3 * L], LT(c0 + 2 * L), LT(c0), A.not_equal))
        wcol = T.WC[:, 5 * k:5 * k + 1]
        es = []
        for c in range(3):
            s = n0 + L * ((c + 1) % 3)
            es.append(op("e%d%d" % (k, c), {"act": (L + 100) * CY}, [n2 if c == 1 else n1, wgt, ac0],
                         lambda q, e, o, s=s, c=c: [q.activation(T.JS[:, n0 + L * c:n0 + L * c + L], T.NE[:, s:s + L], AF.Identity,
                                                                 scale=wcol, accum_out=T.AC[:, 12 * k + 8 + c:12 * k + 9 + c])]))
        ways = (0, 128) if k == 0 else (64, 192)
        pre = dve("pre%d" % k, 4, es + abs_[0::2], lambda q: q.tensor_tensor(T.AC[:, 12 * k + 8:12 * k + 12], T.AC[:, 12 * k + 8:12 * k + 12], T.AC[:, 12 * k:12 * k + 4], A.add))
        sc = pe("sc%d" % k, 4 * 256, [pre] + abs_ + sw,
                lambda q, e, o: [q.matmul(pv(o, 4 * x, 4 * x + 4), T.SW[:, ways[x]:ways[x] + 128], T.AC[:, 12 * k + 4 * j:12 * k + 4 * j + 4], j == 2, j == 1)
                                 for x in range(2) for j in (2, 1)], 1)
        res = []
        for x in range(2):
            F = [T.FL[:, 8 * k + 2 * y + x:8 * k + 2 * y + x + 1] for y in range(3)]
            f2 = dve("f2%d%d" % (k, x), 1, [], lambda q, F=F, x=x: q.tensor_scalar(F[2], pv(sc, 4 * x, 4 * x + 1), pv(sc, 4 * x + 1, 4 * x + 2), pv(sc, 4 * x + 2, 4 * x + 3), A.min, A.is_gt), uses=sc)
            f1 = dve("f1%d%d" % (k, x), 1, [], lambda q, F=F, x=x: q.tensor_scalar(F[1], pv(sc, 4 * x, 4 * x + 1), pv(sc, 4 * x + 1, 4 * x + 2), 128.0, A.is_gt, A.mult), uses=sc)
            res.append((F[0], ts("fw%d%d" % (k, x), F[0], F[2], 256.0, F[1], A.mult, A.max, [f1, f2])))
        return res
    no = [0]

    def offs(name, base, F, how, deps):
        c = 8 * no[0]
        no[0] += 1
        return c, ts("of" + name, T.OF[:, c:c + 8], base, F[0], None, how, None, deps + [F[1]])

    def pick(name, to, c0, n, of, k, deps):
        w = LT(c0, n * L).indirect(T.OF[:, of:of + 8 * k])
        dur = {"dve": (L * k * GA + 60) * CY}
        if to is None:
            u = ulist(k)
            return u, op("pu" + name, dur, deps, lambda q, e, o: [q.tensor_copy(U(u, k * L), w)])
        dur["act"] = (L * k * GA + 75) * CY
        return op("pk" + name, dur, deps, lambda q, e, o: [q.tensor_copy(LT(to, k * L), w) if e == "dve" else q.activation(LT(to, k * L), w, AF.Copy)])

    def ship(name, d, items, late):
        away = [(a, c0) for a, c0, dep in items if a != t]
        k = 3 * t + d - 1
        for a, c0, dep in items:
            if a == t and d < 3:
                home(t, d, T.LT, c0, [dep] + late)
            elif a == t:
                home(t, d, T.YL, L * k, [widen(t, U(c0), [dep])])
        es = topo.engines(core, cores[away[0][0]])
        per = {1: len(es), 2: len(es) // 2, 3: len(es) // 4}[len(away)]

        def f(q):
            q.remote_dma_fused([RemoteDMATransfer(dst_ids=[dst(cores[a])], dma_engine_mask=bits(es[per * n:per * n + per]), remote_sem=T.sem["oa%d" % k],
                                                  src=LT(c0) if d < 3 else U(c0), dst=T.YL[:, L * k:L * k + L] if d < 3 else T.YU[:, L * t:L * t + L])
                                for n, (a, c0) in enumerate(away)], local_sem=T.sem.lsem)
            return []
        gq.append(remote(name, f, per * len(away), [dep for a, c0, dep in items if a != t], after=gq[-1:], boost=(30.0, 14.0, 6.5)[d - 1]))

    def widen(s, src, deps):
        return dve("wi%d" % s, L, deps, lambda q: q.tensor_copy(T.YL[:, L * (3 * s + 2):L * (3 * s + 3)], src))

    def home(s, d, B, c0, deps):
        r = 64 * HOME[t][d - 1]
        dma("y%d%d" % (s, d), [(T.ym[32 * s:32 * s + 32, 256 * (d - 1) + L * h:256 * (d - 1) + L * h + L], B[r + 32 * h:r + 32 * h + 32, c0:c0 + L]) for h in range(2)],
            32e3, 64, deps, queues=both if d == 3 else ("sp",))

    B0, B1, BB = T.MW[:, 0:V], T.MW[:, V:2 * V], T.MW[:, 0:2 * V]
    SA, SB = slice(0, 64), slice(64, 128)
    stg = stg + spare[:1]

    def order(q, e, i0):
        prs = [(T.R[:, i:HF:16], T.ST[:, L + 256 * i:2 * L + 256 * i]) for i in range(i0, i0 + 4)]
        return [q.tensor_copy(a, b) if e == "dve" else q.activation(a, b, AF.Copy) for a, b in prs]
    S0 = [op("N%d" % i0, {"dve": 4 * 100 * CY, "act": 4 * 210 * CY}, stg, lambda q, e, o, i0=i0: order(q, e, i0)) for i0 in range(0, 16, 4)]
    S1 = compose(1, T.ST[:, 0:V + L], lu["p1"], stg)
    S2 = compose(2, T.ST[:, 0:V + L], lu["p2"], stg, CUT2)
    wa = [renew("wa", [(0, s, 0, s, 1, 0) for s in range(2)], S0, 2)]
    w1 = wa + [renew("wb", [(1, 0, 3, 1, 1, 5), (1, 1, 3, 0, 1, 7)], S1)]
    w1 += [renew("wc%d" % s, [(2, s, 5, s, 1, (5, 7)[s])], S2, queues=both[s:s + 1]) for s in range(2)]
    behind = {a: stg if a == t else (wa, w1[:2], w1)[EARLY[a ^ t]] for a in range(4)}
    w1 = w1 + spare[1:]
    fw = [[fwin(0, 0, 1, behind[1]), fwin(0, 1, 3, behind[3])]]
    fr = [[fleft(0, s, LEFT[0][s], behind[LEFT[0][s]]) for s in range(2)]]
    fr += [[fleft(k, s, LEFT[k][s], w1 + fw[0] + fr[0]) for s in range(2)] for k in (1, 2)]
    fw.append([fwin(1, 0, 2, w1 + fw[0] + fr[0]), fwin(1, 1, 3, w1 + fw[0] + fr[0])])
    w0 = [renew("wd", [(0, s, 1, s, 0, 1) for s in range(2)], S0, 2, after=fw[1] + fr[1]),
          renew("wh", [(0, s, 1, 1 - s, 0, 2) for s in range(2)], S0, after=fw[1] + fr[1])]
    for name, pair, places, wu in (("1", ("02", "13"), [T3], 1), ("2", ("12", "03"), [T4, TZ + L], 1), ("0", ("01", "23"), [T1], 1), ("3", ("32", "10"), [T2], 0),
                                   ("5", None, [TW + 2 * L], 0)):
        p = given(name, pair, (1, 16)) if pair else tolist("g" + name, 0, "2x", stg)
        if wu:
            lu[name] = tou(name, p)
        for n, c0 in enumerate(places):
            lf[c0] = [tof("%s%d" % (name, n), p, c0)]
    ab = {(k, 0): evaluate(k, 0, lu[str(k)]) for k in range(3)}
    S3 = compose(3, B1, lu["1"], w1)
    S4 = compose(4, B1, lu["2"], w1)
    w0 += [renew("we", [(3, 0, 2, 1, 0, 0), (3, 0, 2, 0, 0, 4), (3, 1, 2, 0, 0, 7), (3, 1, 2, 1, 0, 6)], S3 + w0[:1]),
           renew("wf", [(4, 0, 4, 0, 0, 0), (4, 0, 4, 1, 0, 4), (4, 1, 4, 1, 0, 7), (4, 1, 4, 0, 0, 6)], S4 + w0[:1])]
    for name, k, m, S, ca, cb in (("1", 1, "3s", S1, T2 + 2 * L, T1 + L), ("2", 2, "5x", S2, T2 + L, T1 + 2 * L),
                                  ("3", 3, "2s", S3, T1 + L, T2 + 2 * L), ("4", 4, "4x", S4, T1 + 2 * L, T2 + L)):
        p = tolist(name, k, m, S)
        for c0, part in sorted(((ca, SA), (cb, SB)), key=lambda z: z[0]):
            lf.setdefault(c0, []).append(tof("c%s%d" % (name, c0 // L), p, c0, part))
    for c in (1, 2):
        u = ulist()
        ab[(0, c)] = evaluate(0, c, (u, dve("uc%d" % c, L, lf[T1 + c * L], lambda q, u=u, c=c: q.tensor_copy(U(u), LT(T1 + c * L)))))
    t1 = lf[T1] + lf[T1 + L] + lf[T1 + 2 * L]
    t12 = t1 + lf[T2] + lf[T2 + L] + lf[T2 + 2 * L]
    FA, FB = decide(0, T1, t1, ab[(0, 0)] + ab[(0, 1)] + ab[(0, 2)])
    matrix("dx", "x", T.MK[:, 72:73], [mask("mdx", T.MK[:, 72:73], (sl["d"][0], FB[0]), [sl["d"][1], FB[1]])])
    of5, o = offs("5", T.PC[:, 8:16], FA, A.add, [pcb])
    S5 = compose(5, B0, pick("5", None, T1, 6, of5, 1, t12 + [o]), w0)
    r1 = pick("o1", O1, T1, 6, of5, 1, t12 + [o])
    of6, o = offs("6", T.PC[:, 16:24], FB, A.add, [pca])
    r2 = pick("o2", O2, T1, 6, of6, 1, t12 + [o])
    u = ulist()
    lu["v"] = u, dve("uv", L, [r2], lambda q, u=u: q.tensor_copy(U(u), LT(O2)))
    mk1 = [mask("k1", T.MK[:, 0:7:3], (trio, FA[0]), [sl[n][1] for n in "nfg"] + [FA[1]])]
    ship("x1", 1, [(0, O1, r1), (1, O1, r1), (2, O2, r2), (3, O2, r2)], [])
    for c, k, m, S in ((2, 4, "dx", S4), (1, 5, "3s", S5)):
        p = tolist("r%d" % c, k, m, S)
        lu["r"] = tou("r%d" % c, p)
        ab[(1, c)] = evaluate(1, c, lu["r"])
        lf[T3 + c * L] = [tof("r%d" % c, p, T3 + c * L)]
    S6 = compose(6, B1, lu["r"], w1)
    for name, k, m, S, c0 in (("y", 3, "dx", S3, TZ + 3 * L), ("x", 5, "5x", S5, TZ), ("z", 6, "dx", S6, TZ + 2 * L)):
        lf[c0] = [tof(name, tolist(name, k, m, S), c0)]
    t3 = lf[T3] + lf[T3 + L] + lf[T3 + 2 * L]
    FO, FX = decide(1, T3, t3, ab[(1, 0)] + ab[(1, 1)] + ab[(1, 2)])
    tz = sum([lf[TZ + n * L] for n in range(4)], [])
    ofa, oa = offs("a", T.PC[:, 0:8], FO, A.add, [pc0])
    ofb, ob = offs("b", T.PC[:, 24:32], FX, A.subtract, [pc3])
    u3, o3 = pick("3", None, TZ, 4, ofa, 2, tz + [oa, ob])
    lf[T4 + L] = [pick("3", T4 + L, TZ, 4, ofa, 2, tz + [oa, ob])]
    r3 = pick("o3", O3, T3, 3, ofa, 1, t3 + [oa])
    g7 = ts("g7", T.FL[:, 30:31], FX[0], 256.0, 128.0, A.is_lt, A.mult, [FX[1]])
    g8 = ts("g8", T.FL[:, 31:32], FX[0], 256.0, float(V), A.is_equal, A.mult, [FX[1]])
    of7, o = offs("7", T.PC[:, 0:8], (T.FL[:, 30:31], g7), A.add, [pc0])
    u = ulist()
    S7 = compose(7, BB, (u, dve("pu7", L * GA + 25, [r2, o, g8] + lf[TW + 2 * L], lambda q, u=u: q.tensor_scalar(
        U(u), LT(O2, 2 * L).indirect(T.OF[:, of7:of7 + 8]), T.FL[:, 31:32], None, A.add))), w0 + w1)
    du = [ts("du%d" % x, T.OF[:, 72 + x:73 + x], F[0], 1.0 / 128, c, A.mult, A.add, [F[1]]) for x, F, c in ((0, FO, 5.0), (1, FX, 2.0))]
    pm = dve("pm", 48, mk + mk1 + du, lambda q: q.tensor_copy(T.MK[:, 16:48], T.MK[:, 0:8].indirect(T.OF[:, 72:74])))
    matrix("7", "s", T.MK[:, 32:33], [pm])
    matrix("8", "s", T.MK[:, 0:1], mk1)
    matrix("9", "s", T.MK[:, 16:17], [pm])
    p = tolist("7", 7, "7", S7)
    r4 = tof("7", p, TW)
    w2 = renew("wg", [(7, s, 0, 1 - s, 1, 1) for s in range(2)], S7 + S6, 2)
    ship("x2", 2, [(0, O3, r3), (1, O3, r3)], [w2])
    ship("x5", 2, [(2, TW, r4), (3, TW, r4)], [w2])
    for c in (1, 2):
        ab[(2, c)] = evaluate(2, c, (u3 + L * (c - 1), o3))
    t4 = lf[T4] + lf[T4 + L]
    GO, GX = decide(2, T4, t4, ab[(2, 0)] + ab[(2, 1)] + ab[(2, 2)])
    inv = [tof("8", tolist("8", 8, "8", compose(8, B0, tou("8", p), w0)), TW + 3 * L),
           tof("9", tolist("9", 9, "9", compose(9, B1, lu["v"], [w2])), TW + 4 * L)]
    of8, o = offs("8", T.PC[:, 0:8], GX, A.add, [pc0])
    u6, r6 = pick("o6", None, TW + 2 * L, 3, of8, 1, lf[TW + 2 * L] + inv + [o])
    of9, o = offs("9", T.PC[:, 0:8], GO, A.add, [pc0])
    u5, r5 = pick("o5", None, T4, 3, of9, 1, t4 + [o])
    last = [[(0, u5, r5), (1, u5, r5)], [(2, u6, r6), (3, u6, r6)]]
    if ONE:
        ship("x3", 3, last[0] + last[1], [])
    else:
        ship("x3", 3, last[0], [])
        ship("x4", 3, last[1], [])
    for d, mine, late in ((1, r2, [w2]), (2, r4, [GO[1]]), (3, r5 if t < 2 else r6, [])):
        for s in range(4):
            if s == t:
                continue
            ne = len(topo.engines(cores[s], core))
            grp = [a for a in ([0, 1, 2, 3] if d < 2 or ONE else [t & 2, (t & 2) + 1]) if a != s]
            k = 3 * s + d - 1
            ar = arrive("oa%d" % k, "oa%d" % k, {1: ne, 2: ne // 2, 3: ne // 4}[len(grp)], 0.0, [mine])
            ar["tail"] = 4.0
            home(s, d, T.YL, L * k, [ar] + late if d < 3 else [widen(s, T.YU[:, L * s:L * s + L], [ar])])
    named = {o["name"]: o for o in ops}
    for e, names in ORDER.items():
        row = [named[x] for x in names.split()]
        for a, b in zip([None] + row, row):
            b["dur"] = {e: b["dur"][e]}
            b["ord"] += [a] if a else []
    return ops


def rank_program(g, core, T, topo):
    rank = T.rank_of(core)
    if rank is None:
        for a, c in enumerate(T.cores):
            hs = helpers(topo, c)
            if core not in (hs[:3], hs[:2], hs[1:2], hs)[DIRECT]:
                continue
            up = len(topo.engines(c, core)) // SHARE
            k, d, s, v = ((0, 1, "hs0", up // 2), (1, 3, "hs0", up // 2), (2, 2, "hs1", up // 2 if DIRECT else up), (2, 2, "hs1", up // 2))[hs.index(core)]
            to = T.cores[a ^ d]
            r, p, _ = topo.addr(to)
            g.wait_ge(T.sem[s], v)
            out, src = T.FD[a], T.FS[:, Q * k:Q * k + Q]
            if DIRECT == 3 and k == 2:
                y = 3 - hs.index(core)
                out, src = T.FE[y], T.FS[:, 2 * Q + 512 * y:2 * Q + 512 * y + 512]
            g.remote_dma(out, src, T.sem["fa%d" % a], T.sem.lsem, p, r, topo.mask(core, to))
            g.wait_ge(T.sem.lsem, len(topo.engines(core, to)))
        return
    order = arrange(lambda: build(rank, T, topo, core), SEEDS[rank])
    queue = {"pe": g.tensor, "dve": g.vector, "act": g.scalar, "sp": g.sync, "g": g}
    own = {"pe": "pe", "dve": "dve", "act": "act", "g": "pool"}
    count = {}
    seen = {}

    def wait(e, d):
        if "tok" not in d:
            return
        s, v = d["tok"]
        if seen.get((e, s), 0) < v:
            queue[e].wait_ge(T.sem[s], v)
            seen[(e, s)] = v

    for o in order:
        e = o["eng"]
        if e == "arr":
            count[o["tok"][0]] = o["tok"][1]
            continue
        need = {}
        for d in o["deps"]:
            if "tok" in d and d["tok"][1] > need.get(d["tok"][0], {"tok": (0, 0)})["tok"][1]:
                need[d["tok"][0]] = d
        for d in need.values():
            wait(e, d)
        o["wait"] = lambda d, e=e: wait(e, d)
        ins = o["fn"](queue[e], e, o)
        if "lsem" in o:
            count["lsem"] = count.get("lsem", 0) + o["lsem"]
            continue
        s, step = (o["sem"], 16) if o["sem"] else (own[e], 1)
        for x in ins:
            x.then_inc(T.sem[s], step)
        count[s] = count.get(s, 0) + step * len(ins)
        o["tok"] = (s, count[s])
    for s, v in count.items():
        g.wait_ge(T.sem[s], v)
